import numpy as np, ml_dtypes
CORES = [6,15,38,47]
N = 4
BF = ml_dtypes.bfloat16
D, L, H, S1, S2, VI = 3456, 256, 256, 1, 1, 4
def effects(rng):
    cap = rng.integers(1, 256, (N, 8, 1, D))
    return np.minimum((rng.random((N, 8, 16, D)) * (cap + 1)).astype(np.int64), cap)
def near(rng, n, share, few=64):
    pop = rng.integers(0, D, (N, 8, few)); v = rng.integers(0, D, (N, 8, 16, n))
    c = np.take_along_axis(pop, rng.integers(0, few, (N, 8, 16 * n)), 2).reshape(N, 8, 16, n)
    return np.where(rng.random(v.shape) < share, c, v)
def rows(rng, n):
    return np.argsort(np.argsort(rng.random((N, 8, 16, L)), axis=2), axis=2) < n
def forest(rng, filled, own, deep):
    o = np.argsort(np.where(filled, rng.random(filled.shape), 2.0), axis=2); r = np.arange(16)[:, None]
    u = rng.random(filled.shape); b = np.minimum((rng.random(filled.shape) * (r + 1)).astype(np.int64), r)
    b = np.where(u < own, r, np.where(u > 1 - deep, np.maximum(r - 1, 0), b))
    w = np.zeros(filled.shape, np.int64); np.put_along_axis(w, o, np.take_along_axis(o, b, 2), 2)
    return np.where(filled, w, 0)
def pack(eff, rem, lim, drugs, why, filled):
    return {"eff": np.ascontiguousarray(eff.reshape(N, 128, D)).astype(np.float32).astype(BF), "rem": np.ascontiguousarray(rem.reshape(N, 128, D)).astype(np.int32),
            "lim": np.repeat(lim, 16, axis=1)[:, :, None].astype(np.int32), "drugs": np.ascontiguousarray(np.where(filled, drugs, D).reshape(N, 128, L)).astype(np.int32),
            "why": np.ascontiguousarray(np.where(filled, why, 0).reshape(N, 128, L)).astype(np.int32)}
def setup_inputs(rng):
    n = np.maximum(rng.integers(0, 17, (N, 8, 1, L)), rng.integers(0, 17, (N, 8, 1, L)))
    filled = rows(rng, n); why = forest(rng, filled, 0.3, 0.3)
    return pack(effects(rng), near(rng, D, 0.3), rng.integers(6000, 20000, (N, 8)), near(rng, L, 0.3), why, filled)
def setup_inputs_ties(rng):
    v = rng.integers(0, 256, (N, 8, 16)); v[:, :, 0] = 255
    sh = rng.integers(0, 16, (N, 8, 1, D)); sh[:, ::2, :, 1::2] = sh[:, ::2, :, ::2] + 8
    ix = (np.arange(16)[:, None] + sh) % 16
    eff = np.take_along_axis(v, ix.reshape(N, 8, 16 * D), 2).reshape(N, 8, 16, D)
    lim = np.minimum(rng.integers(3, 12, (N, 8)) * np.add.reduce(v, axis=2), 65280)
    filled = rows(rng, rng.integers(1, 17, (N, 8, 1, L))); drugs = near(rng, L, 0.9, 6)
    pair = rng.random((N, 8, 1, L)) < 0.5; pair[:, 1::2] = False
    twin = np.repeat(drugs[:, :, ::2], 2, axis=2); twin[:, :, 1::2] = twin[:, :, 1::2] ^ 1
    drugs = np.where(pair, twin, drugs); filled = np.where(pair, np.repeat(filled[:, :, ::2], 2, axis=2), filled)
    why = forest(rng, filled, 0.4, 0.2)
    return pack(eff, near(rng, D, 0.7, 6), lim, drugs, why, filled)
def setup_inputs_corners(rng):
    eff = effects(rng); eff[..., 0] = 0; eff[..., D - 1] = 255
    lim = rng.choice(np.array([1, 12000, 65280]), (N, 8)); lim[:, 1] = 1; lim[:, 2] = 65280
    kind = rng.integers(0, 10, (N, 8, 1, L)); m = np.arange(16)[:, None]; hv = rng.random((N, 8, 1, L)) < 0.5
    filled = rows(rng, np.where(kind == 6, 15, rng.integers(0, 17, (N, 8, 1, L))))
    filled = filled | (kind == 1) | (kind == 2) | (kind == 5) | (kind == 8) | (kind == 9)
    filled = np.where(kind == 0, False, np.where(kind == 3, m == 15, np.where(kind == 4, m == 0, filled)))
    why = forest(rng, filled, 0.2, 0.2)
    for k, w in ((1, np.maximum(m - 1, 0)), (2, m), (5, 0 * m), (8, np.minimum(m + 1, 15)), (9, 0 * m + 15)):
        why = np.where(kind == k, w, why)
    drugs = near(rng, L, 0.3)
    low = (kind == 1) | (kind == 5); high = (kind == 8) | (kind == 9)
    top = (low & (m == np.where(hv, 0, 15))) | (high & (m == np.where(hv, 15, 0)))
    drugs = np.where(top | (kind == 3), D - 1, np.where(kind == 4, 0, drugs))
    return pack(eff, near(rng, D, 0.3), lim, drugs, why, filled)
def setup_inputs_great(rng):
    low = np.array([11, 0, 1, 0, 11, 0, 0, 11]).reshape(8, 1, 1); lane = np.arange(L)
    eff = effects(rng); rem = near(rng, D, 0.3); drugs = near(rng, L, 0.3); lim = rng.integers(6000, 20000, (N, 8))
    filled = rows(rng, rng.integers(low, 16, (N, 8, 1, L)))
    for g in (1, 6):
        eff[:, g] = rng.integers(0, 16, (N, 16, D)) < np.array([0, 1, 2, 4, 6, 8, 12, 16])[np.arange(D) % 8]
        lim[:, g] = 1
        h = np.maximum(rng.integers(-4, 8, (N, 1, L)), 0); pure = rng.random((N, 1, L)) < 0.6
        drugs[:, g] = np.where(pure, drugs[:, g] // 8 * 8 + h, drugs[:, g])
        filled[:, g] = filled[:, g] | (pure & (h == 0))
        faint = rng.random((N, 1, D)) < 0.3
        rem[:, g] = np.where(faint, rem[:, g] // 8 * 8 + rng.integers(0, 2, (N, 16, D)), rem[:, g])
    eff[:, 2] = rng.integers(0, 101, (N, 16, D)); lim[:, 2] = 1
    for q in range(N):
        o = rng.permutation(D); i = rng.integers(0, 16, L)
        eff[q, 2][:, o[:L]] = rng.integers(128, 256, (16, L))
        v = rng.choice(o[L:], (16, L)); v[i, lane] = o[:L]; drugs[q, 2] = v
        filled[q, 2][i, lane] = True
    for g in (0, 4, 7):
        eff[:, g] = rng.integers(0, 32, (N, 16, D)) + rng.integers(192, 225, (N, 1, 1))
        if g == 7:
            eff[:, g, :, 7::8] = 255
            drugs[:, g, :, L - 1] = drugs[:, g, :, L - 1] // 8 * 8 + 7
            filled[:, g, :, L - 1] = np.arange(16)[None, :] != rng.integers(0, 16, (N, 1))
        e = np.add.reduce(eff[:, g], axis=1)
        b = np.add.reduce(np.where(filled[:, g], np.take_along_axis(e, drugs[:, g].reshape(N, 16 * L), 1).reshape(N, 16, L), 0), axis=1)
        i = np.argmax(rng.random((N, L)) * (b % 128 > 0), axis=1); v = b[np.arange(N), i]
        lim[:, g] = v + (v % 256 > 128)
    lim[N - 1, 7] = 61200
    filled[0] = True; filled[2] = True
    o = rng.permutation(8 * L)[:int(rng.integers(100, 201))]
    for j in o: filled[2, j // L, :, j % L] = False
    return pack(eff, rem, lim, drugs, forest(rng, filled, 0.3, 0.3), filled)
def setup_inputs_spread(rng):
    cap = np.exp2(8 * rng.random((N, 8, 1, D))).astype(np.int64); cap = np.minimum(cap, 255)
    eff = np.minimum((rng.random((N, 8, 16, D)) * (cap + 1)).astype(np.int64), cap)
    e = rng.choice(np.array([1.0, 3.0, 8.0]), (N, 8, 1, 1))
    rem = np.minimum((D * rng.random((N, 8, 16, D)) ** 3).astype(np.int64), D - 1); drugs = np.minimum((D * rng.random((N, 8, 16, L)) ** e).astype(np.int64), D - 1)
    lim = np.minimum(np.maximum(np.exp2(16 * rng.random((N, 8))).astype(np.int64), 1), 65280); lim[:, 5] = rng.integers(3000, 9000, N)
    filled = rows(rng, rng.integers(0, 17, (N, 8, 1, L))); why = forest(rng, filled, rng.random((N, 8, 1, L)), 0.3)
    return pack(eff, rem, lim, drugs, why, filled)
def setup_inputs_ends(rng):
    eff = 255 * (rng.random((N, 8, 16, D)) < rng.choice(np.array([0.0, 0.5, 1.0]), (N, 8, 1, D))).astype(np.int64)
    case = rng.integers(0, 4, (N, 8)); case[0, 0] = 1; case[N - 1, 7] = 0; case[:, 4] = 2
    a = np.where((case == 0) | (case == 3), 255, np.where(case == 1, 0, -1))[:, :, None]; b = np.where(case == 0, 255, np.where((case == 1) | (case == 3), 0, -1))[:, :, None]
    eff[..., 0] = np.where(a >= 0, a, eff[..., 0]); eff[..., D - 1] = np.where(b >= 0, b, eff[..., D - 1])
    rem = (D - 1) * rng.integers(0, 2, (N, 8, 16, D))
    lim = np.where(rng.random((N, 8)) < 0.5, 1, 65280); lim[:, 0] = 1; lim[:, 7] = 65280
    filled = rng.random((N, 8, 16, L)) < 0.65; filled[:, :, 0] = True; filled[:, :, 15] = True
    none = rng.random((N, 8, 1, L)) < 0.05; full = rng.random((N, 8, 1, L)) < 0.1; full[..., 1] = True; full[..., L - 1] = True
    filled = full | (filled & ~none)
    drugs = np.where(rng.random((N, 8, 16, L)) < 0.7, 0, D - 1); drugs[..., 1] = 0; drugs[..., L - 1] = D - 1
    why = 15 * rng.integers(0, 2, (N, 8, 16, L)); z = rng.integers(0, 2, (N, 8, L))
    why[:, :, 0] = 15 * z; why[:, :, 15] = np.where(z == 1, 15, why[:, :, 15])
    return pack(eff, rem, lim, drugs, why, filled)
def check_inputs(d):
    bad = []
    for k, lo, hi in (("eff", 0, 255), ("rem", 0, D - 1), ("lim", 1, 65280), ("drugs", 0, D), ("why", 0, 15)):
        v = np.asarray(d[k]).astype(np.float64)
        if not (np.min(v) >= lo and np.max(v) <= hi): bad.append("range of " + k)
        elif k == "eff" and np.any(v != np.floor(v)): bad.append("whole numbers in eff")
    v = np.asarray(d["lim"]).reshape(N, 8, 16)
    if np.any(v != v[:, :, :1]): bad.append("lim alike in a group")
    if "range of drugs" in bad or "range of why" in bad: return bad
    filled = np.asarray(d["drugs"]).reshape(N, 8, 16, L) < D; w = np.asarray(d["why"]).astype(np.int64).reshape(N, 8, 16, L)
    if np.any(~filled & (w != 0)): bad.append("why is 0 in empty rows")
    if np.any(filled & ~np.take_along_axis(filled, w, 2)): bad.append("reasons are filled rows")
    c = w
    for _ in range(4): c = np.take_along_axis(c, c, 2)
    if np.any(filled & (np.take_along_axis(w, c, 2) != c)): bad.append("reasons end in a row that is its own reason")
    return bad
def stand(A, a, t):
    return np.concatenate([A[(a - S1 * t) % N][..., :H], A[(a - S2 * t) % N][..., H:]], axis=2)
def reference(eff, rem, lim, drugs, why):
    X = eff.astype(np.float32).astype(np.int32).reshape(N, 8, 16, D)
    X = np.concatenate([X, np.zeros((N, 8, 16, 1), np.int32)], axis=3)
    R = rem.astype(np.int64).reshape(N, 8, 16, D); B = lim.astype(np.int64).reshape(N, 8, 16)[:, :, :1]
    P = drugs.astype(np.int64).reshape(N, 8, 16, L); Q = why.astype(np.int64).reshape(N, 8, 16, L)
    m16 = np.arange(16)[None, :, None]; c = np.zeros(N, np.int64)
    for t in range(VI):
        NP = np.zeros_like(P); NQ = np.zeros_like(Q); stops = np.zeros(N, np.int64)
        for a in range(N):
            p = stand(P, a, t); w = stand(Q, a, t); filled = p < D
            x = np.take_along_axis(X[a], p.reshape(8, 1, 16 * L), 2).reshape(8, 16, 16, L)
            T = np.add.reduce(x, axis=2); burden = np.add.reduce(T, axis=1)
            stop = np.any(filled, axis=1) & ((burden >= B[a] + c[a]) | np.all(filled, axis=1))
            s = np.argmax(np.where(filled, np.add.reduce(x, axis=1), -1), axis=1)[:, None, :]
            cur = np.broadcast_to(m16, p.shape); reach = np.zeros(p.shape, bool)
            for _ in range(16):
                reach = reach | (cur == s); cur = np.take_along_axis(w, cur, 1)
            gone = reach & filled & stop[:, None, :]
            d = np.take_along_axis(p, s, 1)[:, 0]; xs = np.take_along_axis(x, s[:, None], 2)[:, :, 0]; xn = (xs + (T >> 4)) >> 1
            p = np.where(gone, D, p); w = np.where(gone, 0, w); filled = p < D; some = np.any(filled, axis=1)
            U = np.add.reduce(np.where(filled[:, None], x, 0), axis=2)
            f = np.argmax(U, axis=1)
            k = np.argmax(np.where(filled, np.take_along_axis(x, f[:, None, None, :], 1)[:, 0], -1), axis=1)
            dk = np.minimum(np.take_along_axis(p, k[:, None, :], 1), D - 1)
            cand = np.take_along_axis(R[a], dk, 2)
            xc = np.take_along_axis(X[a], cand.reshape(8, 1, 16 * L), 2).reshape(8, 16, 16, L)
            score = np.add.reduce(np.abs(255 - xc - (U >> 4)[:, :, None, :]), axis=1)
            new = np.take_along_axis(cand, np.argmin(score, axis=1)[:, None, :], 1)
            put = (m16 == np.argmin(filled, axis=1)[:, None, :]) & some[:, None, :]
            p = np.where(put, new, p); w = np.where(put, k[:, None, :], w)
            for A, v in ((NP, p), (NQ, w)):
                A[(a - S1 * t) % N, :, :, :H] = v[..., :H]; A[(a - S2 * t) % N, :, :, H:] = v[..., H:]
            for g in range(8):
                lanes = np.flatnonzero(stop[g]); u, i = np.unique(d[g, lanes], return_index=True)
                X[a, g][:, u] = xn[g][:, lanes[i]]
            stops[a] = np.count_nonzero(stop)
        P, Q, c = NP, NQ, stops & 255
    yp = np.stack([stand(P, a, VI - 1) for a in range(N)]); yq = np.stack([stand(Q, a, VI - 1) for a in range(N)])
    return {"yp": yp.reshape(N, 128, L).astype(np.float32), "yq": yq.reshape(N, 128, L).astype(np.float32),
            "yx": np.ascontiguousarray(X[..., :D]).reshape(N, 128, D).astype(np.float32).astype(BF)}

@@ -1,0 +1,613 @@
+import math
+from concourse.mybir import dt, AluOpType, AxisListType, ActivationFunctionType
+
+A = AluOpType
+AF = ActivationFunctionType
+N, D, NV, CH = 4, 3456, 4, 128
+PAD = 4112
+XW = PAD + 256
+MAGIC = 12582912.0
+SPL = 128
+
+POOLS = {"float32": ("pf", 4), "bfloat16": ("pb", 2), "int32": ("pi", 4), "uint16": ("pu", 2)}
+TILES, SIZE = {}, {"float32": 0, "bfloat16": 0, "int32": 0, "uint16": 0}
+
+
+def tile(name, dtype, cols):
+    b = POOLS[dtype][1]
+    per = 32 // b
+    TILES[name] = (POOLS[dtype][0], SIZE[dtype], cols)
+    SIZE[dtype] += -(-cols // per) * per
+
+
+for _n, _c in (("ONES", 256), ("IDENT", 128), ("BO", 128), ("E16", 8), ("E16N", 8), ("CONSTL", 128), ("KC", 128), ("KS", 128),
+               ("LT", 128), ("P15", 128), ("P2", 128), ("M64", 128), ("NBO", 128), ("BO4K", 128), ("I8K", 128), ("INEG", 128),
+               ("ONE16", 128), ("BIGM", 128), ("SELP", 1024), ("SELN", 1024), ("DQ", 128)):
+    tile(_n, "bfloat16", _c)
+for _n, _c in (("BOF", 128), ("MASK", 128), ("IDF", 128), ("DQF", 128), ("SELC", 8), ("DUM", 16), ("MCOL", 1), ("M64C", 1), ("THR", 1), ("THR2", 1), ("B135", 1),
+               ("PC15", 1), ("PC2", 1), ("LIMF", 1), ("THETA", 1), ("CNT", 2), ("RJ", 2048)):
+    tile(_n, "float32", _c)
+for _n, _c in (("MI", 1), ("MI2", 1), ("PCI", 1), ("PCI2", 1), ("LIMI", 1), ("CI", 1), ("CI2", 1), ("DI", 256), ("WI", 256)):
+    tile(_n, "int32", _c)
+for _h in range(2):
+    for _n in ("F1", "DHI", "DLO", "FULL", "ST", "OHS", "F2", "KP", "OHE", "NOE", "OHK", "OHD", "MBH", "MBL", "VMW"):
+        tile(_n + str(_h), "bfloat16", CH)
+    for _n in ("SC", "SCA", "D1", "D2", "T32", "U32", "Y", "W2", "MBK", "VM", "MBA", "CF", "MB2", "D3", "VMD", "XS", "AA", "F0", "FN", "WF", "E2", "BF", "T1", "T2", "YP", "YQ", "YR"):
+        tile(_n + str(_h), "float32", CH)
+    for _n in ("TI", "GI", "A2", "TF", "XN", "E2I", "BI", "BIT"):
+        tile(_n + str(_h), "int32", CH)
+    for _n in ("RED", "DC", "WM", "LL", "TT", "OFF"):
+        tile(_n + str(_h), "float32", 8)
+    for _n in ("L2", "CU"):
+        tile(_n + str(_h), "uint16", CH)
+    for _n in ("LC", "GL", "SL"):
+        tile(_n + str(_h), "uint16", 16)
+    for _t in range(NV):
+        tile("LU%d%d" % (_h, _t), "uint16", CH)
+        tile("W%d%d" % (_h, _t), "float32", CH)
+    for _t in range(1, NV):
+        tile("SLU%d%d" % (_h, _t), "uint16", CH)
+        tile("SW%d%d" % (_h, _t), "float32", CH)
+
+SCRATCH = {"X": ("sbuf", [128, XW], "bfloat16"), "Y": ("sbuf", [128, XW], "bfloat16"), "R": ("sbuf", [128, D], "int32")}
+for _d in POOLS:
+    SCRATCH[POOLS[_d][0]] = ("sbuf", [128, SIZE[_d]], _d)
+for _h in range(2):
+    for _n in ("x1", "x2", "z", "xc", "mx"):
+        SCRATCH[_n + str(_h)] = ("sbuf", [128, 16 * CH], "bfloat16")
+    SCRATCH["P0_" + str(_h)] = ("psum", [128, 512], "float32")
+    for _b in (1, 2, 3):
+        SCRATCH["P%d_%d" % (_b, _h)] = ("psum", [128, 4, CH], "float32")
+
+SEMAPHORES = ["cV", "cS", "cT", "cG"] + ["d%d" % k for k in range(40)] + \
+    ["r%d" % k for k in range(12)] + ["l%d" % k for k in range(12)]
+
+
+def rank_program(g, core, T, topo):
+    rank = T.rank_of(core)
+    if rank is None:
+        return
+    nxt, prv = T.cores[(rank + 1) % N], T.cores[(rank - 1) % N]
+    QUEUE = {"V": g.vector, "S": g.scalar, "T": g.tensor, "G": g, "Y": g.sync, "SD": g.scalar, "GD": g}
+
+    def t(name, a=0, b=None, s=None):
+        if name in TILES:
+            pool, off, cols = TILES[name]
+            b = cols if b is None else b
+            return T[pool][:, off + a:off + b:s] if s else T[pool][:, off + a:off + b]
+        return T[name][:] if b is None and a == 0 else T[name][:, a:b]
+
+    ops = []
+    last_w, readers, bank_acc = {}, {}, {}
+    dcount = [0]
+
+    def add(eng, fn, rd, wr, cost, sem=None, need=1, extra=()):
+        k = len(ops)
+        deps = {}
+        phys = {"SD": "S", "GD": "G"}.get(eng, eng)
+        comp = eng in ("V", "S", "T", "G")
+
+        def dep(o, kind):
+            if o == k:
+                return
+            if kind == "war" and comp and ops[o]["phys"] == phys and ops[o]["comp"]:
+                deps.setdefault(o, "order")
+            else:
+                deps[o] = "wait"
+        for x in rd:
+            if x in last_w:
+                dep(last_w[x], "raw")
+        for x in wr:
+            if x in last_w:
+                dep(last_w[x], "waw")
+            for o in readers.get(x, ()):
+                dep(o, "war")
+        for x in set(rd) | set(wr):
+            if x[0] == "P" and x[2:3] == "_":
+                ep = bank_acc.setdefault(x[:4], [phys, [], []])
+                if ep[0] != phys:
+                    ep[0], ep[1], ep[2] = phys, [], ep[1]
+                for o in ep[2]:
+                    dep(o, "bank")
+                if k not in ep[1]:
+                    ep[1].append(k)
+        for o in extra:
+            deps.setdefault(o, "order")
+        ops.append(dict(eng=eng, phys=phys, comp=comp, fn=fn, deps=deps, cost=cost, sem=sem, need=need))
+        for x in rd:
+            readers.setdefault(x, []).append(k)
+        for x in wr:
+            last_w[x] = k
+            readers[x] = []
+        return k
+
+    def V(fn, rd, wr, n, c=0.83):
+        return add("V", lambda: fn(g.vector), rd, wr, 0.06 + n * c / 1000)
+
+    def S(fn, rd, wr, n):
+        return add("S", lambda: fn(g.scalar), rd, wr, 0.07 + n * 0.83 / 1000)
+
+    def P(fn, rd, wr, n):
+        return add("T", lambda: fn(g.tensor), rd, wr, 0.06 + n * 0.45 / 1000)
+
+    def G(fn, rd, wr, n):
+        return add("G", lambda: fn(g), rd, wr, 0.17 + n * 1.66 / 1000)
+
+    def dma(eng, out, in_, rd, wr, lat):
+        s = "d%d" % dcount[0]
+        dcount[0] += 1
+        return add(eng, lambda: QUEUE[eng].dma_start(out, in_), rd, wr, lat, sem=s, need=16)
+
+    def ts(out, i0, s1, op0, s2=None, op1=None):
+        if s2 is None:
+            return lambda v: v.tensor_scalar(out, i0, s1, None, op0)
+        return lambda v: v.tensor_scalar(out, i0, s1, s2, op0, op1)
+
+    def tt(out, a, b, op):
+        return lambda v: v.tensor_tensor(out, a, b, op)
+
+    def cp(out, a):
+        return lambda v: v.tensor_copy(out, a)
+
+    def act(out, a, func=AF.Identity, bias=0.0, scale=1.0):
+        return lambda s: s.activation(out, a, func, bias=bias, scale=scale)
+
+    def mms(lst):
+        def f(pe):
+            r = None
+            for k, (o, l, x) in enumerate(lst):
+                r = pe.matmul(o, l, x, k == 0, k == len(lst) - 1)
+            return r
+        return f
+
+    dma("Y", t("DI"), T.drugs[:], [], ["DI"], 2.5)
+    dma("SD", t("WI"), T.why[:], [], ["WI"], 2.5)
+    NP = 4
+    PW = D // NP
+    for k in range(NP):
+        dma("Y" if k % 2 == 0 else "SD", T.X[:, k * PW:(k + 1) * PW], T.eff[:, k * PW:(k + 1) * PW], [], ["Xr%d" % k], 4.0 + 1.2 * k)
+    dma("Y", t("LIMI"), T.lim[:], [], ["LIMI"], 3)
+    dma("Y", T.R[:, :D // 2], T.rem[:, :D // 2], [], ["Ra"], 11.0)
+    dma("SD", T.R[:, D // 2:], T.rem[:, D // 2:], [], ["Rb"], 11.0)
+
+    V(lambda v: v.memset(t("ONES"), 1.0), [], ["ONES"], 128)
+    V(lambda v: v.memset(T.X[:, D:], 0.0), [], ["Xz"], 456)
+    G(lambda q: q.affine_select(t("IDENT"), t("ONES", 0, 128), [[-1, 128]], A.is_equal, 0.0, 0, 1), ["ONES"], ["IDENT"], 128)
+    G(lambda q: q.affine_select(t("BO"), t("ONES", 0, 128), [[-16, 8], [0, 16]], A.is_ge, 0.0, 0, 1), ["ONES"], ["BO"], 128)
+    G(lambda q: q.affine_select(t("BO"), t("BO"), [[16, 8], [0, 16]], A.is_ge, 0.0, 15, -1), ["BO"], ["BO"], 128)
+    G(lambda q: q.iota(t("MI"), [[0, 1]], 0, 1), [], ["MI"], 1)
+    V(ts(t("MI2"), t("MI"), 15, A.bitwise_and), ["MI"], ["MI2"], 64)
+    V(cp(t("MCOL"), t("MI2")), ["MI2"], ["MCOL"], 64)
+    LN2 = math.log(2.0)
+    S(act(t("PC15"), t("MCOL"), AF.Exp, 0.0, -LN2), ["MCOL"], ["PC15"], 1500)
+    V(ts(t("PCI"), t("PC15"), 32768.0, A.mult), ["PC15"], ["PCI"], 64)
+    V(cp(t("PC15"), t("PCI")), ["PCI"], ["PC15"], 64)
+    S(act(t("PC2"), t("MCOL"), AF.Exp, 0.0, LN2), ["MCOL"], ["PC2"], 64)
+    V(cp(t("PCI2"), t("PC2")), ["PC2"], ["PCI2"], 64)
+    V(cp(t("PC2"), t("PCI2")), ["PCI2"], ["PC2"], 64)
+    V(ts(t("DQ"), t("ONES", 0, 128), 0.0, A.mult), ["ONES"], ["DQ"], 64)
+    for k in range(8):
+        G((lambda k: lambda q: q.affine_select(t("DQ"), t("DQ"), [[0, 8], [1, 16]], A.not_equal, 1.0, 16 * k, -1))(k), ["DQ"], ["DQ"], 128)
+    V(cp(t("DQF"), t("DQ")), ["DQ"], ["DQF"], 128)
+    V(cp(t("BOF"), t("BO")), ["BO"], ["BOF"], 128)
+    for j in range(16):
+        S(act(t("RJ", j * 128, j * 128 + 128), t("BOF"), AF.Copy, 0.0, t("DQF", j, j + 1)), ["BOF", "DQF"], ["RJ%d" % j], 128)
+    for h in range(2):
+        H = str(h)
+        cs = slice(h * CH, h * CH + CH)
+        DI = t("DI", h * CH, h * CH + CH)
+        WI = t("WI", h * CH, h * CH + CH)
+        V(cp(t("LU%d0" % h), DI), ["DI"], ["LU%d0" % h], 128)
+        V(ts(t("F0" + H), DI, 3456.0, A.is_lt), ["DI"], ["F0" + H], 128)
+        V(cp(t("WF" + H), WI), ["WI"], ["WF" + H], 128)
+        V(ts(t("FN" + H), WI, t("MCOL"), A.not_equal), ["WI", "MCOL"], ["FN" + H], 128)
+        V(tt(t("FN" + H), t("FN" + H), t("F0" + H), A.mult), ["FN" + H, "F0" + H], ["FN" + H], 256)
+        S(act(t("E2" + H), t("WF" + H), AF.Exp, 0.0, LN2), ["WF" + H], ["E2" + H], 128)
+        V(cp(t("E2I" + H), t("E2" + H)), ["E2" + H], ["E2I" + H], 128)
+        V(tt(t("BF" + H), t("E2I" + H), t("FN" + H), A.mult), ["E2I" + H, "FN" + H], ["BF" + H], 256)
+        V(cp(t("BI" + H), t("BF" + H)), ["BF" + H], ["BI" + H], 128)
+    for j in range(16):
+        for h in range(2):
+            H = str(h)
+            bk = "P1_" + H
+            V(ts(t("BIT" + H), t("BI" + H), j, A.logical_shift_right, 1, A.bitwise_and), ["BI" + H], ["BIT" + H], 128)
+            P(mms([(T[bk][:, 0, :], t("RJ", j * 128, j * 128 + 128), t("BF" + H))]), ["RJ%d" % j, "BF" + H], [bk + "0"], 512)
+            V(tt(T[bk][:, 1, :], T[bk][:, 0, :], t("BIT" + H), A.mult), [bk + "0", "BIT" + H], [bk + "1"], 128)
+            V(tt(t("BI" + H), t("BF" + H), T[bk][:, 1, :], A.add), ["BF" + H, bk + "1"], ["BI" + H], 128)
+            V(tt(t("BF" + H), t("BF" + H), T[bk][:, 1, :], A.add), ["BF" + H, bk + "1"], ["BF" + H], 128)
+    for h in range(2):
+        H = str(h)
+        V(ts(t("T1" + H), t("F0" + H), t("PC2"), A.mult), ["F0" + H, "PC2"], ["T1" + H], 128)
+        V(ts(t("T2" + H), t("WF" + H), 1 / 64, A.mult), ["WF" + H], ["T2" + H], 128)
+        V(tt(t("T2" + H), t("T1" + H), t("T2" + H), A.add), ["T1" + H, "T2" + H], ["T2" + H], 256)
+        V(tt(t("W%d0" % h), t("BF" + H), t("T2" + H), A.add), ["BF" + H, "T2" + H], ["W%d0" % h], 256)
+    V(ts(t("E16"), t("BO", 0, 128, 16), 16.0, A.mult), ["BO"], ["E16"], 64)
+    V(ts(t("E16N"), t("BO", 0, 128, 16), -32.0, A.mult), ["BO"], ["E16N"], 64)
+    V(cp(t("SELC"), t("BO", 0, 128, 16)), ["BO"], ["SELC"], 64)
+    G(lambda q: q.affine_select(t("CONSTL"), t("ONES", 0, 128), [[0, 128]], A.is_ge, 0.0, 1, -1), ["ONES"], ["CONSTL"], 128)
+    G(lambda q: q.iota(t("KC"), [[0, 8], [-1, 16]], 15, 0, allow_small_or_imprecise_dtypes=True), [], ["KC"], 128)
+    G(lambda q: q.affine_select(t("KS"), t("KC"), [[0, 128]], A.is_ge, 131072.0, 0, -1), ["KC"], ["KS"], 128)
+    G(lambda q: q.affine_select(t("KC"), t("KC"), [[0, 128]], A.is_ge, 0.0, 0, -1), ["KC"], ["KC"], 128)
+    EPS = 2.0 ** -8
+    G(lambda q: q.affine_select(t("LT"), t("BO"), [[1, 128]], A.is_gt, EPS, 0, -1), ["BO"], ["LT"], 128)
+    G(lambda q: q.affine_select(t("LT"), t("LT"), [[1, 128]], A.not_equal, -32.0, 0, -1), ["LT"], ["LT"], 128)
+    V(tt(t("LT"), t("LT"), t("BO"), A.mult), ["LT", "BO"], ["LT"], 256)
+    V(ts(t("THR"), t("MCOL"), 0.5, A.subtract, EPS / 2, A.max), ["MCOL"], ["THR"], 64)
+    V(ts(t("THR2"), t("MCOL"), 0.46875 * (1 - EPS), A.mult, 0.46875 * (15 * EPS - 32), A.add), ["MCOL"], ["THR2"], 64)
+    V(tt(t("THR"), t("THR"), t("THR2"), A.add), ["THR", "THR2"], ["THR"], 64)
+    V(ts(t("P15"), t("BO"), t("PC15"), A.mult), ["BO", "PC15"], ["P15"], 64)
+    V(ts(t("P2"), t("BO"), t("PC2"), A.mult), ["BO", "PC2"], ["P2"], 64)
+    V(ts(t("M64C"), t("MCOL"), 1 / 64, A.mult), ["MCOL"], ["M64C"], 64)
+    V(ts(t("M64"), t("BO"), t("M64C"), A.mult), ["BO", "M64C"], ["M64"], 64)
+    V(ts(t("NBO"), t("BO"), -1.0, A.mult), ["BO"], ["NBO"], 64)
+    V(ts(t("BO4K"), t("BO"), 4096.0, A.mult), ["BO"], ["BO4K"], 64)
+    V(ts(t("I8K"), t("IDENT"), 8192.0, A.mult), ["IDENT"], ["I8K"], 64)
+    V(ts(t("INEG"), t("IDENT"), -131072.0, A.mult), ["IDENT"], ["INEG"], 64)
+    V(lambda v: v.memset(t("ONE16"), 1 / 16), [], ["ONE16"], 64)
+    V(ts(t("B135"), t("MCOL"), -1.0, A.mult, 135.0, A.add), ["MCOL"], ["B135"], 64)
+    V(lambda v: v.memset(t("MASK"), 1.0), [], ["MASK"], 128)
+    V(lambda v: v.memset(t("MASK", 0, 128, 16), 0.0), [], ["MASK"], 64)
+    V(cp(t("IDF"), t("IDENT")), ["IDENT"], ["IDF"], 128)
+    V(ts(t("BIGM"), t("ONES", 0, 128), 65536.0, A.mult), ["ONES"], ["BIGM"], 64)
+    G(lambda q: q.affine_select(t("BIGM"), t("BIGM"), [[1, 128]], A.is_ge, 0.0, 0, -1), ["BIGM"], ["BIGM"], 128)
+    for w in range(8):
+        V(ts(t("SELP", w * 128, w * 128 + 128), t("ONES", 0, 128), t("SELC", w, w + 1), A.mult), ["ONES", "SELC"], ["SELP%d" % w], 64)
+        V(ts(t("SELN", w * 128, w * 128 + 128), t("ONES", 0, 128), t("SELC", w, w + 1), A.mult, -1.0, A.mult), ["ONES", "SELC"], ["SELN%d" % w], 64)
+    G(lambda q: q.iota(t("DUM"), [[16, 16]], PAD + 1, 0, allow_small_or_imprecise_dtypes=True), [], ["DUM"], 16)
+    V(ts(t("DUM"), t("DUM"), t("MCOL"), A.add), ["DUM", "MCOL"], ["DUM"], 64)
+    for k in range(NP):
+        sl = T.X[:, k * PW:(k + 1) * PW]
+        V(ts(sl, sl, 1.0, A.add), ["Xr%d" % k], ["Xr%d" % k], PW / 2)
+    V(cp(t("LIMF"), t("LIMI")), ["LIMI"], ["LIMF"], 64)
+    V(ts(t("THETA"), t("LIMF"), 120.0, A.subtract), ["LIMF"], ["THETA"], 64)
+    XK = ["Xr%d" % k for k in range(NP)] + ["Xz"]
+    XALL = T.X[:]
+    arrive = {}
+
+    def gather(dst, lst, lkey, h):
+        w = []
+        for (e, a, b) in (("S", 0, SPL), ("V", SPL, CH)):
+            if a < b:
+                key = "%s%d:%s" % (dst, h, e)
+                o, s = T[dst + str(h)][:, 16 * a:16 * b], XALL.indirect(t(lst, a, b))
+                if e == "S":
+                    S(act(o, s, AF.Copy), XK + [lkey], [key], 16 * (b - a) * 1.5)
+                else:
+                    V(cp(o, s), XK + [lkey], [key], 16 * (b - a) * 1.5)
+                w.append(key)
+        return w
+
+    def argmax(h, srckeys):
+        H = str(h)
+        p0 = T["P0_" + H]
+        V(lambda v: v.tensor_tensor_scan(t("SCA" + H), t("MASK"), p0[:, 0:128], 0.0, A.mult, A.max), srckeys + ["MASK"], ["SCA" + H], 128)
+        V(lambda v: v.tensor_tensor_scan(t("SC" + H)[:, ::-1], t("MASK"), t("SCA" + H)[:, ::-1], 0.0, A.mult, A.max), ["SCA" + H, "MASK"], ["SC" + H], 128)
+        V(tt(t("OHD" + H), p0[:, 0:128], t("SC" + H), A.is_equal), srckeys + ["SC" + H], ["OHD" + H], 128)
+
+    def phase1(vt, h):
+        H = str(h)
+        LU, W = "LU%d%d" % (h, vt), "W%d%d" % (h, vt)
+        p0, p1, p2, p3 = T["P0_" + H], T["P1_" + H], T["P2_" + H], T["P3_" + H]
+        x = T["x1" + H]
+        kx = gather("x1", LU, LU, h)
+        V(ts(t("D1" + H), t(LU), 1.0, A.add), [LU], ["D1" + H], 128)
+        V(ts(t("F1" + H), t("D1" + H), 3457.0, A.is_lt, 0.46875, A.add), ["D1" + H], ["F1" + H], 128)
+        S(act(t("DHI" + H), t("D1" + H), AF.Copy), ["D1" + H], ["DHI" + H], 128)
+        V(tt(t("DLO" + H), t("D1" + H), t("DHI" + H), A.subtract), ["D1" + H, "DHI" + H], ["DLO" + H], 256)
+        P(mms([(p1[:, 3, :], t("BO"), t("F1" + H))]), ["BO", "F1" + H], ["P1_%s3" % H], 128)
+        V(ts(t("FULL" + H), p1[:, 3, :], 23.0, A.is_ge), ["P1_%s3" % H], ["FULL" + H], 128)
+        P(mms([(p0[:, 0:128], t("CONSTL"), t("KC"))] + [(p0[:, m:128:16], x[:, m::16], t("E16")) for m in range(16)]),
+          ["CONSTL", "KC", "E16"] + kx, ["P0_" + H], 128 + 16 * 64)
+        argmax(h, ["P0_" + H])
+        P(mms([(p3[:, 0, :], t("IDENT"), x[:, m::16]) for m in range(16)] + [(p3[:, 0, :], t("NBO"), t("F1" + H))]),
+          ["IDENT", "NBO", "F1" + H] + kx, ["P3_%s0" % H], 17 * 128)
+        S(act(t("T32" + H), p3[:, 0, :], AF.Copy), ["P3_%s0" % H], ["T32" + H], 128)
+        P(mms([(p3[:, 1, :], t("BOF"), t("T32" + H)), (p3[:, 1, :], t("BO4K"), t("FULL" + H))]),
+          ["BOF", "T32" + H, "BO4K", "FULL" + H], ["P3_%s1" % H], 640)
+        V(ts(t("ST" + H), p3[:, 1, :], t("THETA"), A.is_ge), ["P3_%s1" % H, "THETA"], ["ST" + H], 128)
+        P(mms([(p1[:, 0, :], t("OHD" + H), t("IDENT"))]), ["OHD" + H, "IDENT"], ["P1_%s0" % H], 128)
+        V(tt(t("OHS" + H), p1[:, 0, :], t("ST" + H), A.mult), ["P1_%s0" % H, "ST" + H], ["OHS" + H], 128)
+        P(mms([(p1[:, 1, :], t("P15"), t("OHS" + H))]), ["P15", "OHS" + H], ["P1_%s1" % H], 128)
+        V(tt(t("TI" + H), t(W), p1[:, 1, :], A.mult), [W, "P1_%s1" % H], ["TI" + H], 128)
+        V(ts(t("GI" + H), t("TI" + H), 3, A.logical_shift_right, 4096, A.bitwise_and), ["TI" + H], ["GI" + H], 128)
+        V(tt(t("D2" + H), t("D1" + H), t("GI" + H), A.max), ["D1" + H, "GI" + H], ["D2" + H], 256)
+        V(ts(t("L2" + H), t("D2" + H), 1.0, A.subtract), ["D2" + H], ["L2" + H], 128)
+
+    def phase2(vt, h):
+        H = str(h)
+        LU, W = "LU%d%d" % (h, vt), "W%d%d" % (h, vt)
+        p0, p1, p2, p3 = T["P0_" + H], T["P1_" + H], T["P2_" + H], T["P3_" + H]
+        x = T["x2" + H]
+        kx = gather("x2", "L2" + H, "L2" + H, h)
+        V(ts(t("F2" + H), t("D2" + H), 3457.0, A.is_lt, 0.46875, A.add), ["D2" + H], ["F2" + H], 128)
+        V(ts(t("KP" + H), t("D2" + H), 3457.0, A.is_lt), ["D2" + H], ["KP" + H], 128)
+        P(mms([(p1[:, 2, :], t("LT"), t("F2" + H))]), ["LT", "F2" + H], ["P1_%s2" % H], 128)
+        V(ts(t("OHE" + H), p1[:, 2, :], t("THR"), A.is_ge), ["P1_%s2" % H, "THR"], ["OHE" + H], 128)
+        V(ts(t("NOE" + H), p1[:, 2, :], t("THR"), A.is_lt), ["P1_%s2" % H, "THR"], ["NOE" + H], 128)
+        V(tt(t("W2" + H), t(W), t("KP" + H), A.mult), [W, "KP" + H], ["W2" + H], 256)
+        V(cp(t("A2" + H), t("W2" + H)), ["W2" + H], ["A2" + H], 128)
+        P(mms([(p3[:, 2, :], t("IDENT"), x[:, m::16]) for m in range(16)] + [(p3[:, 2, :], t("NBO"), t("F2" + H))]),
+          ["IDENT", "NBO", "F2" + H] + kx, ["P3_%s2" % H], 17 * 128)
+        S(act(t("U32" + H), p3[:, 2, :], AF.Identity, t("B135"), 16.0), ["P3_%s2" % H, "B135"], ["U32" + H], 128)
+        S(act(t("Y" + H), p3[:, 2, :], AF.Identity, MAGIC, 1 / 16), ["P3_%s2" % H], ["Y" + H], 128)
+        P(mms([(p0[:, 0:128], t("U32" + H), t("IDF"))]), ["U32" + H, "IDF"], ["P0_" + H], 512)
+        S(act(p3[:, 1, :], t("Y" + H), AF.Identity, MAGIC + 256, -1.0), ["Y" + H], ["P3_%s1" % H], 128)
+        argmax(h, ["P0_" + H])
+        P(mms([(p3[:, 3, :], t("OHD" + H), t("IDENT"))]), ["OHD" + H, "IDENT"], ["P3_%s3" % H], 128)
+
+    def phase3(vt, h):
+        H = str(h)
+        p0, p1, p2, p3 = T["P0_" + H], T["P1_" + H], T["P2_" + H], T["P3_" + H]
+        x, z = T["x2" + H], T["z" + H]
+        kx = ["x2%d:S" % h] + (["x2%d:V" % h] if SPL < CH else [])
+        for q in range(2):
+            ms = range(8 * q, 8 * q + 8)
+
+            def kf(v, ms=ms):
+                for m in ms:
+                    r = v.tensor_tensor(z[:, m::16], x[:, m::16], p3[:, 3, :], A.mult)
+                return r
+            V(kf, kx + ["P3_%s3" % H], ["z%s:%d" % (H, q)], 8 * 128)
+
+            def yf(pe, q=q, ms=ms):
+                if q == 0:
+                    pe.matmul(p0[:, 0:128], t("CONSTL"), t("KC"), True, False)
+                for m in ms:
+                    r = pe.matmul(p0[:, m:128:16], z[:, m::16], t("E16"), False, m == 15)
+                return r
+            P(yf, ["CONSTL", "KC", "E16", "z%s:%d" % (H, q)], ["P0_" + H], 128 * (1 - q) + 8 * 64)
+        argmax(h, ["P0_" + H])
+        P(mms([(p1[:, 0, :], t("OHD" + H), t("IDENT"))]), ["OHD" + H, "IDENT"], ["P1_%s0" % H], 128)
+        V(tt(t("MBK" + H), p1[:, 0, :], t("D2" + H), A.mult), ["P1_%s0" % H, "D2" + H], ["MBK" + H], 128)
+        V(tt(t("MBA" + H), p1[:, 0, :], t("A2" + H), A.mult), ["P1_%s0" % H, "A2" + H], ["MBA" + H], 128)
+        S(act(t("OHK" + H), p1[:, 0, :], AF.Copy), ["P1_%s0" % H], ["OHK" + H], 128)
+        P(mms([(p1[:, 1, :], t("MBK" + H), t("BOF"))]), ["MBK" + H, "BOF"], ["P1_%s1" % H], 512)
+        V(tt(t("VM" + H), p1[:, 1, :], t("DQF"), A.mult), ["P1_%s1" % H, "DQF"], ["VM" + H], 128)
+        P(mms([(p1[:, 3, 0:8], t("VM" + H), t("SELC"))]), ["VM" + H, "SELC"], ["P1_%s3" % H], 256)
+        V(ts(t("LC" + H, 0, 8), p1[:, 3, 0:8], 1.0, A.subtract, 3455.0, A.min), ["P1_%s3" % H], ["LC" + H], 64)
+        V(cp(t("CU" + H), T.R[:].indirect(t("LC" + H, 0, 8))), ["Ra", "Rb", "LC" + H], ["CU" + H], 200)
+
+    def phase4(vt, h):
+        H = str(h)
+        p0, p1, p2, p3 = T["P0_" + H], T["P1_" + H], T["P2_" + H], T["P3_" + H]
+        xc, mx = T["xc" + H], T["mx" + H]
+        hs = CH // 2
+        for q in range(2):
+            S(act(xc[:, 16 * hs * q:16 * hs * (q + 1)], XALL.indirect(t("CU" + H, hs * q, hs * q + hs)), AF.Copy),
+              XK + ["CU" + H], ["xc%s:%d" % (H, q)], 16 * hs * 1.5)
+        V(ts(t("CF" + H), t("CU" + H), 1.0, A.add), ["CU" + H], ["CF" + H], 128)
+        P(mms([(p1[:, 2, :], t("BOF"), t("MBA" + H)), (p1[:, 2, :], t("M64"), t("OHK" + H)), (p1[:, 2, :], t("P2"), t("OHE" + H)),
+               (p1[:, 2, :], t("INEG"), t("NOE" + H))]),
+          ["BOF", "MBA" + H, "M64", "OHK" + H, "P2", "OHE" + H, "INEG", "NOE" + H], ["P1_%s2" % H], 900)
+        last = vt == NV - 1
+        WN = ("SW%d%d" % (h, vt + 1)) if not last else "W2" + H
+        V(tt(t(WN), t("W2" + H), p1[:, 2, :], A.max), ["W2" + H, "P1_%s2" % H], [WN], 128)
+        if not last:
+            send(WN, "W%d%d" % (h, vt + 1), 6 * h + 2 * vt)
+        for q in range(2):
+            for b in range(2 if q else 1):
+                js = range(8 * b, 8 * b + 8) if q else range(16)
+
+                def mf(v, q=q, js=js):
+                    for j in js:
+                        lo, hi = 16 * hs * q + j, 16 * hs * (q + 1)
+                        r = v.tensor_tensor(mx[:, lo:hi:16], xc[:, lo:hi:16], p3[:, 1, hs * q:hs * q + hs], A.max)
+                    return r
+                V(mf, ["xc%s:%d" % (H, q), "P3_%s1" % H], ["mx%s:%d%d" % (H, q, b)], 64 * len(js))
+
+        def sf0(pe):
+            r = pe.matmul(p0[:, 0:128], t("CONSTL"), t("KS"), True, False)
+            for j in range(16):
+                r = pe.matmul(p0[:, j:128:16], xc[:, j::16], t("E16"), False, False)
+            return r
+        P(sf0, ["CONSTL", "KS", "E16", "xc%s:0" % H, "xc%s:1" % H], ["P0_" + H], 128 + 1024)
+        for b in range(2):
+            def sf(pe, b=b):
+                for j in range(8 * b, 8 * b + 8):
+                    r = pe.matmul(p0[:, j:128:16], mx[:, j::16], t("E16N"), False, j == 15)
+                return r
+            P(sf, ["E16N", "mx%s:00" % H, "mx%s:1%d" % (H, b)], ["P0_" + H], 512)
+        argmax(h, ["P0_" + H])
+        P(mms([(p1[:, 0, :], t("OHD" + H), t("IDENT"))]), ["OHD" + H, "IDENT"], ["P1_%s0" % H], 128)
+        V(tt(t("MB2" + H), p1[:, 0, :], t("CF" + H), A.mult), ["P1_%s0" % H, "CF" + H], ["MB2" + H], 128)
+        P(mms([(p1[:, 1, :], t("BOF"), t("MB2" + H)), (p1[:, 1, :], t("I8K"), t("NOE" + H))]),
+          ["BOF", "MB2" + H, "I8K", "NOE" + H], ["P1_%s1" % H], 640)
+        V(tt(t("D3" + H), t("D2" + H), p1[:, 1, :], A.min), ["D2" + H, "P1_%s1" % H], ["D3" + H], 128)
+        if not last:
+            LN = "SLU%d%d" % (h, vt + 1)
+            V(ts(t(LN), t("D3" + H), 1.0, A.subtract), ["D3" + H], [LN], 128)
+            send(LN, "LU%d%d" % (h, vt + 1), 6 * h + 2 * vt + 1)
+        else:
+            V(ts(t("YP" + H), t("D3" + H), 1.0, A.subtract, 3456.0, A.min), ["D3" + H], ["YP" + H], 128)
+            dma("Y", T.yp[:, h * CH:h * CH + CH], t("YP" + H), ["YP" + H], [], 2.5)
+            V(cp(t("A2" + H), t("W2" + H)), ["W2" + H], ["A2" + H], 128)
+            V(tt(t("YQ" + H), t("W2" + H), t("A2" + H), A.subtract), ["W2" + H, "A2" + H], ["YQ" + H], 256)
+            V(ts(t("YR" + H), t("YQ" + H), 64.0, A.mult), ["YQ" + H], ["YR" + H], 128)
+            dma("Y", T.yq[:, h * CH:h * CH + CH], t("YR" + H), ["YR" + H], [], 2.5)
+
+    locals_used = []
+
+    def send(src, dst, k):
+        mask, n = topo.mask(core, nxt), len(topo.engines(core, nxt))
+        rid, pid = topo.addr(nxt)[:2]
+        o = add("G", lambda: g.remote_dma(t(dst), t(src), T.sem["r%d" % k], T.sem["l%d" % k], pid, rid, mask), [src], [], 1.0, sem="l%d" % k, need=n)
+        ops[o]["comp"] = False
+        ops[o]["remote"] = True
+        locals_used.append(o)
+        ni = len(topo.engines(prv, core))
+        a = add("N", None, [], [dst], 2.5, sem="r%d" % k, need=ni, extra=[o])
+        ops[a]["comp"] = False
+
+    def dedup(vt, h):
+        H = str(h)
+        q2 = "P2_" + H
+        p2 = T[q2]
+        V(tt(t("MBH" + H), t("OHS" + H), t("DHI" + H), A.mult), ["OHS" + H, "DHI" + H], ["MBH" + H], 256)
+        V(tt(t("MBL" + H), t("OHS" + H), t("DLO" + H), A.mult), ["OHS" + H, "DLO" + H], ["MBL" + H], 256)
+        P(mms([(p2[:, 0, :], t("MBH" + H), t("BO")), (p2[:, 0, :], t("MBL" + H), t("BO"))]), ["MBH" + H, "MBL" + H, "BO"], [q2 + "0"], 256)
+        P(mms([(p2[:, 2, :], t("ONE16"), t("ST" + H))]), ["ONE16", "ST" + H], [q2 + "2"], 128)
+        V(tt(t("VMD" + H), p2[:, 0, :], t("DQF"), A.mult), [q2 + "0", "DQF"], ["VMD" + H], 128)
+        if vt < NV - 1:
+            S(lambda s: s.activation(t("AA" + H), p2[:, 2, :], AF.Copy, accum_out=t("CNT", h, h + 1)), [q2 + "2"], ["AA" + H, "CNT" + H], 160)
+        P(mms([(p2[:, 1, 0:8], t("VMD" + H), t("SELC"))]), ["VMD" + H, "SELC"], [q2 + "1"], 256)
+        V(cp(t("DC" + H), p2[:, 1, 0:8]), [q2 + "1"], ["DC" + H], 64)
+        V(ts(t("GL" + H, 0, 8), t("DC" + H), 1.0, A.subtract), ["DC" + H], ["GL" + H], 64)
+        for w in range(8):
+            b = "P2_%d" % (w // 4)
+            o = T[b][:, w % 4, :]
+            P(mms([(o, t("SELP", w * 128, w * 128 + 128), t("MBH" + H)), (o, t("SELP", w * 128, w * 128 + 128), t("MBL" + H)),
+                   (o, t("MBH" + H), t("SELN", w * 128, w * 128 + 128)), (o, t("MBL" + H), t("SELN", w * 128, w * 128 + 128)),
+                   (o, t("IDENT"), t("BIGM"))]),
+              ["SELP%d" % w, "SELN%d" % w, "MBH" + H, "MBL" + H, "IDENT", "BIGM"], [b + str(w % 4)], 640)
+            if w % 4 == 3:
+                for u in range(w - 3, w + 1):
+                    V((lambda u, b: lambda v: v.tensor_reduce(t("RED" + H, u, u + 1), T[b][:, u % 4, :], AxisListType.X, A.min,
+                                                              apply_absolute_value=True))(u, b), [b + str(u % 4)], ["RED%s%d" % (H, u)], 128)
+        for w in range(8):
+            S(act(t("VMW" + H, 16 * w, 16 * w + 16), t("DQ", 0, 16), AF.Copy, 0.0, t("RED" + H, w, w + 1)), ["DQ", "RED%s%d" % (H, w)], ["VMW%s%d" % (H, w)], 16)
+        P(mms([(p2[:, 3, 0:8], t("VMW" + H), t("BO", 0, 128, 16))]), ["VMW%s%d" % (H, w) for w in range(8)] + ["BO"], [q2 + "3"], 64)
+        V(tt(t("WM" + H), p2[:, 3, 0:8], t("DC" + H), A.min), [q2 + "3", "DC" + H], ["WM" + H], 64)
+        V(ts(t("LL" + H), t("WM" + H), 0.5, A.is_lt), ["WM" + H], ["LL" + H], 64)
+        V(tt(t("TT" + H), t("LL" + H), t("DUM", 8 * h, 8 * h + 8), A.mult), ["LL" + H, "DUM"], ["TT" + H], 64)
+        V(tt(t("OFF" + H), t("TT" + H), t("DC" + H), A.max), ["TT" + H, "DC" + H], ["OFF" + H], 64)
+        V(ts(t("SL" + H, 0, 8), t("OFF" + H), 1.0, A.subtract), ["OFF" + H], ["SL" + H], 64)
+        V(ts(t("TF" + H), t("T32" + H), 1 / 16, A.mult), ["T32" + H], ["TF" + H], 128)
+        S(act(t("XS" + H), XALL.indirect(t("GL" + H, 0, 8)), AF.Copy), XK + ["GL" + H], ["XS" + H], 200)
+        V(tt(t("AA" + H), t("XS" + H), t("TF" + H), A.add), ["XS" + H, "TF" + H], ["AA" + H], 256)
+        V(ts(t("XN" + H), t("AA" + H), 0.5, A.mult, 0.25 if vt < NV - 1 else -0.75, A.add), ["AA" + H], ["XN" + H], 128)
+
+    def update(vt):
+        if vt < NV - 1:
+            V(tt(t("CI"), t("CNT", 0, 1), t("CNT", 1, 2), A.add), ["CNT0", "CNT1"], ["CI"], 64)
+            V(ts(t("CI2"), t("CI"), 255, A.bitwise_and), ["CI"], ["CI2"], 64)
+            V(ts(t("THETA"), t("CI2"), t("LIMF"), A.add, 120.0, A.subtract), ["CI2", "LIMF"], ["THETA"], 64)
+        dst, keys = (T.X[:], XK) if vt < NV - 1 else (T.Y[:], ["Y%d" % k for k in range(NP)] + ["Yz"])
+        for h in (1, 0):
+            H = str(h)
+            V(cp(dst.indirect(t("SL" + H, 0, 8)), t("XN" + H)), ["SL" + H, "XN" + H], keys, 128 * 3)
+
+    for vt in range(NV):
+        if vt == NV - 1:
+            V(lambda v: v.memset(T.Y[:, D:], 0.0), [], ["Yz"], 456)
+            for k in range(NP):
+                S(act(T.Y[:, k * PW:(k + 1) * PW], T.X[:, k * PW:(k + 1) * PW], AF.Identity, -1.0, 1.0), XK, ["Y%d" % k], PW)
+        for h in range(2):
+            phase1(vt, h)
+        for h in range(2):
+            phase2(vt, h)
+        for h in range(2):
+            phase3(vt, h)
+        if vt == NV - 1:
+            for h in range(2):
+                dedup(vt, h)
+            update(vt)
+            for k in range(NP):
+                dma("Y", T.yx[:, k * PW:(k + 1) * PW], T.Y[:, k * PW:(k + 1) * PW], ["Y%d" % k], [], 4.0)
+        for h in range(2):
+            phase4(vt, h)
+        if vt < NV - 1:
+            for h in range(2):
+                dedup(vt, h)
+            update(vt)
+
+    order = schedule(ops)
+    emit(g, T, ops, order, QUEUE)
+
+
+def schedule(ops):
+    n = len(ops)
+    succ = [[] for _ in range(n)]
+    for k, o in enumerate(ops):
+        for d in o["deps"]:
+            succ[d].append(k)
+    WAKE = 0.12
+    tail = [0.0] * n
+    for k in range(n - 1, -1, -1):
+        tail[k] = ops[k]["cost"] + max([tail[s] + WAKE for s in succ[k]] + [0.0])
+    left = [len(o["deps"]) for o in ops]
+    ready, fin, free = {}, [0.0] * n, {}
+    for k in range(n):
+        if left[k] == 0:
+            ready.setdefault(ops[k]["phys"], []).append((0.0, k))
+    order = []
+    while ready:
+        best = None
+        for e, lst in ready.items():
+            f = free.get(e, 0.0)
+            t0 = min(max(f, r) for r, k in lst)
+            c = max((tail[k], -k) for r, k in lst if max(f, r) <= t0 + 0.03)
+            if best is None or t0 < best[0]:
+                best = (t0, e, -c[1])
+        t0, e, k = best
+        lst = ready[e]
+        st = max(free.get(e, 0.0), [r for r, q in lst if q == k][0])
+        lst[:] = [x for x in lst if x[1] != k]
+        if not lst:
+            del ready[e]
+        o = ops[k]
+        fin[k] = st + o["cost"]
+        if e != "N":
+            free[e] = st + (o["cost"] if o["comp"] else (0.1 if o["eng"] != "G" else 1.0))
+        order.append(k)
+        for s in succ[k]:
+            left[s] -= 1
+            if left[s] == 0:
+                r = max([fin[d] + (WAKE if ops[s]["deps"][d] == "wait" else 0.0) for d in ops[s]["deps"]])
+                ready.setdefault(ops[s]["phys"], []).append((r, s))
+    order_time = {k: fin[k] for k in order}
+    ops[0]["makespan"] = max(fin)
+    ops[0]["fin"] = order_time
+    return order
+
+
+def emit(g, T, ops, order, QUEUE):
+    know = {e: {} for e in ("V", "S", "T", "G", "Y")}
+    cnt = {}
+    for k in order:
+        o = ops[k]
+        e = o["phys"]
+        if e == "N":
+            o["sig"] = (o["sem"], o["need"])
+            o["kn"] = {}
+            continue
+        q = QUEUE[o["eng"]]
+        kn = know[e]
+        waits = {}
+        for d in sorted(o["deps"], key=lambda d: -order.index(d) if len(order) < 50 else -d):
+            if o["deps"][d] != "wait":
+                continue
+            s, v = ops[d]["sig"]
+            if kn.get(s, 0) >= v:
+                continue
+            waits[s] = max(waits.get(s, 0), v)
+        src = {}
+        for d in o["deps"]:
+            if o["deps"][d] == "wait":
+                s, v = ops[d]["sig"]
+                if s in waits and waits[s] == v:
+                    src[s] = d
+        for s in list(waits):
+            if any(s2 != s and ops[src[s2]]["kn"].get(s, 0) >= waits[s] for s2 in waits):
+                del waits[s]
+        for s in sorted(waits):
+            q.wait_ge(T.sem[s], waits[s])
+            for a, b in ops[src[s]]["kn"].items():
+                kn[a] = max(kn.get(a, 0), b)
+            kn[s] = max(kn.get(s, 0), waits[s])
+        ins = o["fn"]()
+        if o["comp"]:
+            s = "c" + e
+            cnt[s] = cnt.get(s, 0) + 1
+            ins.then_inc(T.sem[s], 1)
+            o["sig"] = (s, cnt[s])
+        elif o.get("remote"):
+            o["sig"] = (o["sem"], o["need"])
+        else:
+            ins.then_inc(T.sem[o["sem"]], 16)
+            o["sig"] = (o["sem"], 16)
+        o["kn"] = dict(kn)
+    for s in sorted(cnt):
+        g.wait_ge(T.sem[s], cnt[s])
+    for o in ops:
+        if not o["comp"] and o["phys"] != "N":
+            g.wait_ge(T.sem[o["sig"][0]], o["sig"][1])

@@ -7,41 +7,51 @@ N, D, NV, CH = 4, 3456, 4, 128
 PAD = 4112
 XW = PAD + 256
 MAGIC = 12582912.0
-SPL = 128
+BIG = 131072.0
+KK = 4194304.0
+NP = 4
+PW = D // NP
+HALF = (("S", 0, 64), ("V", 64, 128))
+SHARE = {"f0": (("S", 0, 32), ("V", 32, 64), ("S", 64, 96), ("V", 96, 128)), "f1": (("S", 0, 32), ("V", 32, 64), ("S", 64, 96), ("V", 96, 128)),
+         "a0": HALF, "a1": HALF, "x2": HALF, "xc": HALF}
+BONUS = [3, 7, 6, 9, 7, 4, 2, 5, 5]
 
 POOLS = {"float32": ("pf", 4), "bfloat16": ("pb", 2), "int32": ("pi", 4), "uint16": ("pu", 2)}
 TILES, SIZE = {}, {"float32": 0, "bfloat16": 0, "int32": 0, "uint16": 0}
 
 
 def tile(name, dtype, cols):
-    b = POOLS[dtype][1]
-    per = 32 // b
+    per = 32 // POOLS[dtype][1]
     TILES[name] = (POOLS[dtype][0], SIZE[dtype], cols)
     SIZE[dtype] += -(-cols // per) * per
 
 
-for _n, _c in (("ONES", 256), ("IDENT", 128), ("BO", 128), ("E16", 8), ("E16N", 8), ("CONSTL", 128), ("KC", 128), ("KS", 128),
-               ("LT", 128), ("P15", 128), ("P2", 128), ("M64", 128), ("NBO", 128), ("BO4K", 128), ("I8K", 128), ("INEG", 128),
-               ("ONE16", 128), ("BIGM", 128), ("SELP", 1024), ("SELN", 1024), ("DQ", 128)):
+for _n, _c in (("ONES", 128), ("IDENT", 128), ("BO", 128), ("E16", 8), ("E16N", 8), ("CONSTL", 128), ("KC", 128), ("KS", 128),
+               ("KM", 128), ("K8", 128), ("LT", 128), ("P15", 128), ("P2", 128), ("M64", 128), ("NBO", 128), ("BO4K", 128),
+               ("I8N", 128), ("IBIG", 128), ("NID", 128), ("ONE16", 128), ("BIGM", 128), ("SELP", 1024),
+               ("SELN", 1024), ("DQ", 128), ("ZA", 128), ("ZB", 128)):
     tile(_n, "bfloat16", _c)
-for _n, _c in (("BOF", 128), ("MASK", 128), ("IDF", 128), ("DQF", 128), ("SELC", 8), ("DUM", 16), ("MCOL", 1), ("M64C", 1), ("THR", 1), ("THR2", 1), ("B135", 1),
-               ("PC15", 1), ("PC2", 1), ("LIMF", 1), ("THETA", 1), ("CNT", 2), ("RJ", 2048)):
+for _n, _c in (("BOF", 128), ("MASK", 128), ("IDF", 128), ("DQF", 128), ("SELC", 8), ("DUM", 16), ("MCOL", 1), ("M64C", 1),
+               ("THR", 1), ("THR2", 1), ("B135", 1), ("PC15", 1), ("PC2", 1), ("LIMF", 1), ("THETA", 1), ("CNT", 2), ("RJ", 2048),
+               ("QROW", 128), ("MB1", 1), ("PB1", 1), ("JB", 16), ("DC", 16), ("WM", 16), ("LL", 16), ("TT", 16), ("OFF", 16)):
     tile(_n, "float32", _c)
-for _n, _c in (("MI", 1), ("MI2", 1), ("PCI", 1), ("PCI2", 1), ("LIMI", 1), ("CI", 1), ("CI2", 1), ("DI", 256), ("WI", 256)):
+for _n, _c in (("MI", 1), ("MI2", 1), ("PCI", 1), ("PCI2", 1), ("LIMI", 1), ("CI", 1), ("CI2", 1), ("DI", 256), ("WI", 256), ("XN", 256)):
     tile(_n, "int32", _c)
+tile("XS", "bfloat16", 256)
+tile("GL", "uint16", 16)
+tile("SL", "uint16", 16)
 for _h in range(2):
-    for _n in ("F1", "DHI", "DLO", "FULL", "ST", "OHS", "F2", "KP", "OHE", "NOE", "OHK", "OHD", "MBH", "MBL", "VMW"):
+    for _n in ("F1", "DHI", "DLO", "FULL", "ST", "OHS", "F2", "OHE", "OHK", "OHD", "MBH", "MBL", "VMW", "VB", "SG", "TFB", "Z"):
         tile(_n + str(_h), "bfloat16", CH)
-    for _n in ("SC", "SCA", "D1", "D2", "T32", "U32", "Y", "W2", "MBK", "VM", "MBA", "CF", "MB2", "D3", "VMD", "XS", "AA", "F0", "FN", "WF", "E2", "BF", "T1", "T2", "YP", "YQ", "YR"):
+    for _n in ("SC", "SCA", "D1", "D2", "T32", "U32", "Y", "W2", "MBK", "VM", "MBA", "CF", "MB2", "D3", "VMD", "TM", "AA", "F0",
+               "FN", "VI", "VV", "T1", "T2", "YP", "YQ", "YR"):
         tile(_n + str(_h), "float32", CH)
-    for _n in ("TI", "GI", "A2", "TF", "XN", "E2I", "BI", "BIT"):
+    for _n in ("TI", "GI", "A2"):
         tile(_n + str(_h), "int32", CH)
-    for _n in ("RED", "DC", "WM", "LL", "TT", "OFF"):
-        tile(_n + str(_h), "float32", 8)
+    tile("RED" + str(_h), "float32", 8)
     for _n in ("L2", "CU"):
         tile(_n + str(_h), "uint16", CH)
-    for _n in ("LC", "GL", "SL"):
-        tile(_n + str(_h), "uint16", 16)
+    tile("LC" + str(_h), "uint16", 16)
     for _t in range(NV):
         tile("LU%d%d" % (_h, _t), "uint16", CH)
         tile("W%d%d" % (_h, _t), "float32", CH)
@@ -53,8 +63,9 @@ SCRATCH = {"X": ("sbuf", [128, XW], "bfloat16"), "Y": ("sbuf", [128, XW], "bfloa
 for _d in POOLS:
     SCRATCH[POOLS[_d][0]] = ("sbuf", [128, SIZE[_d]], _d)
 for _h in range(2):
-    for _n in ("x1", "x2", "z", "xc", "mx"):
+    for _n in ("x1", "x2", "z", "xc"):
         SCRATCH[_n + str(_h)] = ("sbuf", [128, 16 * CH], "bfloat16")
+    SCRATCH["ax" + str(_h)] = ("sbuf", [128, 16, CH], "bfloat16")
     SCRATCH["P0_" + str(_h)] = ("psum", [128, 512], "float32")
     for _b in (1, 2, 3):
         SCRATCH["P%d_%d" % (_b, _h)] = ("psum", [128, 4, CH], "float32")
@@ -68,24 +79,21 @@ def rank_program(g, core, T, topo):
     if rank is None:
         return
     nxt, prv = T.cores[(rank + 1) % N], T.cores[(rank - 1) % N]
-    QUEUE = {"V": g.vector, "S": g.scalar, "T": g.tensor, "G": g, "Y": g.sync, "SD": g.scalar, "GD": g}
+    QUEUE = {"V": g.vector, "S": g.scalar, "T": g.tensor, "G": g, "Y": g.sync, "SD": g.scalar}
 
     def t(name, a=0, b=None, s=None):
-        if name in TILES:
-            pool, off, cols = TILES[name]
-            b = cols if b is None else b
-            return T[pool][:, off + a:off + b:s] if s else T[pool][:, off + a:off + b]
-        return T[name][:] if b is None and a == 0 else T[name][:, a:b]
+        pool, off, cols = TILES[name]
+        b = cols if b is None else b
+        return T[pool][:, off + a:off + b:s] if s else T[pool][:, off + a:off + b]
 
     ops = []
-    last_w, readers, bank_acc = {}, {}, {}
-    dcount = [0]
+    last_w, readers, banks = {}, {}, {}
+    dcount, now = [0], [0.0]
 
-    def add(eng, fn, rd, wr, cost, sem=None, need=1, extra=()):
+    def add(eng, fn, rd, wr, cost, sem=None, need=1, extra=(), comp=True):
         k = len(ops)
         deps = {}
-        phys = {"SD": "S", "GD": "G"}.get(eng, eng)
-        comp = eng in ("V", "S", "T", "G")
+        phys = {"SD": "S"}.get(eng, eng)
 
         def dep(o, kind):
             if o == k:
@@ -102,9 +110,9 @@ def rank_program(g, core, T, topo):
                 dep(last_w[x], "waw")
             for o in readers.get(x, ()):
                 dep(o, "war")
-        for x in set(rd) | set(wr):
+        for x in sorted(set(rd) | set(wr)):
             if x[0] == "P" and x[2:3] == "_":
-                ep = bank_acc.setdefault(x[:4], [phys, [], []])
+                ep = banks.setdefault(x[:4], [phys, [], []])
                 if ep[0] != phys:
                     ep[0], ep[1], ep[2] = phys, [], ep[1]
                 for o in ep[2]:
@@ -113,7 +121,7 @@ def rank_program(g, core, T, topo):
                     ep[1].append(k)
         for o in extra:
             deps.setdefault(o, "order")
-        ops.append(dict(eng=eng, phys=phys, comp=comp, fn=fn, deps=deps, cost=cost, sem=sem, need=need))
+        ops.append(dict(eng=eng, phys=phys, comp=comp, fn=fn, deps=deps, cost=cost, sem=sem, need=need, rd=rd, wr=wr, bonus=now[0]))
         for x in rd:
             readers.setdefault(x, []).append(k)
         for x in wr:
@@ -122,13 +130,13 @@ def rank_program(g, core, T, topo):
         return k
 
     def V(fn, rd, wr, n, c=0.83):
-        return add("V", lambda: fn(g.vector), rd, wr, 0.06 + n * c / 1000)
+        return add("V", lambda: fn(g.vector), rd, wr, 0.04 + max(n, 64) * c / 1000)
 
     def S(fn, rd, wr, n):
-        return add("S", lambda: fn(g.scalar), rd, wr, 0.07 + n * 0.83 / 1000)
+        return add("S", lambda: fn(g.scalar), rd, wr, 0.06 + max(n, 64) * 0.83 / 1000)
 
     def P(fn, rd, wr, n):
-        return add("T", lambda: fn(g.tensor), rd, wr, 0.06 + n * 0.45 / 1000)
+        return add("T", lambda: fn(g.tensor), rd, wr, 0.05 + n * 0.45 / 1000)
 
     def G(fn, rd, wr, n):
         return add("G", lambda: fn(g), rd, wr, 0.17 + n * 1.66 / 1000)
@@ -136,7 +144,7 @@ def rank_program(g, core, T, topo):
     def dma(eng, out, in_, rd, wr, lat):
         s = "d%d" % dcount[0]
         dcount[0] += 1
-        return add(eng, lambda: QUEUE[eng].dma_start(out, in_), rd, wr, lat, sem=s, need=16)
+        return add(eng, lambda: QUEUE[eng].dma_start(out, in_), rd, wr, lat, sem=s, need=16, comp=False)
 
     def ts(out, i0, s1, op0, s2=None, op1=None):
         if s2 is None:
@@ -152,79 +160,79 @@ def rank_program(g, core, T, topo):
     def act(out, a, func=AF.Identity, bias=0.0, scale=1.0):
         return lambda s: s.activation(out, a, func, bias=bias, scale=scale)
 
-    def mms(lst):
+    def mms(lst, start=True, stop=True):
         def f(pe):
             r = None
             for k, (o, l, x) in enumerate(lst):
-                r = pe.matmul(o, l, x, k == 0, k == len(lst) - 1)
+                r = pe.matmul(o, l, x, start and k == 0, stop and k == len(lst) - 1)
             return r
         return f
 
-    dma("Y", t("DI"), T.drugs[:], [], ["DI"], 2.5)
-    dma("SD", t("WI"), T.why[:], [], ["WI"], 2.5)
-    NP = 4
-    PW = D // NP
+    dma("Y", t("WI"), T.why[:], [], ["WI"], 2.5)
+    dma("SD", t("DI"), T.drugs[:], [], ["DI"], 2.5)
     for k in range(NP):
         dma("Y" if k % 2 == 0 else "SD", T.X[:, k * PW:(k + 1) * PW], T.eff[:, k * PW:(k + 1) * PW], [], ["Xr%d" % k], 4.0 + 1.2 * k)
     dma("Y", t("LIMI"), T.lim[:], [], ["LIMI"], 3)
     dma("Y", T.R[:, :D // 2], T.rem[:, :D // 2], [], ["Ra"], 11.0)
-    dma("SD", T.R[:, D // 2:], T.rem[:, D // 2:], [], ["Rb"], 11.0)
+    dma("Y", T.R[:, D // 2:], T.rem[:, D // 2:], [], ["Rb"], 11.0)
 
-    V(lambda v: v.memset(t("ONES"), 1.0), [], ["ONES"], 128)
+    LN2 = math.log(2.0)
+    V(lambda v: v.memset(t("ONES"), 1.0), [], ["ONES"], 64)
+    V(lambda v: v.memset(t("SELP"), 1.0), [], ["SELP"], 512)
     V(lambda v: v.memset(T.X[:, D:], 0.0), [], ["Xz"], 456)
-    G(lambda q: q.affine_select(t("IDENT"), t("ONES", 0, 128), [[-1, 128]], A.is_equal, 0.0, 0, 1), ["ONES"], ["IDENT"], 128)
-    G(lambda q: q.affine_select(t("BO"), t("ONES", 0, 128), [[-16, 8], [0, 16]], A.is_ge, 0.0, 0, 1), ["ONES"], ["BO"], 128)
-    G(lambda q: q.affine_select(t("BO"), t("BO"), [[16, 8], [0, 16]], A.is_ge, 0.0, 15, -1), ["BO"], ["BO"], 128)
     G(lambda q: q.iota(t("MI"), [[0, 1]], 0, 1), [], ["MI"], 1)
     V(ts(t("MI2"), t("MI"), 15, A.bitwise_and), ["MI"], ["MI2"], 64)
     V(cp(t("MCOL"), t("MI2")), ["MI2"], ["MCOL"], 64)
-    LN2 = math.log(2.0)
-    S(act(t("PC15"), t("MCOL"), AF.Exp, 0.0, -LN2), ["MCOL"], ["PC15"], 1500)
-    V(ts(t("PCI"), t("PC15"), 32768.0, A.mult), ["PC15"], ["PCI"], 64)
-    V(cp(t("PC15"), t("PCI")), ["PCI"], ["PC15"], 64)
-    S(act(t("PC2"), t("MCOL"), AF.Exp, 0.0, LN2), ["MCOL"], ["PC2"], 64)
+    G(lambda q: q.affine_select(t("IDENT"), t("ONES"), [[-1, 128]], A.is_equal, 0.0, 0, 1), ["ONES"], ["IDENT"], 128)
+    G(lambda q: q.affine_select(t("BO"), t("ONES"), [[-16, 8], [0, 16]], A.is_ge, 0.0, 0, 1), ["ONES"], ["BO"], 128)
+    G(lambda q: q.affine_select(t("BO"), t("BO"), [[16, 8], [0, 16]], A.is_ge, 0.0, 15, -1), ["BO"], ["BO"], 128)
+    G(lambda q: q.iota(t("QROW"), [[0, 8], [1, 16]], 0, 0, allow_small_or_imprecise_dtypes=True), [], ["QROW"], 128)
+    V(ts(t("DQ"), t("QROW"), t("MCOL"), A.is_equal), ["QROW", "MCOL"], ["DQ"], 128)
+    G(lambda q: q.affine_select(t("CONSTL"), t("ONES"), [[0, 128]], A.is_ge, 0.0, 1, -1), ["ONES"], ["CONSTL"], 128)
+    S(act(t("PC2"), t("MCOL"), AF.Exp, 0.0, LN2), ["MCOL"], ["PC2"], 1500)
     V(cp(t("PCI2"), t("PC2")), ["PC2"], ["PCI2"], 64)
     V(cp(t("PC2"), t("PCI2")), ["PCI2"], ["PC2"], 64)
-    V(ts(t("DQ"), t("ONES", 0, 128), 0.0, A.mult), ["ONES"], ["DQ"], 64)
-    for k in range(8):
-        G((lambda k: lambda q: q.affine_select(t("DQ"), t("DQ"), [[0, 8], [1, 16]], A.not_equal, 1.0, 16 * k, -1))(k), ["DQ"], ["DQ"], 128)
-    V(cp(t("DQF"), t("DQ")), ["DQ"], ["DQF"], 128)
-    V(cp(t("BOF"), t("BO")), ["BO"], ["BOF"], 128)
-    for j in range(16):
-        S(act(t("RJ", j * 128, j * 128 + 128), t("BOF"), AF.Copy, 0.0, t("DQF", j, j + 1)), ["BOF", "DQF"], ["RJ%d" % j], 128)
+    S(act(t("PC15"), t("MCOL"), AF.Exp, 0.0, -LN2), ["MCOL"], ["PC15"], 64)
+    V(ts(t("PCI"), t("PC15"), 32768.0, A.mult), ["PC15"], ["PCI"], 64)
+    V(cp(t("PC15"), t("PCI")), ["PCI"], ["PC15"], 64)
+    S(act(t("DQF"), t("DQ"), AF.Copy), ["DQ"], ["DQF"], 128)
+    S(act(t("BOF"), t("BO"), AF.Copy), ["BO"], ["BOF"], 128)
+    V(ts(t("MB1"), t("MCOL"), -BIG, A.mult, -BIG, A.add), ["MCOL"], ["MB1"], 64)
+    V(ts(t("PB1"), t("MCOL"), BIG, A.mult, BIG, A.add), ["MCOL"], ["PB1"], 64)
+    G(lambda q: q.iota(t("JB"), [[int(BIG) // 8, 16]], 0, 0, allow_small_or_imprecise_dtypes=True), [], ["JB"], 16)
+    V(ts(t("JB"), t("JB"), 8.0, A.mult, t("PB1"), A.subtract), ["JB", "PB1"], ["JB"], 64)
+    V(ts(t("JB"), t("JB"), BIG - 0.5, A.add, KK, A.mult), ["JB"], ["JB"], 64)
+
     for h in range(2):
         H = str(h)
-        cs = slice(h * CH, h * CH + CH)
         DI = t("DI", h * CH, h * CH + CH)
         WI = t("WI", h * CH, h * CH + CH)
-        V(cp(t("LU%d0" % h), DI), ["DI"], ["LU%d0" % h], 128)
-        V(ts(t("F0" + H), DI, 3456.0, A.is_lt), ["DI"], ["F0" + H], 128)
-        V(cp(t("WF" + H), WI), ["WI"], ["WF" + H], 128)
         V(ts(t("FN" + H), WI, t("MCOL"), A.not_equal), ["WI", "MCOL"], ["FN" + H], 128)
-        V(tt(t("FN" + H), t("FN" + H), t("F0" + H), A.mult), ["FN" + H, "F0" + H], ["FN" + H], 256)
-        S(act(t("E2" + H), t("WF" + H), AF.Exp, 0.0, LN2), ["WF" + H], ["E2" + H], 128)
-        V(cp(t("E2I" + H), t("E2" + H)), ["E2" + H], ["E2I" + H], 128)
-        V(tt(t("BF" + H), t("E2I" + H), t("FN" + H), A.mult), ["E2I" + H, "FN" + H], ["BF" + H], 256)
-        V(cp(t("BI" + H), t("BF" + H)), ["BF" + H], ["BI" + H], 128)
-    for j in range(16):
+        V(ts(t("VI" + H), WI, 1.0, A.add, BIG, A.mult), ["WI"], ["VI" + H], 128)
+        V(tt(t("VI" + H), t("VI" + H), t("FN" + H), A.mult), ["VI" + H, "FN" + H], ["VI" + H], 256)
+        V(ts(t("VV" + H), t("VI" + H), t("MB1"), A.add, t("PC2"), A.add), ["VI" + H, "MB1", "PC2"], ["VV" + H], 128)
+        V(cp(t("LU%d0" % h), DI), ["DI"], ["LU%d0" % h], 128)
+        V(ts(t("T2" + H), WI, 1 / 64, A.mult), ["WI"], ["T2" + H], 128)
+    for j in range(15, -1, -1):
+        RJ = "RJ%d" % j
+        rj = t("RJ", j * 128, j * 128 + 128)
+        S(act(rj, t("BOF"), AF.Copy, 0.0, t("DQF", j, j + 1)), ["BOF", "DQF"], [RJ], 128)
+        G((lambda rj: lambda q: q.affine_select(rj, rj, [[1, 128]], A.not_equal, 1.0, 0, -1))(rj), [RJ], [RJ], 128)
         for h in range(2):
             H = str(h)
-            bk = "P1_" + H
-            V(ts(t("BIT" + H), t("BI" + H), j, A.logical_shift_right, 1, A.bitwise_and), ["BI" + H], ["BIT" + H], 128)
-            P(mms([(T[bk][:, 0, :], t("RJ", j * 128, j * 128 + 128), t("BF" + H))]), ["RJ%d" % j, "BF" + H], [bk + "0"], 512)
-            V(tt(T[bk][:, 1, :], T[bk][:, 0, :], t("BIT" + H), A.mult), [bk + "0", "BIT" + H], [bk + "1"], 128)
-            V(tt(t("BI" + H), t("BF" + H), T[bk][:, 1, :], A.add), ["BF" + H, bk + "1"], ["BI" + H], 128)
-            V(tt(t("BF" + H), t("BF" + H), T[bk][:, 1, :], A.add), ["BF" + H, bk + "1"], ["BF" + H], 128)
+            o, key = T["P1_" + H][:, 0, :], "P1_%s0" % H
+            S(act(t("SG" + H), t("VV" + H), AF.Relu, t("JB", j, j + 1), -KK), ["VV" + H, "JB"], ["SG" + H], 128)
+            P(mms([(o, rj, t("VV" + H))], True, False), [RJ, "VV" + H], [key], 512)
+            P(mms([(o, t("IDENT"), t("SG" + H))], False, True), ["IDENT", "SG" + H], [key], 128)
+            V(tt(t("VV" + H), t("VV" + H), o, A.min), ["VV" + H, key], ["VV" + H], 128)
     for h in range(2):
         H = str(h)
-        V(ts(t("T1" + H), t("F0" + H), t("PC2"), A.mult), ["F0" + H, "PC2"], ["T1" + H], 128)
-        V(ts(t("T2" + H), t("WF" + H), 1 / 64, A.mult), ["WF" + H], ["T2" + H], 128)
-        V(tt(t("T2" + H), t("T1" + H), t("T2" + H), A.add), ["T1" + H, "T2" + H], ["T2" + H], 256)
-        V(tt(t("W%d0" % h), t("BF" + H), t("T2" + H), A.add), ["BF" + H, "T2" + H], ["W%d0" % h], 256)
+        S(act(t("T1" + H), t("VV" + H), AF.Identity, t("PB1"), 1.0), ["VV" + H, "PB1"], ["T1" + H], 128)
+        V(tt(t("W%d0" % h), t("T1" + H), t("T2" + H), A.add), ["T1" + H, "T2" + H], ["W%d0" % h], 256)
+
     V(ts(t("E16"), t("BO", 0, 128, 16), 16.0, A.mult), ["BO"], ["E16"], 64)
-    V(ts(t("E16N"), t("BO", 0, 128, 16), -32.0, A.mult), ["BO"], ["E16N"], 64)
+    V(ts(t("E16N"), t("BO", 0, 128, 16), -16.0, A.mult), ["BO"], ["E16N"], 64)
     V(cp(t("SELC"), t("BO", 0, 128, 16)), ["BO"], ["SELC"], 64)
-    G(lambda q: q.affine_select(t("CONSTL"), t("ONES", 0, 128), [[0, 128]], A.is_ge, 0.0, 1, -1), ["ONES"], ["CONSTL"], 128)
     G(lambda q: q.iota(t("KC"), [[0, 8], [-1, 16]], 15, 0, allow_small_or_imprecise_dtypes=True), [], ["KC"], 128)
     G(lambda q: q.affine_select(t("KS"), t("KC"), [[0, 128]], A.is_ge, 131072.0, 0, -1), ["KC"], ["KS"], 128)
     G(lambda q: q.affine_select(t("KC"), t("KC"), [[0, 128]], A.is_ge, 0.0, 0, -1), ["KC"], ["KC"], 128)
@@ -235,24 +243,23 @@ def rank_program(g, core, T, topo):
     V(ts(t("THR"), t("MCOL"), 0.5, A.subtract, EPS / 2, A.max), ["MCOL"], ["THR"], 64)
     V(ts(t("THR2"), t("MCOL"), 0.46875 * (1 - EPS), A.mult, 0.46875 * (15 * EPS - 32), A.add), ["MCOL"], ["THR2"], 64)
     V(tt(t("THR"), t("THR"), t("THR2"), A.add), ["THR", "THR2"], ["THR"], 64)
-    V(ts(t("P15"), t("BO"), t("PC15"), A.mult), ["BO", "PC15"], ["P15"], 64)
-    V(ts(t("P2"), t("BO"), t("PC2"), A.mult), ["BO", "PC2"], ["P2"], 64)
     V(ts(t("M64C"), t("MCOL"), 1 / 64, A.mult), ["MCOL"], ["M64C"], 64)
-    V(ts(t("M64"), t("BO"), t("M64C"), A.mult), ["BO", "M64C"], ["M64"], 64)
-    V(ts(t("NBO"), t("BO"), -1.0, A.mult), ["BO"], ["NBO"], 64)
-    V(ts(t("BO4K"), t("BO"), 4096.0, A.mult), ["BO"], ["BO4K"], 64)
-    V(ts(t("I8K"), t("IDENT"), 8192.0, A.mult), ["IDENT"], ["I8K"], 64)
-    V(ts(t("INEG"), t("IDENT"), -131072.0, A.mult), ["IDENT"], ["INEG"], 64)
+    for nm, src, sc in (("P15", "BO", "PC15"), ("P2", "BO", "PC2"), ("M64", "BO", "M64C"), ("NBO", "BO", -1.0), ("BO4K", "BO", 4096.0),
+                        ("I8N", "IDENT", -8192.0), ("IBIG", "IDENT", BIG), ("NID", "IDENT", -1.0), ("IDF", "IDENT", 1.0)):
+        S(act(t(nm), t(src), AF.Copy, 0.0, t(sc) if sc in TILES else sc), [src] + ([sc] if sc in TILES else []), [nm], 128)
+    for k, nm in enumerate(("ZA", "ZB")):
+        G((lambda k, nm: lambda q: q.affine_select(t(nm), t("BO"), [[0, 8], [1, 16]], A.is_equal, 0.0, -k, 0))(k, nm), ["BO"], [nm], 128)
     V(lambda v: v.memset(t("ONE16"), 1 / 16), [], ["ONE16"], 64)
+    V(lambda v: v.memset(t("KM"), -BIG / 2), [], ["KM"], 64)
+    V(lambda v: v.memset(t("K8"), 4096.0), [], ["K8"], 64)
     V(ts(t("B135"), t("MCOL"), -1.0, A.mult, 135.0, A.add), ["MCOL"], ["B135"], 64)
     V(lambda v: v.memset(t("MASK"), 1.0), [], ["MASK"], 128)
     V(lambda v: v.memset(t("MASK", 0, 128, 16), 0.0), [], ["MASK"], 64)
-    V(cp(t("IDF"), t("IDENT")), ["IDENT"], ["IDF"], 128)
-    V(ts(t("BIGM"), t("ONES", 0, 128), 65536.0, A.mult), ["ONES"], ["BIGM"], 64)
+    V(lambda v: v.memset(t("BIGM"), 65536.0), [], ["BIGM"], 64)
     G(lambda q: q.affine_select(t("BIGM"), t("BIGM"), [[1, 128]], A.is_ge, 0.0, 0, -1), ["BIGM"], ["BIGM"], 128)
-    for w in range(8):
-        V(ts(t("SELP", w * 128, w * 128 + 128), t("ONES", 0, 128), t("SELC", w, w + 1), A.mult), ["ONES", "SELC"], ["SELP%d" % w], 64)
-        V(ts(t("SELN", w * 128, w * 128 + 128), t("ONES", 0, 128), t("SELC", w, w + 1), A.mult, -1.0, A.mult), ["ONES", "SELC"], ["SELN%d" % w], 64)
+    G(lambda q: q.affine_select(t("SELP"), t("SELP"), [[-16, 8], [0, 128]], A.is_ge, 0.0, 0, 1), ["SELP"], ["SELP"], 1024)
+    G(lambda q: q.affine_select(t("SELP"), t("SELP"), [[16, 8], [0, 128]], A.is_ge, 0.0, 15, -1), ["SELP"], ["SELP"], 1024)
+    S(act(t("SELN"), t("SELP"), AF.Copy, 0.0, -1.0), ["SELP"], ["SELN"], 1024)
     G(lambda q: q.iota(t("DUM"), [[16, 16]], PAD + 1, 0, allow_small_or_imprecise_dtypes=True), [], ["DUM"], 16)
     V(ts(t("DUM"), t("DUM"), t("MCOL"), A.add), ["DUM", "MCOL"], ["DUM"], 64)
     for k in range(NP):
@@ -262,46 +269,52 @@ def rank_program(g, core, T, topo):
     V(ts(t("THETA"), t("LIMF"), 120.0, A.subtract), ["LIMF"], ["THETA"], 64)
     XK = ["Xr%d" % k for k in range(NP)] + ["Xz"]
     XALL = T.X[:]
-    arrive = {}
 
-    def gather(dst, lst, lkey, h):
+    def gather(dst, lst, h, plan):
         w = []
-        for (e, a, b) in (("S", 0, SPL), ("V", SPL, CH)):
+        for (e, a, b) in plan:
             if a < b:
-                key = "%s%d:%s" % (dst, h, e)
+                key = "%s%d:%d" % (dst, h, a)
                 o, s = T[dst + str(h)][:, 16 * a:16 * b], XALL.indirect(t(lst, a, b))
                 if e == "S":
-                    S(act(o, s, AF.Copy), XK + [lkey], [key], 16 * (b - a) * 1.5)
+                    S(act(o, s, AF.Copy), XK + [lst], [key], 16 * (b - a) * 1.5)
                 else:
-                    V(cp(o, s), XK + [lkey], [key], 16 * (b - a) * 1.5)
+                    V(cp(o, s), XK + [lst], [key], 16 * (b - a) * 1.5)
                 w.append(key)
         return w
 
-    def argmax(h, srckeys):
+    def sums(h, slot, x, f, plan, kx):
         H = str(h)
-        p0 = T["P0_" + H]
-        V(lambda v: v.tensor_tensor_scan(t("SCA" + H), t("MASK"), p0[:, 0:128], 0.0, A.mult, A.max), srckeys + ["MASK"], ["SCA" + H], 128)
+        for (e, a, b), key in zip(plan, kx):
+            o = T["P3_" + H][:, slot, a:b]
+            P(mms([(o, t("IDENT"), x[:, 16 * a + m:16 * b:16]) for m in range(16)] + [(o, t("NBO"), t(f, a, b))]),
+              ["IDENT", "NBO", f, key], ["P3_%s%d" % (H, slot)] if a == 0 else ["P3_%s%d+%d" % (H, slot, a)], 17 * max(64, b - a))
+        return ["P3_%s%d" % (H, slot)] + ["P3_%s%d+%d" % (H, slot, a) for e, a, b in plan if a]
+
+    def argmax(h):
+        H = str(h)
+        src, p0 = "P0_" + H, T["P0_" + H]
+        V(lambda v: v.tensor_tensor_scan(t("SCA" + H), t("MASK"), p0[:, 0:128], 0.0, A.mult, A.max), [src, "MASK"], ["SCA" + H], 128)
         V(lambda v: v.tensor_tensor_scan(t("SC" + H)[:, ::-1], t("MASK"), t("SCA" + H)[:, ::-1], 0.0, A.mult, A.max), ["SCA" + H, "MASK"], ["SC" + H], 128)
-        V(tt(t("OHD" + H), p0[:, 0:128], t("SC" + H), A.is_equal), srckeys + ["SC" + H], ["OHD" + H], 128)
+        V(tt(t("OHD" + H), p0[:, 0:128], t("SC" + H), A.is_equal), [src, "SC" + H], ["OHD" + H], 128)
 
     def phase1(vt, h):
         H = str(h)
         LU, W = "LU%d%d" % (h, vt), "W%d%d" % (h, vt)
-        p0, p1, p2, p3 = T["P0_" + H], T["P1_" + H], T["P2_" + H], T["P3_" + H]
+        p0, p1, p3 = T["P0_" + H], T["P1_" + H], T["P3_" + H]
         x = T["x1" + H]
-        kx = gather("x1", LU, LU, h)
+        kx = gather("x1", LU, h, SHARE[("a" if vt else "f") + H])
         V(ts(t("D1" + H), t(LU), 1.0, A.add), [LU], ["D1" + H], 128)
         V(ts(t("F1" + H), t("D1" + H), 3457.0, A.is_lt, 0.46875, A.add), ["D1" + H], ["F1" + H], 128)
         S(act(t("DHI" + H), t("D1" + H), AF.Copy), ["D1" + H], ["DHI" + H], 128)
         V(tt(t("DLO" + H), t("D1" + H), t("DHI" + H), A.subtract), ["D1" + H, "DHI" + H], ["DLO" + H], 256)
         P(mms([(p1[:, 3, :], t("BO"), t("F1" + H))]), ["BO", "F1" + H], ["P1_%s3" % H], 128)
-        V(ts(t("FULL" + H), p1[:, 3, :], 23.0, A.is_ge), ["P1_%s3" % H], ["FULL" + H], 128)
+        S(act(t("FULL" + H), p1[:, 3, :], AF.Relu, -22.5), ["P1_%s3" % H], ["FULL" + H], 128)
         P(mms([(p0[:, 0:128], t("CONSTL"), t("KC"))] + [(p0[:, m:128:16], x[:, m::16], t("E16")) for m in range(16)]),
           ["CONSTL", "KC", "E16"] + kx, ["P0_" + H], 128 + 16 * 64)
-        argmax(h, ["P0_" + H])
-        P(mms([(p3[:, 0, :], t("IDENT"), x[:, m::16]) for m in range(16)] + [(p3[:, 0, :], t("NBO"), t("F1" + H))]),
-          ["IDENT", "NBO", "F1" + H] + kx, ["P3_%s0" % H], 17 * 128)
-        S(act(t("T32" + H), p3[:, 0, :], AF.Copy), ["P3_%s0" % H], ["T32" + H], 128)
+        argmax(h)
+        kt = sums(h, 0, x, "F1" + H, SHARE[("a" if vt else "f") + H], kx)
+        S(act(t("T32" + H), p3[:, 0, :], AF.Copy), kt, ["T32" + H], 128)
         P(mms([(p3[:, 1, :], t("BOF"), t("T32" + H)), (p3[:, 1, :], t("BO4K"), t("FULL" + H))]),
           ["BOF", "T32" + H, "BO4K", "FULL" + H], ["P3_%s1" % H], 640)
         V(ts(t("ST" + H), p3[:, 1, :], t("THETA"), A.is_ge), ["P3_%s1" % H, "THETA"], ["ST" + H], 128)
@@ -315,31 +328,29 @@ def rank_program(g, core, T, topo):
 
     def phase2(vt, h):
         H = str(h)
-        LU, W = "LU%d%d" % (h, vt), "W%d%d" % (h, vt)
-        p0, p1, p2, p3 = T["P0_" + H], T["P1_" + H], T["P2_" + H], T["P3_" + H]
+        W = "W%d%d" % (h, vt)
+        p0, p1, p3 = T["P0_" + H], T["P1_" + H], T["P3_" + H]
         x = T["x2" + H]
-        kx = gather("x2", "L2" + H, "L2" + H, h)
+        kx = gather("x2", "L2" + H, h, SHARE["x2"])
         V(ts(t("F2" + H), t("D2" + H), 3457.0, A.is_lt, 0.46875, A.add), ["D2" + H], ["F2" + H], 128)
-        V(ts(t("KP" + H), t("D2" + H), 3457.0, A.is_lt), ["D2" + H], ["KP" + H], 128)
         P(mms([(p1[:, 2, :], t("LT"), t("F2" + H))]), ["LT", "F2" + H], ["P1_%s2" % H], 128)
+        P(mms([(p1[:, 3, :], t("IDF"), t(W)), (p1[:, 3, :], t("IBIG"), t("F2" + H))]), ["IDF", W, "IBIG", "F2" + H], ["P1_%s3" % H], 640)
         V(ts(t("OHE" + H), p1[:, 2, :], t("THR"), A.is_ge), ["P1_%s2" % H, "THR"], ["OHE" + H], 128)
-        V(ts(t("NOE" + H), p1[:, 2, :], t("THR"), A.is_lt), ["P1_%s2" % H, "THR"], ["NOE" + H], 128)
-        V(tt(t("W2" + H), t(W), t("KP" + H), A.mult), [W, "KP" + H], ["W2" + H], 256)
+        S(act(t("W2" + H), p1[:, 3, :], AF.Relu, -1.46875 * BIG), ["P1_%s3" % H], ["W2" + H], 128)
         V(cp(t("A2" + H), t("W2" + H)), ["W2" + H], ["A2" + H], 128)
-        P(mms([(p3[:, 2, :], t("IDENT"), x[:, m::16]) for m in range(16)] + [(p3[:, 2, :], t("NBO"), t("F2" + H))]),
-          ["IDENT", "NBO", "F2" + H] + kx, ["P3_%s2" % H], 17 * 128)
-        S(act(t("U32" + H), p3[:, 2, :], AF.Identity, t("B135"), 16.0), ["P3_%s2" % H, "B135"], ["U32" + H], 128)
-        S(act(t("Y" + H), p3[:, 2, :], AF.Identity, MAGIC, 1 / 16), ["P3_%s2" % H], ["Y" + H], 128)
+        ku = sums(h, 2, x, "F2" + H, SHARE["x2"], kx)
+        S(act(t("U32" + H), p3[:, 2, :], AF.Identity, t("B135"), 16.0), ku + ["B135"], ["U32" + H], 128)
+        S(act(t("Y" + H), p3[:, 2, :], AF.Identity, MAGIC, 1 / 16), ku, ["Y" + H], 128)
         P(mms([(p0[:, 0:128], t("U32" + H), t("IDF"))]), ["U32" + H, "IDF"], ["P0_" + H], 512)
-        S(act(p3[:, 1, :], t("Y" + H), AF.Identity, MAGIC + 256, -1.0), ["Y" + H], ["P3_%s1" % H], 128)
-        argmax(h, ["P0_" + H])
+        S(act(t("VB" + H), t("Y" + H), AF.Identity, MAGIC + 256, -1.0), ["Y" + H], ["VB" + H], 128)
+        argmax(h)
         P(mms([(p3[:, 3, :], t("OHD" + H), t("IDENT"))]), ["OHD" + H, "IDENT"], ["P3_%s3" % H], 128)
 
     def phase3(vt, h):
         H = str(h)
-        p0, p1, p2, p3 = T["P0_" + H], T["P1_" + H], T["P2_" + H], T["P3_" + H]
+        p0, p1, p3 = T["P0_" + H], T["P1_" + H], T["P3_" + H]
         x, z = T["x2" + H], T["z" + H]
-        kx = ["x2%d:S" % h] + (["x2%d:V" % h] if SPL < CH else [])
+        kx = ["x2%d:%d" % (h, a) for e, a, b in SHARE["x2"]]
         for q in range(2):
             ms = range(8 * q, 8 * q + 8)
 
@@ -356,7 +367,7 @@ def rank_program(g, core, T, topo):
                     r = pe.matmul(p0[:, m:128:16], z[:, m::16], t("E16"), False, m == 15)
                 return r
             P(yf, ["CONSTL", "KC", "E16", "z%s:%d" % (H, q)], ["P0_" + H], 128 * (1 - q) + 8 * 64)
-        argmax(h, ["P0_" + H])
+        argmax(h)
         P(mms([(p1[:, 0, :], t("OHD" + H), t("IDENT"))]), ["OHD" + H, "IDENT"], ["P1_%s0" % H], 128)
         V(tt(t("MBK" + H), p1[:, 0, :], t("D2" + H), A.mult), ["P1_%s0" % H, "D2" + H], ["MBK" + H], 128)
         V(tt(t("MBA" + H), p1[:, 0, :], t("A2" + H), A.mult), ["P1_%s0" % H, "A2" + H], ["MBA" + H], 128)
@@ -369,49 +380,41 @@ def rank_program(g, core, T, topo):
 
     def phase4(vt, h):
         H = str(h)
-        p0, p1, p2, p3 = T["P0_" + H], T["P1_" + H], T["P2_" + H], T["P3_" + H]
-        xc, mx = T["xc" + H], T["mx" + H]
-        hs = CH // 2
-        for q in range(2):
-            S(act(xc[:, 16 * hs * q:16 * hs * (q + 1)], XALL.indirect(t("CU" + H, hs * q, hs * q + hs)), AF.Copy),
-              XK + ["CU" + H], ["xc%s:%d" % (H, q)], 16 * hs * 1.5)
+        p0, p1, p3 = T["P0_" + H], T["P1_" + H], T["P3_" + H]
+        xc, ax = T["xc" + H], T["ax" + H]
+        kx = gather("xc", "CU" + H, h, SHARE["xc"])
         V(ts(t("CF" + H), t("CU" + H), 1.0, A.add), ["CU" + H], ["CF" + H], 128)
         P(mms([(p1[:, 2, :], t("BOF"), t("MBA" + H)), (p1[:, 2, :], t("M64"), t("OHK" + H)), (p1[:, 2, :], t("P2"), t("OHE" + H)),
-               (p1[:, 2, :], t("INEG"), t("NOE" + H))]),
-          ["BOF", "MBA" + H, "M64", "OHK" + H, "P2", "OHE" + H, "INEG", "NOE" + H], ["P1_%s2" % H], 900)
+               (p1[:, 2, :], t("IBIG"), t("OHE" + H)), (p1[:, 2, :], t("CONSTL"), t("KM"))]),
+          ["BOF", "MBA" + H, "M64", "OHK" + H, "P2", "OHE" + H, "IBIG", "CONSTL", "KM"], ["P1_%s2" % H], 1024)
         last = vt == NV - 1
         WN = ("SW%d%d" % (h, vt + 1)) if not last else "W2" + H
         V(tt(t(WN), t("W2" + H), p1[:, 2, :], A.max), ["W2" + H, "P1_%s2" % H], [WN], 128)
         if not last:
             send(WN, "W%d%d" % (h, vt + 1), 6 * h + 2 * vt)
-        for q in range(2):
-            for b in range(2 if q else 1):
-                js = range(8 * b, 8 * b + 8) if q else range(16)
+        P(mms([(p0[:, 0:128], t("CONSTL"), t("KS"))], True, False), ["CONSTL", "KS"], ["P0_" + H], 128)
+        for b in range(4):
+            pb, kb = (p3, "P3_%s" % H) if b % 2 == 0 else (p1, "P1_%s" % H)
 
-                def mf(v, q=q, js=js):
-                    for j in js:
-                        lo, hi = 16 * hs * q + j, 16 * hs * (q + 1)
-                        r = v.tensor_tensor(mx[:, lo:hi:16], xc[:, lo:hi:16], p3[:, 1, hs * q:hs * q + hs], A.max)
-                    return r
-                V(mf, ["xc%s:%d" % (H, q), "P3_%s1" % H], ["mx%s:%d%d" % (H, q, b)], 64 * len(js))
-
-        def sf0(pe):
-            r = pe.matmul(p0[:, 0:128], t("CONSTL"), t("KS"), True, False)
-            for j in range(16):
-                r = pe.matmul(p0[:, j:128:16], xc[:, j::16], t("E16"), False, False)
-            return r
-        P(sf0, ["CONSTL", "KS", "E16", "xc%s:0" % H, "xc%s:1" % H], ["P0_" + H], 128 + 1024)
-        for b in range(2):
-            def sf(pe, b=b):
-                for j in range(8 * b, 8 * b + 8):
-                    r = pe.matmul(p0[:, j:128:16], mx[:, j::16], t("E16N"), False, j == 15)
+            def df(pe, b=b, pb=pb):
+                for u in range(4):
+                    pe.matmul(pb[:, u, :], t("IDENT"), xc[:, 4 * b + u::16], True, False)
+                    r = pe.matmul(pb[:, u, :], t("NID"), t("VB" + H), False, True)
                 return r
-            P(sf, ["E16N", "mx%s:00" % H, "mx%s:1%d" % (H, b)], ["P0_" + H], 512)
-        argmax(h, ["P0_" + H])
+            P(df, ["IDENT", "NID", "VB" + H] + kx, [kb + str(u) for u in range(4)], 1024)
+            S(act(ax[:, 4 * b:4 * b + 4, :], pb[:, :, :], AF.Abs), [kb + str(u) for u in range(4)], ["ax%s:%d" % (H, b)], 512)
+
+            def sf(pe, b=b):
+                for j in range(4 * b, 4 * b + 4):
+                    r = pe.matmul(p0[:, j:128:16], ax[:, j, :], t("E16N"), False, j == 15)
+                return r
+            P(sf, ["E16N", "ax%s:%d" % (H, b)], ["P0_" + H], 256)
+        argmax(h)
         P(mms([(p1[:, 0, :], t("OHD" + H), t("IDENT"))]), ["OHD" + H, "IDENT"], ["P1_%s0" % H], 128)
         V(tt(t("MB2" + H), p1[:, 0, :], t("CF" + H), A.mult), ["P1_%s0" % H, "CF" + H], ["MB2" + H], 128)
-        P(mms([(p1[:, 1, :], t("BOF"), t("MB2" + H)), (p1[:, 1, :], t("I8K"), t("NOE" + H))]),
-          ["BOF", "MB2" + H, "I8K", "NOE" + H], ["P1_%s1" % H], 640)
+        P(mms([(p1[:, 1, :], t("I8N"), t("OHE" + H)), (p1[:, 1, :], t("CONSTL"), t("K8"))], True, False),
+          ["I8N", "OHE" + H, "CONSTL", "K8"], ["P1_%s1" % H], 256)
+        P(mms([(p1[:, 1, :], t("BOF"), t("MB2" + H))], False, True), ["BOF", "MB2" + H], ["P1_%s1" % H], 512)
         V(tt(t("D3" + H), t("D2" + H), p1[:, 1, :], A.min), ["D2" + H, "P1_%s1" % H], ["D3" + H], 128)
         if not last:
             LN = "SLU%d%d" % (h, vt + 1)
@@ -425,78 +428,79 @@ def rank_program(g, core, T, topo):
             V(ts(t("YR" + H), t("YQ" + H), 64.0, A.mult), ["YQ" + H], ["YR" + H], 128)
             dma("Y", T.yq[:, h * CH:h * CH + CH], t("YR" + H), ["YR" + H], [], 2.5)
 
-    locals_used = []
-
     def send(src, dst, k):
         mask, n = topo.mask(core, nxt), len(topo.engines(core, nxt))
         rid, pid = topo.addr(nxt)[:2]
-        o = add("G", lambda: g.remote_dma(t(dst), t(src), T.sem["r%d" % k], T.sem["l%d" % k], pid, rid, mask), [src], [], 1.0, sem="l%d" % k, need=n)
-        ops[o]["comp"] = False
-        ops[o]["remote"] = True
-        locals_used.append(o)
-        ni = len(topo.engines(prv, core))
-        a = add("N", None, [], [dst], 2.5, sem="r%d" % k, need=ni, extra=[o])
-        ops[a]["comp"] = False
+        o = add("G", lambda: g.remote_dma(t(dst), t(src), T.sem["r%d" % k], T.sem["l%d" % k], pid, rid, mask), [src], [], 1.0,
+                sem="l%d" % k, need=n, comp=False)
+        add("N", None, [], [dst], 2.5, sem="r%d" % k, need=len(topo.engines(prv, core)), extra=[o], comp=False)
 
     def dedup(vt, h):
         H = str(h)
         q2 = "P2_" + H
         p2 = T[q2]
-        V(tt(t("MBH" + H), t("OHS" + H), t("DHI" + H), A.mult), ["OHS" + H, "DHI" + H], ["MBH" + H], 256)
-        V(tt(t("MBL" + H), t("OHS" + H), t("DLO" + H), A.mult), ["OHS" + H, "DLO" + H], ["MBL" + H], 256)
-        P(mms([(p2[:, 0, :], t("MBH" + H), t("BO")), (p2[:, 0, :], t("MBL" + H), t("BO"))]), ["MBH" + H, "MBL" + H, "BO"], [q2 + "0"], 256)
+        P(mms([(p2[:, 3, :], t("IDENT"), t("OHS" + H))]), ["IDENT", "OHS" + H], [q2 + "3"], 128)
+        V(tt(t("MBH" + H), p2[:, 3, :], t("DHI" + H), A.mult), [q2 + "3", "DHI" + H], ["MBH" + H], 128)
+        V(tt(t("MBL" + H), p2[:, 3, :], t("DLO" + H), A.mult), [q2 + "3", "DLO" + H], ["MBL" + H], 128)
+        P(mms([(p2[:, 1, :], t("ZA"), t("MBH" + H)), (p2[:, 1, :], t("ZB"), t("MBL" + H))]), ["MBH" + H, "MBL" + H, "ZA", "ZB"], [q2 + "1"], 256)
+        S(act(t("Z" + H), p2[:, 1, :], AF.Copy), [q2 + "1"], ["Z" + H], 128)
+        P(mms([(p2[:, 0, :], t("Z" + H), t("BO"))]), ["Z" + H, "BO"], [q2 + "0"], 128)
         P(mms([(p2[:, 2, :], t("ONE16"), t("ST" + H))]), ["ONE16", "ST" + H], [q2 + "2"], 128)
         V(tt(t("VMD" + H), p2[:, 0, :], t("DQF"), A.mult), [q2 + "0", "DQF"], ["VMD" + H], 128)
         if vt < NV - 1:
             S(lambda s: s.activation(t("AA" + H), p2[:, 2, :], AF.Copy, accum_out=t("CNT", h, h + 1)), [q2 + "2"], ["AA" + H, "CNT" + H], 160)
         P(mms([(p2[:, 1, 0:8], t("VMD" + H), t("SELC"))]), ["VMD" + H, "SELC"], [q2 + "1"], 256)
-        V(cp(t("DC" + H), p2[:, 1, 0:8]), [q2 + "1"], ["DC" + H], 64)
-        V(ts(t("GL" + H, 0, 8), t("DC" + H), 1.0, A.subtract), ["DC" + H], ["GL" + H], 64)
+        V(cp(t("DC", 8 * h, 8 * h + 8), p2[:, 1, 0:8]), [q2 + "1"], ["DC" + H], 64)
         for w in range(8):
-            b = "P2_%d" % (w // 4)
+            b = q2
             o = T[b][:, w % 4, :]
-            P(mms([(o, t("SELP", w * 128, w * 128 + 128), t("MBH" + H)), (o, t("SELP", w * 128, w * 128 + 128), t("MBL" + H)),
-                   (o, t("MBH" + H), t("SELN", w * 128, w * 128 + 128)), (o, t("MBL" + H), t("SELN", w * 128, w * 128 + 128)),
-                   (o, t("IDENT"), t("BIGM"))]),
-              ["SELP%d" % w, "SELN%d" % w, "MBH" + H, "MBL" + H, "IDENT", "BIGM"], [b + str(w % 4)], 640)
+            sp, sn = t("SELP", w * 128, w * 128 + 128), t("SELN", w * 128, w * 128 + 128)
+            P(mms([(o, sp, t("Z" + H)), (o, t("Z" + H), sn), (o, t("IDENT"), t("BIGM"))]),
+              ["SELP", "SELN", "Z" + H, "IDENT", "BIGM"], [b + str(w % 4)], 384)
             if w % 4 == 3:
                 for u in range(w - 3, w + 1):
                     V((lambda u, b: lambda v: v.tensor_reduce(t("RED" + H, u, u + 1), T[b][:, u % 4, :], AxisListType.X, A.min,
                                                               apply_absolute_value=True))(u, b), [b + str(u % 4)], ["RED%s%d" % (H, u)], 128)
         for w in range(8):
             S(act(t("VMW" + H, 16 * w, 16 * w + 16), t("DQ", 0, 16), AF.Copy, 0.0, t("RED" + H, w, w + 1)), ["DQ", "RED%s%d" % (H, w)], ["VMW%s%d" % (H, w)], 16)
-        P(mms([(p2[:, 3, 0:8], t("VMW" + H), t("BO", 0, 128, 16))]), ["VMW%s%d" % (H, w) for w in range(8)] + ["BO"], [q2 + "3"], 64)
-        V(tt(t("WM" + H), p2[:, 3, 0:8], t("DC" + H), A.min), [q2 + "3", "DC" + H], ["WM" + H], 64)
-        V(ts(t("LL" + H), t("WM" + H), 0.5, A.is_lt), ["WM" + H], ["LL" + H], 64)
-        V(tt(t("TT" + H), t("LL" + H), t("DUM", 8 * h, 8 * h + 8), A.mult), ["LL" + H, "DUM"], ["TT" + H], 64)
-        V(tt(t("OFF" + H), t("TT" + H), t("DC" + H), A.max), ["TT" + H, "DC" + H], ["OFF" + H], 64)
-        V(ts(t("SL" + H, 0, 8), t("OFF" + H), 1.0, A.subtract), ["OFF" + H], ["SL" + H], 64)
-        V(ts(t("TF" + H), t("T32" + H), 1 / 16, A.mult), ["T32" + H], ["TF" + H], 128)
-        S(act(t("XS" + H), XALL.indirect(t("GL" + H, 0, 8)), AF.Copy), XK + ["GL" + H], ["XS" + H], 200)
-        V(tt(t("AA" + H), t("XS" + H), t("TF" + H), A.add), ["XS" + H, "TF" + H], ["AA" + H], 256)
-        V(ts(t("XN" + H), t("AA" + H), 0.5, A.mult, 0.25 if vt < NV - 1 else -0.75, A.add), ["AA" + H], ["XN" + H], 128)
+        S(act(t("TM" + H), t("T32" + H), AF.Identity, MAGIC, 1 / 16), ["T32" + H], ["TM" + H], 128)
+        S(act(t("TFB" + H), t("TM" + H), AF.Identity, -MAGIC, 1.0), ["TM" + H], ["TFB" + H], 128)
 
     def update(vt):
+        pa, pb = T.P2_0, T.P2_1
+        for h in range(2):
+            H = str(h)
+            P(mms([(pa[:, 3, 8 * h:8 * h + 8], t("VMW" + H), t("BO", 0, 128, 16))]), ["VMW%s%d" % (H, w) for w in range(8)] + ["BO"], ["P2_03%d" % h], 64)
+        V(ts(t("GL"), t("DC"), 1.0, A.subtract), ["DC0", "DC1"], ["GL"], 64)
+        S(act(t("XS"), XALL.indirect(t("GL")), AF.Copy), XK + ["GL"], ["XS"], 400)
+        for h in range(2):
+            H = str(h)
+            P(mms([(pb[:, h, :], t("IDENT"), t("XS", 128 * h, 128 * h + 128)), (pb[:, h, :], t("IDENT"), t("TFB" + H))]),
+              ["IDENT", "XS", "TFB" + H], ["P2_1%d" % h], 256)
+        V(ts(t("XN"), pb[:, 0:2, :], 0.5, A.mult, 0.25 if vt < NV - 1 else -0.75, A.add), ["P2_10", "P2_11"], ["XN"], 256)
+        V(tt(t("WM"), pa[:, 3, 0:16], t("DC"), A.min), ["P2_030", "P2_031", "DC0", "DC1"], ["WM"], 64)
+        V(ts(t("LL"), t("WM"), 0.5, A.is_lt), ["WM"], ["LL"], 64)
+        V(tt(t("TT"), t("LL"), t("DUM"), A.mult), ["LL", "DUM"], ["TT"], 64)
+        V(tt(t("OFF"), t("TT"), t("DC"), A.max), ["TT", "DC0", "DC1"], ["OFF"], 64)
+        V(ts(t("SL"), t("OFF"), 1.0, A.subtract), ["OFF"], ["SL"], 64)
         if vt < NV - 1:
             V(tt(t("CI"), t("CNT", 0, 1), t("CNT", 1, 2), A.add), ["CNT0", "CNT1"], ["CI"], 64)
             V(ts(t("CI2"), t("CI"), 255, A.bitwise_and), ["CI"], ["CI2"], 64)
             V(ts(t("THETA"), t("CI2"), t("LIMF"), A.add, 120.0, A.subtract), ["CI2", "LIMF"], ["THETA"], 64)
         dst, keys = (T.X[:], XK) if vt < NV - 1 else (T.Y[:], ["Y%d" % k for k in range(NP)] + ["Yz"])
         for h in (1, 0):
-            H = str(h)
-            V(cp(dst.indirect(t("SL" + H, 0, 8)), t("XN" + H)), ["SL" + H, "XN" + H], keys, 128 * 3)
+            V(cp(dst.indirect(t("SL", 8 * h, 8 * h + 8)), t("XN", 128 * h, 128 * h + 128)), ["SL", "XN"], keys, 128 * 3)
 
     for vt in range(NV):
         if vt == NV - 1:
             V(lambda v: v.memset(T.Y[:, D:], 0.0), [], ["Yz"], 456)
             for k in range(NP):
                 S(act(T.Y[:, k * PW:(k + 1) * PW], T.X[:, k * PW:(k + 1) * PW], AF.Identity, -1.0, 1.0), XK, ["Y%d" % k], PW)
-        for h in range(2):
-            phase1(vt, h)
-        for h in range(2):
-            phase2(vt, h)
-        for h in range(2):
-            phase3(vt, h)
+        for ph in (phase1, phase2, phase3):
+            for h in range(2):
+                now[0] = BONUS[2 * (phase1, phase2, phase3).index(ph) + h]
+                ph(vt, h)
+        now[0] = BONUS[8]
         if vt == NV - 1:
             for h in range(2):
                 dedup(vt, h)
@@ -504,14 +508,18 @@ def rank_program(g, core, T, topo):
             for k in range(NP):
                 dma("Y", T.yx[:, k * PW:(k + 1) * PW], T.Y[:, k * PW:(k + 1) * PW], ["Y%d" % k], [], 4.0)
         for h in range(2):
+            now[0] = BONUS[6 + h]
             phase4(vt, h)
+        now[0] = BONUS[8]
         if vt < NV - 1:
             for h in range(2):
                 dedup(vt, h)
             update(vt)
 
-    order = schedule(ops)
-    emit(g, T, ops, order, QUEUE)
+    emit(g, T, ops, schedule(ops), QUEUE)
+
+
+WAKE = 0.12
 
 
 def schedule(ops):
@@ -520,10 +528,11 @@ def schedule(ops):
     for k, o in enumerate(ops):
         for d in o["deps"]:
             succ[d].append(k)
-    WAKE = 0.12
     tail = [0.0] * n
     for k in range(n - 1, -1, -1):
         tail[k] = ops[k]["cost"] + max([tail[s] + WAKE for s in succ[k]] + [0.0])
+    for k in range(n):
+        tail[k] += ops[k]["bonus"]
     left = [len(o["deps"]) for o in ops]
     ready, fin, free = {}, [0.0] * n, {}
     for k in range(n):
@@ -554,9 +563,8 @@ def schedule(ops):
             if left[s] == 0:
                 r = max([fin[d] + (WAKE if ops[s]["deps"][d] == "wait" else 0.0) for d in ops[s]["deps"]])
                 ready.setdefault(ops[s]["phys"], []).append((r, s))
-    order_time = {k: fin[k] for k in order}
     ops[0]["makespan"] = max(fin)
-    ops[0]["fin"] = order_time
+    ops[0]["fin"] = {k: fin[k] for k in order}
     return order
 
 
@@ -567,25 +575,15 @@ def emit(g, T, ops, order, QUEUE):
         o = ops[k]
         e = o["phys"]
         if e == "N":
-            o["sig"] = (o["sem"], o["need"])
-            o["kn"] = {}
+            o["sig"], o["kn"] = (o["sem"], o["need"]), {}
             continue
-        q = QUEUE[o["eng"]]
-        kn = know[e]
-        waits = {}
-        for d in sorted(o["deps"], key=lambda d: -order.index(d) if len(order) < 50 else -d):
-            if o["deps"][d] != "wait":
-                continue
-            s, v = ops[d]["sig"]
-            if kn.get(s, 0) >= v:
-                continue
-            waits[s] = max(waits.get(s, 0), v)
-        src = {}
+        q, kn = QUEUE[o["eng"]], know[e]
+        waits, src = {}, {}
         for d in o["deps"]:
             if o["deps"][d] == "wait":
                 s, v = ops[d]["sig"]
-                if s in waits and waits[s] == v:
-                    src[s] = d
+                if kn.get(s, 0) < v and waits.get(s, 0) < v:
+                    waits[s], src[s] = v, d
         for s in list(waits):
             if any(s2 != s and ops[src[s2]]["kn"].get(s, 0) >= waits[s] for s2 in waits):
                 del waits[s]
@@ -600,11 +598,10 @@ def emit(g, T, ops, order, QUEUE):
             cnt[s] = cnt.get(s, 0) + 1
             ins.then_inc(T.sem[s], 1)
             o["sig"] = (s, cnt[s])
-        elif o.get("remote"):
-            o["sig"] = (o["sem"], o["need"])
         else:
-            ins.then_inc(T.sem[o["sem"]], 16)
-            o["sig"] = (o["sem"], 16)
+            o["sig"] = (o["sem"], o["need"])
+            if o["eng"] != "G":
+                ins.then_inc(T.sem[o["sem"]], 16)
         o["kn"] = dict(kn)
     for s in sorted(cnt):
         g.wait_ge(T.sem[s], cnt[s])

@@ -14,7 +14,8 @@ PW = D // NP
 HALF = (("S", 0, 64), ("V", 64, 128))
 SHARE = {"f0": (("S", 0, 32), ("V", 32, 64), ("S", 64, 96), ("V", 96, 128)), "f1": (("S", 0, 32), ("V", 32, 64), ("S", 64, 96), ("V", 96, 128)),
          "a0": HALF, "a1": HALF, "x2": HALF, "xc": HALF}
-BONUS = [3, 7, 6, 9, 7, 4, 2, 5, 5]
+PRI = {}
+BONUS = [-4, -2, -2, 13, 18, 1, 0, 2, 0, 6]
 
 POOLS = {"float32": ("pf", 4), "bfloat16": ("pb", 2), "int32": ("pi", 4), "uint16": ("pu", 2)}
 TILES, SIZE = {}, {"float32": 0, "bfloat16": 0, "int32": 0, "uint16": 0}
@@ -26,14 +27,14 @@ def tile(name, dtype, cols):
     SIZE[dtype] += -(-cols // per) * per
 
 
-for _n, _c in (("ONES", 128), ("IDENT", 128), ("BO", 128), ("E16", 8), ("E16N", 8), ("CONSTL", 128), ("KC", 128), ("KS", 128),
+for _n, _c in (("ONES", 128), ("IDENT", 128), ("BO", 128), ("E16", 8), ("E16N", 8), ("E32N", 8), ("CONSTL", 128), ("KC", 128), ("KS", 128),
                ("KM", 128), ("K8", 128), ("LT", 128), ("P15", 128), ("P2", 128), ("M64", 128), ("NBO", 128), ("BO4K", 128),
-               ("I8N", 128), ("IBIG", 128), ("NID", 128), ("ONE16", 128), ("BIGM", 128), ("SELP", 1024),
+               ("I8N", 128), ("IBIG", 128), ("NID", 128), ("ONE16", 128), ("K63", 8), ("K155", 128), ("PNUM", 128), ("ZC", 128), ("BO01", 128), ("INEG", 128), ("I8P", 128), ("SELP", 1024),
                ("SELN", 1024), ("DQ", 128), ("ZA", 128), ("ZB", 128)):
     tile(_n, "bfloat16", _c)
 for _n, _c in (("BOF", 128), ("MASK", 128), ("IDF", 128), ("DQF", 128), ("SELC", 8), ("DUM", 16), ("MCOL", 1), ("M64C", 1),
                ("THR", 1), ("THR2", 1), ("B135", 1), ("PC15", 1), ("PC2", 1), ("LIMF", 1), ("THETA", 1), ("CNT", 2), ("RJ", 2048),
-               ("QROW", 128), ("MB1", 1), ("PB1", 1), ("JB", 16), ("DC", 16), ("WM", 16), ("LL", 16), ("TT", 16), ("OFF", 16)):
+               ("QROW", 128), ("MB1", 1), ("PB1", 1), ("R01", 1), ("WN", 1), ("WP", 1), ("M3", 1), ("M3B", 1), ("JB", 16), ("DC", 16), ("WM", 16), ("LL", 16), ("TT", 16), ("OFF", 16)):
     tile(_n, "float32", _c)
 for _n, _c in (("MI", 1), ("MI2", 1), ("PCI", 1), ("PCI2", 1), ("LIMI", 1), ("CI", 1), ("CI2", 1), ("DI", 256), ("WI", 256), ("XN", 256)):
     tile(_n, "int32", _c)
@@ -41,7 +42,7 @@ tile("XS", "bfloat16", 256)
 tile("GL", "uint16", 16)
 tile("SL", "uint16", 16)
 for _h in range(2):
-    for _n in ("F1", "DHI", "DLO", "FULL", "ST", "OHS", "F2", "OHE", "OHK", "OHD", "MBH", "MBL", "VMW", "VB", "SG", "TFB", "Z"):
+    for _n in ("F1", "DHI", "DLO", "FULL", "ST", "OHS", "F2", "OHE", "NOE", "OHK", "OHD", "MBH", "MBL", "VMW", "VB", "SG", "TFB", "Z"):
         tile(_n + str(_h), "bfloat16", CH)
     for _n in ("SC", "SCA", "D1", "D2", "T32", "U32", "Y", "W2", "MBK", "VM", "MBA", "CF", "MB2", "D3", "VMD", "TM", "AA", "F0",
                "FN", "VI", "VV", "T1", "T2", "YP", "YQ", "YR"):
@@ -90,7 +91,7 @@ def rank_program(g, core, T, topo):
     last_w, readers, banks = {}, {}, {}
     dcount, now = [0], [0.0]
 
-    def add(eng, fn, rd, wr, cost, sem=None, need=1, extra=(), comp=True):
+    def add(eng, fn, rd, wr, cost, sem=None, need=1, extra=(), comp=True, acc=False):
         k = len(ops)
         deps = {}
         phys = {"SD": "S"}.get(eng, eng)
@@ -98,7 +99,7 @@ def rank_program(g, core, T, topo):
         def dep(o, kind):
             if o == k:
                 return
-            if kind == "war" and comp and ops[o]["phys"] == phys and ops[o]["comp"]:
+            if (kind == "war" or kind == "waw" and acc) and comp and ops[o]["phys"] == phys and ops[o]["comp"]:
                 deps.setdefault(o, "order")
             else:
                 deps[o] = "wait"
@@ -121,7 +122,7 @@ def rank_program(g, core, T, topo):
                     ep[1].append(k)
         for o in extra:
             deps.setdefault(o, "order")
-        ops.append(dict(eng=eng, phys=phys, comp=comp, fn=fn, deps=deps, cost=cost, sem=sem, need=need, rd=rd, wr=wr, bonus=now[0]))
+        ops.append(dict(eng=eng, phys=phys, comp=comp, fn=fn, deps=deps, cost=cost, sem=sem, need=need, name=(wr or rd)[0], base=now[0], bonus=now[0] + PRI.get((wr or rd)[0], 0)))
         for x in rd:
             readers.setdefault(x, []).append(k)
         for x in wr:
@@ -135,8 +136,8 @@ def rank_program(g, core, T, topo):
     def S(fn, rd, wr, n):
         return add("S", lambda: fn(g.scalar), rd, wr, 0.06 + max(n, 64) * 0.83 / 1000)
 
-    def P(fn, rd, wr, n):
-        return add("T", lambda: fn(g.tensor), rd, wr, 0.05 + n * 0.45 / 1000)
+    def P(fn, rd, wr, n, acc=False, extra=()):
+        return add("T", lambda: fn(g.tensor), rd, wr, 0.05 + n * 0.45 / 1000, acc=acc, extra=extra)
 
     def G(fn, rd, wr, n):
         return add("G", lambda: fn(g), rd, wr, 0.17 + n * 1.66 / 1000)
@@ -205,6 +206,7 @@ def rank_program(g, core, T, topo):
 
     for h in range(2):
         H = str(h)
+        now[0] = BONUS[9] * (1 - h)
         DI = t("DI", h * CH, h * CH + CH)
         WI = t("WI", h * CH, h * CH + CH)
         V(ts(t("FN" + H), WI, t("MCOL"), A.not_equal), ["WI", "MCOL"], ["FN" + H], 128)
@@ -213,6 +215,7 @@ def rank_program(g, core, T, topo):
         V(ts(t("VV" + H), t("VI" + H), t("MB1"), A.add, t("PC2"), A.add), ["VI" + H, "MB1", "PC2"], ["VV" + H], 128)
         V(cp(t("LU%d0" % h), DI), ["DI"], ["LU%d0" % h], 128)
         V(ts(t("T2" + H), WI, 1 / 64, A.mult), ["WI"], ["T2" + H], 128)
+    now[0] = 0.0
     for j in range(15, -1, -1):
         RJ = "RJ%d" % j
         rj = t("RJ", j * 128, j * 128 + 128)
@@ -220,18 +223,23 @@ def rank_program(g, core, T, topo):
         G((lambda rj: lambda q: q.affine_select(rj, rj, [[1, 128]], A.not_equal, 1.0, 0, -1))(rj), [RJ], [RJ], 128)
         for h in range(2):
             H = str(h)
+            now[0] = BONUS[9] * (1 - h)
             o, key = T["P1_" + H][:, 0, :], "P1_%s0" % H
             S(act(t("SG" + H), t("VV" + H), AF.Relu, t("JB", j, j + 1), -KK), ["VV" + H, "JB"], ["SG" + H], 128)
             P(mms([(o, rj, t("VV" + H))], True, False), [RJ, "VV" + H], [key], 512)
-            P(mms([(o, t("IDENT"), t("SG" + H))], False, True), ["IDENT", "SG" + H], [key], 128)
+            P(mms([(o, t("IDENT"), t("SG" + H))], False, True), ["IDENT", "SG" + H], [key], 128, True)
             V(tt(t("VV" + H), t("VV" + H), o, A.min), ["VV" + H, key], ["VV" + H], 128)
     for h in range(2):
         H = str(h)
+        now[0] = BONUS[9] * (1 - h)
         S(act(t("T1" + H), t("VV" + H), AF.Identity, t("PB1"), 1.0), ["VV" + H, "PB1"], ["T1" + H], 128)
         V(tt(t("W%d0" % h), t("T1" + H), t("T2" + H), A.add), ["T1" + H, "T2" + H], ["W%d0" % h], 256)
 
+    now[0] = 0.0
+
     V(ts(t("E16"), t("BO", 0, 128, 16), 16.0, A.mult), ["BO"], ["E16"], 64)
     V(ts(t("E16N"), t("BO", 0, 128, 16), -16.0, A.mult), ["BO"], ["E16N"], 64)
+    V(ts(t("E32N"), t("BO", 0, 128, 16), -32.0, A.mult), ["BO"], ["E32N"], 64)
     V(cp(t("SELC"), t("BO", 0, 128, 16)), ["BO"], ["SELC"], 64)
     G(lambda q: q.iota(t("KC"), [[0, 8], [-1, 16]], 15, 0, allow_small_or_imprecise_dtypes=True), [], ["KC"], 128)
     G(lambda q: q.affine_select(t("KS"), t("KC"), [[0, 128]], A.is_ge, 131072.0, 0, -1), ["KC"], ["KS"], 128)
@@ -241,25 +249,37 @@ def rank_program(g, core, T, topo):
     G(lambda q: q.affine_select(t("LT"), t("LT"), [[1, 128]], A.not_equal, -32.0, 0, -1), ["LT"], ["LT"], 128)
     V(tt(t("LT"), t("LT"), t("BO"), A.mult), ["LT", "BO"], ["LT"], 256)
     V(ts(t("THR"), t("MCOL"), 0.5, A.subtract, EPS / 2, A.max), ["MCOL"], ["THR"], 64)
-    V(ts(t("THR2"), t("MCOL"), 0.46875 * (1 - EPS), A.mult, 0.46875 * (15 * EPS - 32), A.add), ["MCOL"], ["THR2"], 64)
+    V(ts(t("THR"), t("THR"), 2.0, A.mult), ["THR"], ["THR"], 64)
+    V(ts(t("THR2"), t("MCOL"), EPS - 1, A.mult, 32 - 15 * EPS, A.add), ["MCOL"], ["THR2"], 64)
     V(tt(t("THR"), t("THR"), t("THR2"), A.add), ["THR", "THR2"], ["THR"], 64)
     V(ts(t("M64C"), t("MCOL"), 1 / 64, A.mult), ["MCOL"], ["M64C"], 64)
-    for nm, src, sc in (("P15", "BO", "PC15"), ("P2", "BO", "PC2"), ("M64", "BO", "M64C"), ("NBO", "BO", -1.0), ("BO4K", "BO", 4096.0),
-                        ("I8N", "IDENT", -8192.0), ("IBIG", "IDENT", BIG), ("NID", "IDENT", -1.0), ("IDF", "IDENT", 1.0)):
+    for nm, src, sc in (("P15", "BO", "PC15"), ("P2", "BO", "PC2"), ("M64", "BO", "M64C"), ("NBO", "BO", -0.5), ("BO4K", "BO", 4096.0),
+                        ("I8P", "IDENT", 8192.0), ("INEG", "IDENT", -BIG), ("IBIG", "IDENT", BIG), ("NID", "IDENT", -1.0), ("IDF", "IDENT", 1.0)):
         S(act(t(nm), t(src), AF.Copy, 0.0, t(sc) if sc in TILES else sc), [src] + ([sc] if sc in TILES else []), [nm], 128)
     for k, nm in enumerate(("ZA", "ZB")):
         G((lambda k, nm: lambda q: q.affine_select(t(nm), t("BO"), [[0, 8], [1, 16]], A.is_equal, 0.0, -k, 0))(k, nm), ["BO"], [nm], 128)
     V(lambda v: v.memset(t("ONE16"), 1 / 16), [], ["ONE16"], 64)
-    V(lambda v: v.memset(t("KM"), -BIG / 2), [], ["KM"], 64)
-    V(lambda v: v.memset(t("K8"), 4096.0), [], ["K8"], 64)
     V(ts(t("B135"), t("MCOL"), -1.0, A.mult, 135.0, A.add), ["MCOL"], ["B135"], 64)
     V(lambda v: v.memset(t("MASK"), 1.0), [], ["MASK"], 128)
     V(lambda v: v.memset(t("MASK", 0, 128, 16), 0.0), [], ["MASK"], 64)
-    V(lambda v: v.memset(t("BIGM"), 65536.0), [], ["BIGM"], 64)
-    G(lambda q: q.affine_select(t("BIGM"), t("BIGM"), [[1, 128]], A.is_ge, 0.0, 0, -1), ["BIGM"], ["BIGM"], 128)
+    V(lambda v: v.memset(t("K63"), -31.5), [], ["K63"], 64)
+    V(lambda v: v.memset(t("K155"), -7.75), [], ["K155"], 64)
+    G(lambda q: q.iota(t("PNUM"), [[1, 128]], 0, 0, allow_small_or_imprecise_dtypes=True), [], ["PNUM"], 128)
+    G(lambda q: q.affine_select(t("PNUM"), t("PNUM"), [[0, 128]], A.is_ge, 1.0, 0, -1), ["PNUM"], ["PNUM"], 128)
+    V(lambda v: v.memset(t("ZC"), 0.0), [], ["ZC"], 64)
+    for r, m in ((0, 2), (1, 3)):
+        G((lambda r, m: lambda q: q.affine_select(t("ZC"), t("ZC"), [[0, 8], [1, 16]], A.not_equal, 1.0, 64 * r - m, -64))(r, m), ["ZC"], ["ZC"], 128)
+    V(ts(t("R01"), t("MCOL"), 1.5, A.is_lt), ["MCOL"], ["R01"], 64)
+    V(ts(t("BO01"), t("BO"), t("R01"), A.mult), ["BO", "R01"], ["BO01"], 64)
+    V(ts(t("WN"), t("R01"), -255.0, A.mult, -1.0, A.add), ["R01"], ["WN"], 64)
+    V(ts(t("M3"), t("MCOL"), 2.5, A.is_lt), ["MCOL"], ["M3"], 64)
+    V(tt(t("WN"), t("WN"), t("M3"), A.mult), ["WN", "M3"], ["WN"], 64)
+    V(ts(t("M3B"), t("MCOL"), 3.0, A.is_equal, 64.0, A.mult), ["MCOL"], ["M3B"], 64)
+    V(tt(t("WP"), t("M3B"), t("WN"), A.subtract), ["M3B", "WN"], ["WP"], 64)
     G(lambda q: q.affine_select(t("SELP"), t("SELP"), [[-16, 8], [0, 128]], A.is_ge, 0.0, 0, 1), ["SELP"], ["SELP"], 1024)
     G(lambda q: q.affine_select(t("SELP"), t("SELP"), [[16, 8], [0, 128]], A.is_ge, 0.0, 15, -1), ["SELP"], ["SELP"], 1024)
-    S(act(t("SELN"), t("SELP"), AF.Copy, 0.0, -1.0), ["SELP"], ["SELN"], 1024)
+    S(act(t("SELN"), t("SELP"), AF.Copy, 0.0, t("WN")), ["SELP", "WN"], ["SELN"], 1024)
+    S(act(t("SELP"), t("SELP"), AF.Copy, 0.0, t("WP")), ["SELP", "WP"], ["SELP"], 1024)
     G(lambda q: q.iota(t("DUM"), [[16, 16]], PAD + 1, 0, allow_small_or_imprecise_dtypes=True), [], ["DUM"], 16)
     V(ts(t("DUM"), t("DUM"), t("MCOL"), A.add), ["DUM", "MCOL"], ["DUM"], 64)
     for k in range(NP):
@@ -287,8 +307,8 @@ def rank_program(g, core, T, topo):
         H = str(h)
         for (e, a, b), key in zip(plan, kx):
             o = T["P3_" + H][:, slot, a:b]
-            P(mms([(o, t("IDENT"), x[:, 16 * a + m:16 * b:16]) for m in range(16)] + [(o, t("NBO"), t(f, a, b))]),
-              ["IDENT", "NBO", f, key], ["P3_%s%d" % (H, slot)] if a == 0 else ["P3_%s%d+%d" % (H, slot, a)], 17 * max(64, b - a))
+            P(mms([(o, t("IDENT"), x[:, 16 * a + m:16 * b:16]) for m in range(16)] + [(o, t("NBO"), t(f, a, b)), (o, t("CONSTL"), t("K155", a, b))]),
+              ["IDENT", "NBO", "CONSTL", "K155", f, key], ["P3_%s%d" % (H, slot)] if a == 0 else ["P3_%s%d+%d" % (H, slot, a)], 18 * max(64, b - a))
         return ["P3_%s%d" % (H, slot)] + ["P3_%s%d+%d" % (H, slot, a) for e, a, b in plan if a]
 
     def argmax(h):
@@ -305,11 +325,11 @@ def rank_program(g, core, T, topo):
         x = T["x1" + H]
         kx = gather("x1", LU, h, SHARE[("a" if vt else "f") + H])
         V(ts(t("D1" + H), t(LU), 1.0, A.add), [LU], ["D1" + H], 128)
-        V(ts(t("F1" + H), t("D1" + H), 3457.0, A.is_lt, 0.46875, A.add), ["D1" + H], ["F1" + H], 128)
+        S(act(t("F1" + H), t("D1" + H), AF.Sign, 3456.5, -1.0), ["D1" + H], ["F1" + H], 128)
         S(act(t("DHI" + H), t("D1" + H), AF.Copy), ["D1" + H], ["DHI" + H], 128)
         V(tt(t("DLO" + H), t("D1" + H), t("DHI" + H), A.subtract), ["D1" + H, "DHI" + H], ["DLO" + H], 256)
         P(mms([(p1[:, 3, :], t("BO"), t("F1" + H))]), ["BO", "F1" + H], ["P1_%s3" % H], 128)
-        S(act(t("FULL" + H), p1[:, 3, :], AF.Relu, -22.5), ["P1_%s3" % H], ["FULL" + H], 128)
+        S(act(t("FULL" + H), p1[:, 3, :], AF.Relu, -15.0), ["P1_%s3" % H], ["FULL" + H], 128)
         P(mms([(p0[:, 0:128], t("CONSTL"), t("KC"))] + [(p0[:, m:128:16], x[:, m::16], t("E16")) for m in range(16)]),
           ["CONSTL", "KC", "E16"] + kx, ["P0_" + H], 128 + 16 * 64)
         argmax(h)
@@ -332,11 +352,12 @@ def rank_program(g, core, T, topo):
         p0, p1, p3 = T["P0_" + H], T["P1_" + H], T["P3_" + H]
         x = T["x2" + H]
         kx = gather("x2", "L2" + H, h, SHARE["x2"])
-        V(ts(t("F2" + H), t("D2" + H), 3457.0, A.is_lt, 0.46875, A.add), ["D2" + H], ["F2" + H], 128)
+        S(act(t("F2" + H), t("D2" + H), AF.Sign, 3456.5, -1.0), ["D2" + H], ["F2" + H], 128)
         P(mms([(p1[:, 2, :], t("LT"), t("F2" + H))]), ["LT", "F2" + H], ["P1_%s2" % H], 128)
         P(mms([(p1[:, 3, :], t("IDF"), t(W)), (p1[:, 3, :], t("IBIG"), t("F2" + H))]), ["IDF", W, "IBIG", "F2" + H], ["P1_%s3" % H], 640)
         V(ts(t("OHE" + H), p1[:, 2, :], t("THR"), A.is_ge), ["P1_%s2" % H, "THR"], ["OHE" + H], 128)
-        S(act(t("W2" + H), p1[:, 3, :], AF.Relu, -1.46875 * BIG), ["P1_%s3" % H], ["W2" + H], 128)
+        S(act(t("NOE" + H), t("OHE" + H), AF.Identity, 1.0, -1.0), ["OHE" + H], ["NOE" + H], 128)
+        S(act(t("W2" + H), p1[:, 3, :], AF.Relu, -BIG), ["P1_%s3" % H], ["W2" + H], 128)
         V(cp(t("A2" + H), t("W2" + H)), ["W2" + H], ["A2" + H], 128)
         ku = sums(h, 2, x, "F2" + H, SHARE["x2"], kx)
         S(act(t("U32" + H), p3[:, 2, :], AF.Identity, t("B135"), 16.0), ku + ["B135"], ["U32" + H], 128)
@@ -366,7 +387,7 @@ def rank_program(g, core, T, topo):
                 for m in ms:
                     r = pe.matmul(p0[:, m:128:16], z[:, m::16], t("E16"), False, m == 15)
                 return r
-            P(yf, ["CONSTL", "KC", "E16", "z%s:%d" % (H, q)], ["P0_" + H], 128 * (1 - q) + 8 * 64)
+            P(yf, ["CONSTL", "KC", "E16", "z%s:%d" % (H, q)], ["P0_" + H], 128 * (1 - q) + 8 * 64, q == 1)
         argmax(h)
         P(mms([(p1[:, 0, :], t("OHD" + H), t("IDENT"))]), ["OHD" + H, "IDENT"], ["P1_%s0" % H], 128)
         V(tt(t("MBK" + H), p1[:, 0, :], t("D2" + H), A.mult), ["P1_%s0" % H, "D2" + H], ["MBK" + H], 128)
@@ -385,15 +406,33 @@ def rank_program(g, core, T, topo):
         kx = gather("xc", "CU" + H, h, SHARE["xc"])
         V(ts(t("CF" + H), t("CU" + H), 1.0, A.add), ["CU" + H], ["CF" + H], 128)
         P(mms([(p1[:, 2, :], t("BOF"), t("MBA" + H)), (p1[:, 2, :], t("M64"), t("OHK" + H)), (p1[:, 2, :], t("P2"), t("OHE" + H)),
-               (p1[:, 2, :], t("IBIG"), t("OHE" + H)), (p1[:, 2, :], t("CONSTL"), t("KM"))]),
-          ["BOF", "MBA" + H, "M64", "OHK" + H, "P2", "OHE" + H, "IBIG", "CONSTL", "KM"], ["P1_%s2" % H], 1024)
+               (p1[:, 2, :], t("INEG"), t("NOE" + H))]),
+          ["BOF", "MBA" + H, "M64", "OHK" + H, "P2", "OHE" + H, "INEG", "NOE" + H], ["P1_%s2" % H], 896)
         last = vt == NV - 1
         WN = ("SW%d%d" % (h, vt + 1)) if not last else "W2" + H
         V(tt(t(WN), t("W2" + H), p1[:, 2, :], A.max), ["W2" + H, "P1_%s2" % H], [WN], 128)
         if not last:
             send(WN, "W%d%d" % (h, vt + 1), 6 * h + 2 * vt)
-        P(mms([(p0[:, 0:128], t("CONSTL"), t("KS"))], True, False), ["CONSTL", "KS"], ["P0_" + H], 128)
-        for b in range(4):
+        ks = P(mms([(p0[:, 0:128], t("CONSTL"), t("KS"))], True, False), ["CONSTL", "KS"], ["P0_" + H], 128)
+        def mf(v):
+            for j in range(12, 16):
+                r = v.tensor_tensor(ax[:, j, :], xc[:, j::16], t("VB" + H), A.max)
+            return r
+        V(mf, kx + ["VB" + H], ["ax%s:3" % H], 1024)
+
+        def lf(pe):
+            for j in range(12, 16):
+                pe.matmul(p0[:, j:128:16], xc[:, j::16], t("E16"), False, False)
+                r = pe.matmul(p0[:, j:128:16], t("VB" + H), t("E16"), False, False)
+            return r
+        parts = [P(lf, ["E16", "VB" + H] + kx, ["P0_%s#l" % H], 512, True, [ks])]
+
+        def gf(pe):
+            for j in range(12, 16):
+                r = pe.matmul(p0[:, j:128:16], ax[:, j, :], t("E32N"), False, False)
+            return r
+        parts.append(P(gf, ["E32N", "ax%s:3" % H], ["P0_%s#g" % H], 256, True, [ks]))
+        for b in range(3):
             pb, kb = (p3, "P3_%s" % H) if b % 2 == 0 else (p1, "P1_%s" % H)
 
             def df(pe, b=b, pb=pb):
@@ -406,15 +445,14 @@ def rank_program(g, core, T, topo):
 
             def sf(pe, b=b):
                 for j in range(4 * b, 4 * b + 4):
-                    r = pe.matmul(p0[:, j:128:16], ax[:, j, :], t("E16N"), False, j == 15)
+                    r = pe.matmul(p0[:, j:128:16], ax[:, j, :], t("E16N"), False, j == 11)
                 return r
-            P(sf, ["E16N", "ax%s:%d" % (H, b)], ["P0_" + H], 256)
+            parts.append(P(sf, ["E16N", "ax%s:%d" % (H, b)], ["P0_%s#%d" % (H, b) if b < 2 else "P0_" + H], 256, True, [ks] if b < 2 else parts))
         argmax(h)
         P(mms([(p1[:, 0, :], t("OHD" + H), t("IDENT"))]), ["OHD" + H, "IDENT"], ["P1_%s0" % H], 128)
         V(tt(t("MB2" + H), p1[:, 0, :], t("CF" + H), A.mult), ["P1_%s0" % H, "CF" + H], ["MB2" + H], 128)
-        P(mms([(p1[:, 1, :], t("I8N"), t("OHE" + H)), (p1[:, 1, :], t("CONSTL"), t("K8"))], True, False),
-          ["I8N", "OHE" + H, "CONSTL", "K8"], ["P1_%s1" % H], 256)
-        P(mms([(p1[:, 1, :], t("BOF"), t("MB2" + H))], False, True), ["BOF", "MB2" + H], ["P1_%s1" % H], 512)
+        P(mms([(p1[:, 1, :], t("I8P"), t("NOE" + H))], True, False), ["I8P", "NOE" + H], ["P1_%s1" % H], 128)
+        P(mms([(p1[:, 1, :], t("BOF"), t("MB2" + H))], False, True), ["BOF", "MB2" + H], ["P1_%s1" % H], 512, True)
         V(tt(t("D3" + H), t("D2" + H), p1[:, 1, :], A.min), ["D2" + H, "P1_%s1" % H], ["D3" + H], 128)
         if not last:
             LN = "SLU%d%d" % (h, vt + 1)
@@ -442,9 +480,10 @@ def rank_program(g, core, T, topo):
         P(mms([(p2[:, 3, :], t("IDENT"), t("OHS" + H))]), ["IDENT", "OHS" + H], [q2 + "3"], 128)
         V(tt(t("MBH" + H), p2[:, 3, :], t("DHI" + H), A.mult), [q2 + "3", "DHI" + H], ["MBH" + H], 128)
         V(tt(t("MBL" + H), p2[:, 3, :], t("DLO" + H), A.mult), [q2 + "3", "DLO" + H], ["MBL" + H], 128)
-        P(mms([(p2[:, 1, :], t("ZA"), t("MBH" + H)), (p2[:, 1, :], t("ZB"), t("MBL" + H))]), ["MBH" + H, "MBL" + H, "ZA", "ZB"], [q2 + "1"], 256)
+        P(mms([(p2[:, 1, :], t("ZA"), t("MBH" + H)), (p2[:, 1, :], t("ZB"), t("MBL" + H)), (p2[:, 1, :], t("ZC"), t("PNUM"))]),
+          ["MBH" + H, "MBL" + H, "ZA", "ZB", "ZC", "PNUM"], [q2 + "1"], 384)
         S(act(t("Z" + H), p2[:, 1, :], AF.Copy), [q2 + "1"], ["Z" + H], 128)
-        P(mms([(p2[:, 0, :], t("Z" + H), t("BO"))]), ["Z" + H, "BO"], [q2 + "0"], 128)
+        P(mms([(p2[:, 0, :], t("Z" + H), t("BO01"))]), ["Z" + H, "BO01"], [q2 + "0"], 128)
         P(mms([(p2[:, 2, :], t("ONE16"), t("ST" + H))]), ["ONE16", "ST" + H], [q2 + "2"], 128)
         V(tt(t("VMD" + H), p2[:, 0, :], t("DQF"), A.mult), [q2 + "0", "DQF"], ["VMD" + H], 128)
         if vt < NV - 1:
@@ -455,8 +494,7 @@ def rank_program(g, core, T, topo):
             b = q2
             o = T[b][:, w % 4, :]
             sp, sn = t("SELP", w * 128, w * 128 + 128), t("SELN", w * 128, w * 128 + 128)
-            P(mms([(o, sp, t("Z" + H)), (o, t("Z" + H), sn), (o, t("IDENT"), t("BIGM"))]),
-              ["SELP", "SELN", "Z" + H, "IDENT", "BIGM"], [b + str(w % 4)], 384)
+            P(mms([(o, sp, t("Z" + H)), (o, t("Z" + H), sn)]), ["SELP", "SELN", "Z" + H], [b + str(w % 4)], 256)
             if w % 4 == 3:
                 for u in range(w - 3, w + 1):
                     V((lambda u, b: lambda v: v.tensor_reduce(t("RED" + H, u, u + 1), T[b][:, u % 4, :], AxisListType.X, A.min,
@@ -470,7 +508,8 @@ def rank_program(g, core, T, topo):
         pa, pb = T.P2_0, T.P2_1
         for h in range(2):
             H = str(h)
-            P(mms([(pa[:, 3, 8 * h:8 * h + 8], t("VMW" + H), t("BO", 0, 128, 16))]), ["VMW%s%d" % (H, w) for w in range(8)] + ["BO"], ["P2_03%d" % h], 64)
+            P(mms([(pa[:, 3, 8 * h:8 * h + 8], t("VMW" + H), t("BO", 0, 128, 16)), (pa[:, 3, 8 * h:8 * h + 8], t("CONSTL"), t("K63"))]),
+              ["VMW%s%d" % (H, w) for w in range(8)] + ["BO", "CONSTL", "K63"], ["P2_03%d" % h], 128)
         V(ts(t("GL"), t("DC"), 1.0, A.subtract), ["DC0", "DC1"], ["GL"], 64)
         S(act(t("XS"), XALL.indirect(t("GL")), AF.Copy), XK + ["GL"], ["XS"], 400)
         for h in range(2):
@@ -519,7 +558,7 @@ def rank_program(g, core, T, topo):
     emit(g, T, ops, schedule(ops), QUEUE)
 
 
-WAKE = 0.12
+WAKE, LOOK, IDLE = 0.12, 0.06, 0.0
 
 
 def schedule(ops):
@@ -534,23 +573,22 @@ def schedule(ops):
     for k in range(n):
         tail[k] += ops[k]["bonus"]
     left = [len(o["deps"]) for o in ops]
-    ready, fin, free = {}, [0.0] * n, {}
+    fin, free, order = [0.0] * n, {}, []
+    ready = {}
     for k in range(n):
         if left[k] == 0:
-            ready.setdefault(ops[k]["phys"], []).append((0.0, k))
-    order = []
+            ready.setdefault(ops[k]["phys"], {})[k] = 0.0
     while ready:
         best = None
         for e, lst in ready.items():
             f = free.get(e, 0.0)
-            t0 = min(max(f, r) for r, k in lst)
-            c = max((tail[k], -k) for r, k in lst if max(f, r) <= t0 + 0.03)
+            t0 = max(f, min(lst.values()))
             if best is None or t0 < best[0]:
-                best = (t0, e, -c[1])
-        t0, e, k = best
+                best = (t0, e)
+        t0, e = best
         lst = ready[e]
-        st = max(free.get(e, 0.0), [r for r, q in lst if q == k][0])
-        lst[:] = [x for x in lst if x[1] != k]
+        k = max((tail[k] - IDLE * max(0.0, r - t0), -k) for k, r in lst.items() if r <= t0 + LOOK)[1] * -1
+        st = max(free.get(e, 0.0), lst.pop(k))
         if not lst:
             del ready[e]
         o = ops[k]
@@ -561,10 +599,9 @@ def schedule(ops):
         for s in succ[k]:
             left[s] -= 1
             if left[s] == 0:
-                r = max([fin[d] + (WAKE if ops[s]["deps"][d] == "wait" else 0.0) for d in ops[s]["deps"]])
-                ready.setdefault(ops[s]["phys"], []).append((r, s))
+                ready.setdefault(ops[s]["phys"], {})[s] = max([fin[d] + (WAKE if ops[s]["deps"][d] == "wait" else 0.0) for d in ops[s]["deps"]])
     ops[0]["makespan"] = max(fin)
-    ops[0]["fin"] = {k: fin[k] for k in order}
+    ops[0]["fin"] = dict(enumerate(fin))
     return order
 
 

import math
from concourse.mybir import dt, AluOpType, AxisListType, ActivationFunctionType

A = AluOpType
AF = ActivationFunctionType
N, D, NV, CH = 4, 3456, 4, 128
PAD = 4112
XW = PAD + 256
MAGIC = 12582912.0
BIG = 131072.0
KK = 4194304.0
NP = 4
PW = D // NP
HALF = (("S", 0, 64), ("V", 64, 128))
SHARE = {"f0": (("S", 0, 32), ("V", 32, 64), ("S", 64, 96), ("V", 96, 128)), "f1": (("S", 0, 32), ("V", 32, 64), ("S", 64, 96), ("V", 96, 128)),
         "a0": HALF, "a1": HALF, "x2": HALF, "xc": HALF}
PRI = {}
BONUS = [-4, -2, -2, 13, 18, 1, 0, 2, 0, 6]

POOLS = {"float32": ("pf", 4), "bfloat16": ("pb", 2), "int32": ("pi", 4), "uint16": ("pu", 2)}
TILES, SIZE = {}, {"float32": 0, "bfloat16": 0, "int32": 0, "uint16": 0}


def tile(name, dtype, cols):
    per = 32 // POOLS[dtype][1]
    TILES[name] = (POOLS[dtype][0], SIZE[dtype], cols)
    SIZE[dtype] += -(-cols // per) * per


for _n, _c in (("ONES", 128), ("IDENT", 128), ("BO", 128), ("E16", 8), ("E16N", 8), ("E32N", 8), ("CONSTL", 128), ("KC", 128), ("KS", 128),
               ("KM", 128), ("K8", 128), ("LT", 128), ("P15", 128), ("P2", 128), ("M64", 128), ("NBO", 128), ("BO4K", 128),
               ("I8N", 128), ("IBIG", 128), ("NID", 128), ("ONE16", 128), ("K63", 8), ("K155", 128), ("PNUM", 128), ("ZC", 128), ("BO01", 128), ("INEG", 128), ("I8P", 128), ("SELP", 1024),
               ("SELN", 1024), ("DQ", 128), ("ZA", 128), ("ZB", 128)):
    tile(_n, "bfloat16", _c)
for _n, _c in (("BOF", 128), ("MASK", 128), ("IDF", 128), ("DQF", 128), ("SELC", 8), ("DUM", 16), ("MCOL", 1), ("M64C", 1),
               ("THR", 1), ("THR2", 1), ("B135", 1), ("PC15", 1), ("PC2", 1), ("LIMF", 1), ("THETA", 1), ("CNT", 2), ("RJ", 2048),
               ("QROW", 128), ("MB1", 1), ("PB1", 1), ("R01", 1), ("WN", 1), ("WP", 1), ("M3", 1), ("M3B", 1), ("JB", 16), ("DC", 16), ("WM", 16), ("LL", 16), ("TT", 16), ("OFF", 16)):
    tile(_n, "float32", _c)
for _n, _c in (("MI", 1), ("MI2", 1), ("PCI", 1), ("PCI2", 1), ("LIMI", 1), ("CI", 1), ("CI2", 1), ("DI", 256), ("WI", 256), ("XN", 256)):
    tile(_n, "int32", _c)
tile("XS", "bfloat16", 256)
tile("GL", "uint16", 16)
tile("SL", "uint16", 16)
for _h in range(2):
    for _n in ("F1", "DHI", "DLO", "FULL", "ST", "OHS", "F2", "OHE", "NOE", "OHK", "OHD", "MBH", "MBL", "VMW", "VB", "SG", "TFB", "Z"):
        tile(_n + str(_h), "bfloat16", CH)
    for _n in ("SC", "SCA", "D1", "D2", "T32", "U32", "Y", "W2", "MBK", "VM", "MBA", "CF", "MB2", "D3", "VMD", "TM", "AA", "F0",
               "FN", "VI", "VV", "T1", "T2", "YP", "YQ", "YR"):
        tile(_n + str(_h), "float32", CH)
    for _n in ("TI", "GI", "A2"):
        tile(_n + str(_h), "int32", CH)
    tile("RED" + str(_h), "float32", 8)
    for _n in ("L2", "CU"):
        tile(_n + str(_h), "uint16", CH)
    tile("LC" + str(_h), "uint16", 16)
    for _t in range(NV):
        tile("LU%d%d" % (_h, _t), "uint16", CH)
        tile("W%d%d" % (_h, _t), "float32", CH)
    for _t in range(1, NV):
        tile("SLU%d%d" % (_h, _t), "uint16", CH)
        tile("SW%d%d" % (_h, _t), "float32", CH)

SCRATCH = {"X": ("sbuf", [128, XW], "bfloat16"), "Y": ("sbuf", [128, XW], "bfloat16"), "R": ("sbuf", [128, D], "int32")}
for _d in POOLS:
    SCRATCH[POOLS[_d][0]] = ("sbuf", [128, SIZE[_d]], _d)
for _h in range(2):
    for _n in ("x1", "x2", "z", "xc"):
        SCRATCH[_n + str(_h)] = ("sbuf", [128, 16 * CH], "bfloat16")
    SCRATCH["ax" + str(_h)] = ("sbuf", [128, 16, CH], "bfloat16")
    SCRATCH["P0_" + str(_h)] = ("psum", [128, 512], "float32")
    for _b in (1, 2, 3):
        SCRATCH["P%d_%d" % (_b, _h)] = ("psum", [128, 4, CH], "float32")

SEMAPHORES = ["cV", "cS", "cT", "cG"] + ["d%d" % k for k in range(40)] + \
    ["r%d" % k for k in range(12)] + ["l%d" % k for k in range(12)]


def rank_program(g, core, T, topo):
    rank = T.rank_of(core)
    if rank is None:
        return
    nxt, prv = T.cores[(rank + 1) % N], T.cores[(rank - 1) % N]
    QUEUE = {"V": g.vector, "S": g.scalar, "T": g.tensor, "G": g, "Y": g.sync, "SD": g.scalar}

    def t(name, a=0, b=None, s=None):
        pool, off, cols = TILES[name]
        b = cols if b is None else b
        return T[pool][:, off + a:off + b:s] if s else T[pool][:, off + a:off + b]

    ops = []
    last_w, readers, banks = {}, {}, {}
    dcount, now = [0], [0.0]

    def add(eng, fn, rd, wr, cost, sem=None, need=1, extra=(), comp=True, acc=False):
        k = len(ops)
        deps = {}
        phys = {"SD": "S"}.get(eng, eng)

        def dep(o, kind):
            if o == k:
                return
            if (kind == "war" or kind == "waw" and acc) and comp and ops[o]["phys"] == phys and ops[o]["comp"]:
                deps.setdefault(o, "order")
            else:
                deps[o] = "wait"
        for x in rd:
            if x in last_w:
                dep(last_w[x], "raw")
        for x in wr:
            if x in last_w:
                dep(last_w[x], "waw")
            for o in readers.get(x, ()):
                dep(o, "war")
        for x in sorted(set(rd) | set(wr)):
            if x[0] == "P" and x[2:3] == "_":
                ep = banks.setdefault(x[:4], [phys, [], []])
                if ep[0] != phys:
                    ep[0], ep[1], ep[2] = phys, [], ep[1]
                for o in ep[2]:
                    dep(o, "bank")
                if k not in ep[1]:
                    ep[1].append(k)
        for o in extra:
            deps.setdefault(o, "order")
        ops.append(dict(eng=eng, phys=phys, comp=comp, fn=fn, deps=deps, cost=cost, sem=sem, need=need, name=(wr or rd)[0], base=now[0], bonus=now[0] + PRI.get((wr or rd)[0], 0)))
        for x in rd:
            readers.setdefault(x, []).append(k)
        for x in wr:
            last_w[x] = k
            readers[x] = []
        return k

    def V(fn, rd, wr, n, c=0.83):
        return add("V", lambda: fn(g.vector), rd, wr, 0.04 + max(n, 64) * c / 1000)

    def S(fn, rd, wr, n):
        return add("S", lambda: fn(g.scalar), rd, wr, 0.06 + max(n, 64) * 0.83 / 1000)

    def P(fn, rd, wr, n, acc=False, extra=()):
        return add("T", lambda: fn(g.tensor), rd, wr, 0.05 + n * 0.45 / 1000, acc=acc, extra=extra)

    def G(fn, rd, wr, n):
        return add("G", lambda: fn(g), rd, wr, 0.17 + n * 1.66 / 1000)

    def dma(eng, out, in_, rd, wr, lat):
        s = "d%d" % dcount[0]
        dcount[0] += 1
        return add(eng, lambda: QUEUE[eng].dma_start(out, in_), rd, wr, lat, sem=s, need=16, comp=False)

    def ts(out, i0, s1, op0, s2=None, op1=None):
        if s2 is None:
            return lambda v: v.tensor_scalar(out, i0, s1, None, op0)
        return lambda v: v.tensor_scalar(out, i0, s1, s2, op0, op1)

    def tt(out, a, b, op):
        return lambda v: v.tensor_tensor(out, a, b, op)

    def cp(out, a):
        return lambda v: v.tensor_copy(out, a)

    def act(out, a, func=AF.Identity, bias=0.0, scale=1.0):
        return lambda s: s.activation(out, a, func, bias=bias, scale=scale)

    def mms(lst, start=True, stop=True):
        def f(pe):
            r = None
            for k, (o, l, x) in enumerate(lst):
                r = pe.matmul(o, l, x, start and k == 0, stop and k == len(lst) - 1)
            return r
        return f

    dma("Y", t("WI"), T.why[:], [], ["WI"], 2.5)
    dma("SD", t("DI"), T.drugs[:], [], ["DI"], 2.5)
    for k in range(NP):
        dma("Y" if k % 2 == 0 else "SD", T.X[:, k * PW:(k + 1) * PW], T.eff[:, k * PW:(k + 1) * PW], [], ["Xr%d" % k], 4.0 + 1.2 * k)
    dma("Y", t("LIMI"), T.lim[:], [], ["LIMI"], 3)
    dma("Y", T.R[:, :D // 2], T.rem[:, :D // 2], [], ["Ra"], 11.0)
    dma("Y", T.R[:, D // 2:], T.rem[:, D // 2:], [], ["Rb"], 11.0)

    LN2 = math.log(2.0)
    V(lambda v: v.memset(t("ONES"), 1.0), [], ["ONES"], 64)
    V(lambda v: v.memset(t("SELP"), 1.0), [], ["SELP"], 512)
    V(lambda v: v.memset(T.X[:, D:], 0.0), [], ["Xz"], 456)
    G(lambda q: q.iota(t("MI"), [[0, 1]], 0, 1), [], ["MI"], 1)
    V(ts(t("MI2"), t("MI"), 15, A.bitwise_and), ["MI"], ["MI2"], 64)
    V(cp(t("MCOL"), t("MI2")), ["MI2"], ["MCOL"], 64)
    G(lambda q: q.affine_select(t("IDENT"), t("ONES"), [[-1, 128]], A.is_equal, 0.0, 0, 1), ["ONES"], ["IDENT"], 128)
    G(lambda q: q.affine_select(t("BO"), t("ONES"), [[-16, 8], [0, 16]], A.is_ge, 0.0, 0, 1), ["ONES"], ["BO"], 128)
    G(lambda q: q.affine_select(t("BO"), t("BO"), [[16, 8], [0, 16]], A.is_ge, 0.0, 15, -1), ["BO"], ["BO"], 128)
    G(lambda q: q.iota(t("QROW"), [[0, 8], [1, 16]], 0, 0, allow_small_or_imprecise_dtypes=True), [], ["QROW"], 128)
    V(ts(t("DQ"), t("QROW"), t("MCOL"), A.is_equal), ["QROW", "MCOL"], ["DQ"], 128)
    G(lambda q: q.affine_select(t("CONSTL"), t("ONES"), [[0, 128]], A.is_ge, 0.0, 1, -1), ["ONES"], ["CONSTL"], 128)
    S(act(t("PC2"), t("MCOL"), AF.Exp, 0.0, LN2), ["MCOL"], ["PC2"], 1500)
    V(cp(t("PCI2"), t("PC2")), ["PC2"], ["PCI2"], 64)
    V(cp(t("PC2"), t("PCI2")), ["PCI2"], ["PC2"], 64)
    S(act(t("PC15"), t("MCOL"), AF.Exp, 0.0, -LN2), ["MCOL"], ["PC15"], 64)
    V(ts(t("PCI"), t("PC15"), 32768.0, A.mult), ["PC15"], ["PCI"], 64)
    V(cp(t("PC15"), t("PCI")), ["PCI"], ["PC15"], 64)
    S(act(t("DQF"), t("DQ"), AF.Copy), ["DQ"], ["DQF"], 128)
    S(act(t("BOF"), t("BO"), AF.Copy), ["BO"], ["BOF"], 128)
    V(ts(t("MB1"), t("MCOL"), -BIG, A.mult, -BIG, A.add), ["MCOL"], ["MB1"], 64)
    V(ts(t("PB1"), t("MCOL"), BIG, A.mult, BIG, A.add), ["MCOL"], ["PB1"], 64)
    G(lambda q: q.iota(t("JB"), [[int(BIG) // 8, 16]], 0, 0, allow_small_or_imprecise_dtypes=True), [], ["JB"], 16)
    V(ts(t("JB"), t("JB"), 8.0, A.mult, t("PB1"), A.subtract), ["JB", "PB1"], ["JB"], 64)
    V(ts(t("JB"), t("JB"), BIG - 0.5, A.add, KK, A.mult), ["JB"], ["JB"], 64)

    for h in range(2):
        H = str(h)
        now[0] = BONUS[9] * (1 - h)
        DI = t("DI", h * CH, h * CH + CH)
        WI = t("WI", h * CH, h * CH + CH)
        V(ts(t("FN" + H), WI, t("MCOL"), A.not_equal), ["WI", "MCOL"], ["FN" + H], 128)
        V(ts(t("VI" + H), WI, 1.0, A.add, BIG, A.mult), ["WI"], ["VI" + H], 128)
        V(tt(t("VI" + H), t("VI" + H), t("FN" + H), A.mult), ["VI" + H, "FN" + H], ["VI" + H], 256)
        V(ts(t("VV" + H), t("VI" + H), t("MB1"), A.add, t("PC2"), A.add), ["VI" + H, "MB1", "PC2"], ["VV" + H], 128)
        V(cp(t("LU%d0" % h), DI), ["DI"], ["LU%d0" % h], 128)
        V(ts(t("T2" + H), WI, 1 / 64, A.mult), ["WI"], ["T2" + H], 128)
    now[0] = 0.0
    for j in range(15, -1, -1):
        RJ = "RJ%d" % j
        rj = t("RJ", j * 128, j * 128 + 128)
        S(act(rj, t("BOF"), AF.Copy, 0.0, t("DQF", j, j + 1)), ["BOF", "DQF"], [RJ], 128)
        G((lambda rj: lambda q: q.affine_select(rj, rj, [[1, 128]], A.not_equal, 1.0, 0, -1))(rj), [RJ], [RJ], 128)
        for h in range(2):
            H = str(h)
            now[0] = BONUS[9] * (1 - h)
            o, key = T["P1_" + H][:, 0, :], "P1_%s0" % H
            S(act(t("SG" + H), t("VV" + H), AF.Relu, t("JB", j, j + 1), -KK), ["VV" + H, "JB"], ["SG" + H], 128)
            P(mms([(o, rj, t("VV" + H))], True, False), [RJ, "VV" + H], [key], 512)
            P(mms([(o, t("IDENT"), t("SG" + H))], False, True), ["IDENT", "SG" + H], [key], 128, True)
            V(tt(t("VV" + H), t("VV" + H), o, A.min), ["VV" + H, key], ["VV" + H], 128)
    for h in range(2):
        H = str(h)
        now[0] = BONUS[9] * (1 - h)
        S(act(t("T1" + H), t("VV" + H), AF.Identity, t("PB1"), 1.0), ["VV" + H, "PB1"], ["T1" + H], 128)
        V(tt(t("W%d0" % h), t("T1" + H), t("T2" + H), A.add), ["T1" + H, "T2" + H], ["W%d0" % h], 256)

    now[0] = 0.0

    V(ts(t("E16"), t("BO", 0, 128, 16), 16.0, A.mult), ["BO"], ["E16"], 64)
    V(ts(t("E16N"), t("BO", 0, 128, 16), -16.0, A.mult), ["BO"], ["E16N"], 64)
    V(ts(t("E32N"), t("BO", 0, 128, 16), -32.0, A.mult), ["BO"], ["E32N"], 64)
    V(cp(t("SELC"), t("BO", 0, 128, 16)), ["BO"], ["SELC"], 64)
    G(lambda q: q.iota(t("KC"), [[0, 8], [-1, 16]], 15, 0, allow_small_or_imprecise_dtypes=True), [], ["KC"], 128)
    G(lambda q: q.affine_select(t("KS"), t("KC"), [[0, 128]], A.is_ge, 131072.0, 0, -1), ["KC"], ["KS"], 128)
    G(lambda q: q.affine_select(t("KC"), t("KC"), [[0, 128]], A.is_ge, 0.0, 0, -1), ["KC"], ["KC"], 128)
    EPS = 2.0 ** -8
    G(lambda q: q.affine_select(t("LT"), t("BO"), [[1, 128]], A.is_gt, EPS, 0, -1), ["BO"], ["LT"], 128)
    G(lambda q: q.affine_select(t("LT"), t("LT"), [[1, 128]], A.not_equal, -32.0, 0, -1), ["LT"], ["LT"], 128)
    V(tt(t("LT"), t("LT"), t("BO"), A.mult), ["LT", "BO"], ["LT"], 256)
    V(ts(t("THR"), t("MCOL"), 0.5, A.subtract, EPS / 2, A.max), ["MCOL"], ["THR"], 64)
    V(ts(t("THR"), t("THR"), 2.0, A.mult), ["THR"], ["THR"], 64)
    V(ts(t("THR2"), t("MCOL"), EPS - 1, A.mult, 32 - 15 * EPS, A.add), ["MCOL"], ["THR2"], 64)
    V(tt(t("THR"), t("THR"), t("THR2"), A.add), ["THR", "THR2"], ["THR"], 64)
    V(ts(t("M64C"), t("MCOL"), 1 / 64, A.mult), ["MCOL"], ["M64C"], 64)
    for nm, src, sc in (("P15", "BO", "PC15"), ("P2", "BO", "PC2"), ("M64", "BO", "M64C"), ("NBO", "BO", -0.5), ("BO4K", "BO", 4096.0),
                        ("I8P", "IDENT", 8192.0), ("INEG", "IDENT", -BIG), ("IBIG", "IDENT", BIG), ("NID", "IDENT", -1.0), ("IDF", "IDENT", 1.0)):
        S(act(t(nm), t(src), AF.Copy, 0.0, t(sc) if sc in TILES else sc), [src] + ([sc] if sc in TILES else []), [nm], 128)
    for k, nm in enumerate(("ZA", "ZB")):
        G((lambda k, nm: lambda q: q.affine_select(t(nm), t("BO"), [[0, 8], [1, 16]], A.is_equal, 0.0, -k, 0))(k, nm), ["BO"], [nm], 128)
    V(lambda v: v.memset(t("ONE16"), 1 / 16), [], ["ONE16"], 64)
    V(ts(t("B135"), t("MCOL"), -1.0, A.mult, 135.0, A.add), ["MCOL"], ["B135"], 64)
    V(lambda v: v.memset(t("MASK"), 1.0), [], ["MASK"], 128)
    V(lambda v: v.memset(t("MASK", 0, 128, 16), 0.0), [], ["MASK"], 64)
    V(lambda v: v.memset(t("K63"), -31.5), [], ["K63"], 64)
    V(lambda v: v.memset(t("K155"), -7.75), [], ["K155"], 64)
    G(lambda q: q.iota(t("PNUM"), [[1, 128]], 0, 0, allow_small_or_imprecise_dtypes=True), [], ["PNUM"], 128)
    G(lambda q: q.affine_select(t("PNUM"), t("PNUM"), [[0, 128]], A.is_ge, 1.0, 0, -1), ["PNUM"], ["PNUM"], 128)
    V(lambda v: v.memset(t("ZC"), 0.0), [], ["ZC"], 64)
    for r, m in ((0, 2), (1, 3)):
        G((lambda r, m: lambda q: q.affine_select(t("ZC"), t("ZC"), [[0, 8], [1, 16]], A.not_equal, 1.0, 64 * r - m, -64))(r, m), ["ZC"], ["ZC"], 128)
    V(ts(t("R01"), t("MCOL"), 1.5, A.is_lt), ["MCOL"], ["R01"], 64)
    V(ts(t("BO01"), t("BO"), t("R01"), A.mult), ["BO", "R01"], ["BO01"], 64)
    V(ts(t("WN"), t("R01"), -255.0, A.mult, -1.0, A.add), ["R01"], ["WN"], 64)
    V(ts(t("M3"), t("MCOL"), 2.5, A.is_lt), ["MCOL"], ["M3"], 64)
    V(tt(t("WN"), t("WN"), t("M3"), A.mult), ["WN", "M3"], ["WN"], 64)
    V(ts(t("M3B"), t("MCOL"), 3.0, A.is_equal, 64.0, A.mult), ["MCOL"], ["M3B"], 64)
    V(tt(t("WP"), t("M3B"), t("WN"), A.subtract), ["M3B", "WN"], ["WP"], 64)
    G(lambda q: q.affine_select(t("SELP"), t("SELP"), [[-16, 8], [0, 128]], A.is_ge, 0.0, 0, 1), ["SELP"], ["SELP"], 1024)
    G(lambda q: q.affine_select(t("SELP"), t("SELP"), [[16, 8], [0, 128]], A.is_ge, 0.0, 15, -1), ["SELP"], ["SELP"], 1024)
    S(act(t("SELN"), t("SELP"), AF.Copy, 0.0, t("WN")), ["SELP", "WN"], ["SELN"], 1024)
    S(act(t("SELP"), t("SELP"), AF.Copy, 0.0, t("WP")), ["SELP", "WP"], ["SELP"], 1024)
    G(lambda q: q.iota(t("DUM"), [[16, 16]], PAD + 1, 0, allow_small_or_imprecise_dtypes=True), [], ["DUM"], 16)
    V(ts(t("DUM"), t("DUM"), t("MCOL"), A.add), ["DUM", "MCOL"], ["DUM"], 64)
    for k in range(NP):
        sl = T.X[:, k * PW:(k + 1) * PW]
        V(ts(sl, sl, 1.0, A.add), ["Xr%d" % k], ["Xr%d" % k], PW / 2)
    V(cp(t("LIMF"), t("LIMI")), ["LIMI"], ["LIMF"], 64)
    V(ts(t("THETA"), t("LIMF"), 120.0, A.subtract), ["LIMF"], ["THETA"], 64)
    XK = ["Xr%d" % k for k in range(NP)] + ["Xz"]
    XALL = T.X[:]

    def gather(dst, lst, h, plan):
        w = []
        for (e, a, b) in plan:
            if a < b:
                key = "%s%d:%d" % (dst, h, a)
                o, s = T[dst + str(h)][:, 16 * a:16 * b], XALL.indirect(t(lst, a, b))
                if e == "S":
                    S(act(o, s, AF.Copy), XK + [lst], [key], 16 * (b - a) * 1.5)
                else:
                    V(cp(o, s), XK + [lst], [key], 16 * (b - a) * 1.5)
                w.append(key)
        return w

    def sums(h, slot, x, f, plan, kx):
        H = str(h)
        for (e, a, b), key in zip(plan, kx):
            o = T["P3_" + H][:, slot, a:b]
            P(mms([(o, t("IDENT"), x[:, 16 * a + m:16 * b:16]) for m in range(16)] + [(o, t("NBO"), t(f, a, b)), (o, t("CONSTL"), t("K155", a, b))]),
              ["IDENT", "NBO", "CONSTL", "K155", f, key], ["P3_%s%d" % (H, slot)] if a == 0 else ["P3_%s%d+%d" % (H, slot, a)], 18 * max(64, b - a))
        return ["P3_%s%d" % (H, slot)] + ["P3_%s%d+%d" % (H, slot, a) for e, a, b in plan if a]

    def argmax(h):
        H = str(h)
        src, p0 = "P0_" + H, T["P0_" + H]
        V(lambda v: v.tensor_tensor_scan(t("SCA" + H), t("MASK"), p0[:, 0:128], 0.0, A.mult, A.max), [src, "MASK"], ["SCA" + H], 128)
        V(lambda v: v.tensor_tensor_scan(t("SC" + H)[:, ::-1], t("MASK"), t("SCA" + H)[:, ::-1], 0.0, A.mult, A.max), ["SCA" + H, "MASK"], ["SC" + H], 128)
        V(tt(t("OHD" + H), p0[:, 0:128], t("SC" + H), A.is_equal), [src, "SC" + H], ["OHD" + H], 128)

    def phase1(vt, h):
        H = str(h)
        LU, W = "LU%d%d" % (h, vt), "W%d%d" % (h, vt)
        p0, p1, p3 = T["P0_" + H], T["P1_" + H], T["P3_" + H]
        x = T["x1" + H]
        kx = gather("x1", LU, h, SHARE[("a" if vt else "f") + H])
        V(ts(t("D1" + H), t(LU), 1.0, A.add), [LU], ["D1" + H], 128)
        S(act(t("F1" + H), t("D1" + H), AF.Sign, 3456.5, -1.0), ["D1" + H], ["F1" + H], 128)
        S(act(t("DHI" + H), t("D1" + H), AF.Copy), ["D1" + H], ["DHI" + H], 128)
        V(tt(t("DLO" + H), t("D1" + H), t("DHI" + H), A.subtract), ["D1" + H, "DHI" + H], ["DLO" + H], 256)
        P(mms([(p1[:, 3, :], t("BO"), t("F1" + H))]), ["BO", "F1" + H], ["P1_%s3" % H], 128)
        S(act(t("FULL" + H), p1[:, 3, :], AF.Relu, -15.0), ["P1_%s3" % H], ["FULL" + H], 128)
        P(mms([(p0[:, 0:128], t("CONSTL"), t("KC"))] + [(p0[:, m:128:16], x[:, m::16], t("E16")) for m in range(16)]),
          ["CONSTL", "KC", "E16"] + kx, ["P0_" + H], 128 + 16 * 64)
        argmax(h)
        kt = sums(h, 0, x, "F1" + H, SHARE[("a" if vt else "f") + H], kx)
        S(act(t("T32" + H), p3[:, 0, :], AF.Copy), kt, ["T32" + H], 128)
        P(mms([(p3[:, 1, :], t("BOF"), t("T32" + H)), (p3[:, 1, :], t("BO4K"), t("FULL" + H))]),
          ["BOF", "T32" + H, "BO4K", "FULL" + H], ["P3_%s1" % H], 640)
        V(ts(t("ST" + H), p3[:, 1, :], t("THETA"), A.is_ge), ["P3_%s1" % H, "THETA"], ["ST" + H], 128)
        P(mms([(p1[:, 0, :], t("OHD" + H), t("IDENT"))]), ["OHD" + H, "IDENT"], ["P1_%s0" % H], 128)
        V(tt(t("OHS" + H), p1[:, 0, :], t("ST" + H), A.mult), ["P1_%s0" % H, "ST" + H], ["OHS" + H], 128)
        P(mms([(p1[:, 1, :], t("P15"), t("OHS" + H))]), ["P15", "OHS" + H], ["P1_%s1" % H], 128)
        V(tt(t("TI" + H), t(W), p1[:, 1, :], A.mult), [W, "P1_%s1" % H], ["TI" + H], 128)
        V(ts(t("GI" + H), t("TI" + H), 3, A.logical_shift_right, 4096, A.bitwise_and), ["TI" + H], ["GI" + H], 128)
        V(tt(t("D2" + H), t("D1" + H), t("GI" + H), A.max), ["D1" + H, "GI" + H], ["D2" + H], 256)
        V(ts(t("L2" + H), t("D2" + H), 1.0, A.subtract), ["D2" + H], ["L2" + H], 128)

    def phase2(vt, h):
        H = str(h)
        W = "W%d%d" % (h, vt)
        p0, p1, p3 = T["P0_" + H], T["P1_" + H], T["P3_" + H]
        x = T["x2" + H]
        kx = gather("x2", "L2" + H, h, SHARE["x2"])
        S(act(t("F2" + H), t("D2" + H), AF.Sign, 3456.5, -1.0), ["D2" + H], ["F2" + H], 128)
        P(mms([(p1[:, 2, :], t("LT"), t("F2" + H))]), ["LT", "F2" + H], ["P1_%s2" % H], 128)
        P(mms([(p1[:, 3, :], t("IDF"), t(W)), (p1[:, 3, :], t("IBIG"), t("F2" + H))]), ["IDF", W, "IBIG", "F2" + H], ["P1_%s3" % H], 640)
        V(ts(t("OHE" + H), p1[:, 2, :], t("THR"), A.is_ge), ["P1_%s2" % H, "THR"], ["OHE" + H], 128)
        S(act(t("NOE" + H), t("OHE" + H), AF.Identity, 1.0, -1.0), ["OHE" + H], ["NOE" + H], 128)
        S(act(t("W2" + H), p1[:, 3, :], AF.Relu, -BIG), ["P1_%s3" % H], ["W2" + H], 128)
        V(cp(t("A2" + H), t("W2" + H)), ["W2" + H], ["A2" + H], 128)
        ku = sums(h, 2, x, "F2" + H, SHARE["x2"], kx)
        S(act(t("U32" + H), p3[:, 2, :], AF.Identity, t("B135"), 16.0), ku + ["B135"], ["U32" + H], 128)
        S(act(t("Y" + H), p3[:, 2, :], AF.Identity, MAGIC, 1 / 16), ku, ["Y" + H], 128)
        P(mms([(p0[:, 0:128], t("U32" + H), t("IDF"))]), ["U32" + H, "IDF"], ["P0_" + H], 512)
        S(act(t("VB" + H), t("Y" + H), AF.Identity, MAGIC + 256, -1.0), ["Y" + H], ["VB" + H], 128)
        argmax(h)
        P(mms([(p3[:, 3, :], t("OHD" + H), t("IDENT"))]), ["OHD" + H, "IDENT"], ["P3_%s3" % H], 128)

    def phase3(vt, h):
        H = str(h)
        p0, p1, p3 = T["P0_" + H], T["P1_" + H], T["P3_" + H]
        x, z = T["x2" + H], T["z" + H]
        kx = ["x2%d:%d" % (h, a) for e, a, b in SHARE["x2"]]
        for q in range(2):
            ms = range(8 * q, 8 * q + 8)

            def kf(v, ms=ms):
                for m in ms:
                    r = v.tensor_tensor(z[:, m::16], x[:, m::16], p3[:, 3, :], A.mult)
                return r
            V(kf, kx + ["P3_%s3" % H], ["z%s:%d" % (H, q)], 8 * 128)

            def yf(pe, q=q, ms=ms):
                if q == 0:
                    pe.matmul(p0[:, 0:128], t("CONSTL"), t("KC"), True, False)
                for m in ms:
                    r = pe.matmul(p0[:, m:128:16], z[:, m::16], t("E16"), False, m == 15)
                return r
            P(yf, ["CONSTL", "KC", "E16", "z%s:%d" % (H, q)], ["P0_" + H], 128 * (1 - q) + 8 * 64, q == 1)
        argmax(h)
        P(mms([(p1[:, 0, :], t("OHD" + H), t("IDENT"))]), ["OHD" + H, "IDENT"], ["P1_%s0" % H], 128)
        V(tt(t("MBK" + H), p1[:, 0, :], t("D2" + H), A.mult), ["P1_%s0" % H, "D2" + H], ["MBK" + H], 128)
        V(tt(t("MBA" + H), p1[:, 0, :], t("A2" + H), A.mult), ["P1_%s0" % H, "A2" + H], ["MBA" + H], 128)
        S(act(t("OHK" + H), p1[:, 0, :], AF.Copy), ["P1_%s0" % H], ["OHK" + H], 128)
        P(mms([(p1[:, 1, :], t("MBK" + H), t("BOF"))]), ["MBK" + H, "BOF"], ["P1_%s1" % H], 512)
        V(tt(t("VM" + H), p1[:, 1, :], t("DQF"), A.mult), ["P1_%s1" % H, "DQF"], ["VM" + H], 128)
        P(mms([(p1[:, 3, 0:8], t("VM" + H), t("SELC"))]), ["VM" + H, "SELC"], ["P1_%s3" % H], 256)
        V(ts(t("LC" + H, 0, 8), p1[:, 3, 0:8], 1.0, A.subtract, 3455.0, A.min), ["P1_%s3" % H], ["LC" + H], 64)
        V(cp(t("CU" + H), T.R[:].indirect(t("LC" + H, 0, 8))), ["Ra", "Rb", "LC" + H], ["CU" + H], 200)

    def phase4(vt, h):
        H = str(h)
        p0, p1, p3 = T["P0_" + H], T["P1_" + H], T["P3_" + H]
        xc, ax = T["xc" + H], T["ax" + H]
        kx = gather("xc", "CU" + H, h, SHARE["xc"])
        V(ts(t("CF" + H), t("CU" + H), 1.0, A.add), ["CU" + H], ["CF" + H], 128)
        P(mms([(p1[:, 2, :], t("BOF"), t("MBA" + H)), (p1[:, 2, :], t("M64"), t("OHK" + H)), (p1[:, 2, :], t("P2"), t("OHE" + H)),
               (p1[:, 2, :], t("INEG"), t("NOE" + H))]),
          ["BOF", "MBA" + H, "M64", "OHK" + H, "P2", "OHE" + H, "INEG", "NOE" + H], ["P1_%s2" % H], 896)
        last = vt == NV - 1
        WN = ("SW%d%d" % (h, vt + 1)) if not last else "W2" + H
        V(tt(t(WN), t("W2" + H), p1[:, 2, :], A.max), ["W2" + H, "P1_%s2" % H], [WN], 128)
        if not last:
            send(WN, "W%d%d" % (h, vt + 1), 6 * h + 2 * vt)
        ks = P(mms([(p0[:, 0:128], t("CONSTL"), t("KS"))], True, False), ["CONSTL", "KS"], ["P0_" + H], 128)
        def mf(v):
            for j in range(12, 16):
                r = v.tensor_tensor(ax[:, j, :], xc[:, j::16], t("VB" + H), A.max)
            return r
        V(mf, kx + ["VB" + H], ["ax%s:3" % H], 1024)

        def lf(pe):
            for j in range(12, 16):
                pe.matmul(p0[:, j:128:16], xc[:, j::16], t("E16"), False, False)
                r = pe.matmul(p0[:, j:128:16], t("VB" + H), t("E16"), False, False)
            return r
        parts = [P(lf, ["E16", "VB" + H] + kx, ["P0_%s#l" % H], 512, True, [ks])]

        def gf(pe):
            for j in range(12, 16):
                r = pe.matmul(p0[:, j:128:16], ax[:, j, :], t("E32N"), False, False)
            return r
        parts.append(P(gf, ["E32N", "ax%s:3" % H], ["P0_%s#g" % H], 256, True, [ks]))
        for b in range(3):
            pb, kb = (p3, "P3_%s" % H) if b % 2 == 0 else (p1, "P1_%s" % H)

            def df(pe, b=b, pb=pb):
                for u in range(4):
                    pe.matmul(pb[:, u, :], t("IDENT"), xc[:, 4 * b + u::16], True, False)
                    r = pe.matmul(pb[:, u, :], t("NID"), t("VB" + H), False, True)
                return r
            P(df, ["IDENT", "NID", "VB" + H] + kx, [kb + str(u) for u in range(4)], 1024)
            S(act(ax[:, 4 * b:4 * b + 4, :], pb[:, :, :], AF.Abs), [kb + str(u) for u in range(4)], ["ax%s:%d" % (H, b)], 512)

            def sf(pe, b=b):
                for j in range(4 * b, 4 * b + 4):
                    r = pe.matmul(p0[:, j:128:16], ax[:, j, :], t("E16N"), False, j == 11)
                return r
            parts.append(P(sf, ["E16N", "ax%s:%d" % (H, b)], ["P0_%s#%d" % (H, b) if b < 2 else "P0_" + H], 256, True, [ks] if b < 2 else parts))
        argmax(h)
        P(mms([(p1[:, 0, :], t("OHD" + H), t("IDENT"))]), ["OHD" + H, "IDENT"], ["P1_%s0" % H], 128)
        V(tt(t("MB2" + H), p1[:, 0, :], t("CF" + H), A.mult), ["P1_%s0" % H, "CF" + H], ["MB2" + H], 128)
        P(mms([(p1[:, 1, :], t("I8P"), t("NOE" + H))], True, False), ["I8P", "NOE" + H], ["P1_%s1" % H], 128)
        P(mms([(p1[:, 1, :], t("BOF"), t("MB2" + H))], False, True), ["BOF", "MB2" + H], ["P1_%s1" % H], 512, True)
        V(tt(t("D3" + H), t("D2" + H), p1[:, 1, :], A.min), ["D2" + H, "P1_%s1" % H], ["D3" + H], 128)
        if not last:
            LN = "SLU%d%d" % (h, vt + 1)
            V(ts(t(LN), t("D3" + H), 1.0, A.subtract), ["D3" + H], [LN], 128)
            send(LN, "LU%d%d" % (h, vt + 1), 6 * h + 2 * vt + 1)
        else:
            V(ts(t("YP" + H), t("D3" + H), 1.0, A.subtract, 3456.0, A.min), ["D3" + H], ["YP" + H], 128)
            dma("Y", T.yp[:, h * CH:h * CH + CH], t("YP" + H), ["YP" + H], [], 2.5)
            V(cp(t("A2" + H), t("W2" + H)), ["W2" + H], ["A2" + H], 128)
            V(tt(t("YQ" + H), t("W2" + H), t("A2" + H), A.subtract), ["W2" + H, "A2" + H], ["YQ" + H], 256)
            V(ts(t("YR" + H), t("YQ" + H), 64.0, A.mult), ["YQ" + H], ["YR" + H], 128)
            dma("Y", T.yq[:, h * CH:h * CH + CH], t("YR" + H), ["YR" + H], [], 2.5)

    def send(src, dst, k):
        mask, n = topo.mask(core, nxt), len(topo.engines(core, nxt))
        rid, pid = topo.addr(nxt)[:2]
        o = add("G", lambda: g.remote_dma(t(dst), t(src), T.sem["r%d" % k], T.sem["l%d" % k], pid, rid, mask), [src], [], 1.0,
                sem="l%d" % k, need=n, comp=False)
        add("N", None, [], [dst], 2.5, sem="r%d" % k, need=len(topo.engines(prv, core)), extra=[o], comp=False)

    def dedup(vt, h):
        H = str(h)
        q2 = "P2_" + H
        p2 = T[q2]
        P(mms([(p2[:, 3, :], t("IDENT"), t("OHS" + H))]), ["IDENT", "OHS" + H], [q2 + "3"], 128)
        V(tt(t("MBH" + H), p2[:, 3, :], t("DHI" + H), A.mult), [q2 + "3", "DHI" + H], ["MBH" + H], 128)
        V(tt(t("MBL" + H), p2[:, 3, :], t("DLO" + H), A.mult), [q2 + "3", "DLO" + H], ["MBL" + H], 128)
        P(mms([(p2[:, 1, :], t("ZA"), t("MBH" + H)), (p2[:, 1, :], t("ZB"), t("MBL" + H)), (p2[:, 1, :], t("ZC"), t("PNUM"))]),
          ["MBH" + H, "MBL" + H, "ZA", "ZB", "ZC", "PNUM"], [q2 + "1"], 384)
        S(act(t("Z" + H), p2[:, 1, :], AF.Copy), [q2 + "1"], ["Z" + H], 128)
        P(mms([(p2[:, 0, :], t("Z" + H), t("BO01"))]), ["Z" + H, "BO01"], [q2 + "0"], 128)
        P(mms([(p2[:, 2, :], t("ONE16"), t("ST" + H))]), ["ONE16", "ST" + H], [q2 + "2"], 128)
        V(tt(t("VMD" + H), p2[:, 0, :], t("DQF"), A.mult), [q2 + "0", "DQF"], ["VMD" + H], 128)
        if vt < NV - 1:
            S(lambda s: s.activation(t("AA" + H), p2[:, 2, :], AF.Copy, accum_out=t("CNT", h, h + 1)), [q2 + "2"], ["AA" + H, "CNT" + H], 160)
        P(mms([(p2[:, 1, 0:8], t("VMD" + H), t("SELC"))]), ["VMD" + H, "SELC"], [q2 + "1"], 256)
        V(cp(t("DC", 8 * h, 8 * h + 8), p2[:, 1, 0:8]), [q2 + "1"], ["DC" + H], 64)
        for w in range(8):
            b = q2
            o = T[b][:, w % 4, :]
            sp, sn = t("SELP", w * 128, w * 128 + 128), t("SELN", w * 128, w * 128 + 128)
            P(mms([(o, sp, t("Z" + H)), (o, t("Z" + H), sn)]), ["SELP", "SELN", "Z" + H], [b + str(w % 4)], 256)
            if w % 4 == 3:
                for u in range(w - 3, w + 1):
                    V((lambda u, b: lambda v: v.tensor_reduce(t("RED" + H, u, u + 1), T[b][:, u % 4, :], AxisListType.X, A.min,
                                                              apply_absolute_value=True))(u, b), [b + str(u % 4)], ["RED%s%d" % (H, u)], 128)
        for w in range(8):
            S(act(t("VMW" + H, 16 * w, 16 * w + 16), t("DQ", 0, 16), AF.Copy, 0.0, t("RED" + H, w, w + 1)), ["DQ", "RED%s%d" % (H, w)], ["VMW%s%d" % (H, w)], 16)
        S(act(t("TM" + H), t("T32" + H), AF.Identity, MAGIC, 1 / 16), ["T32" + H], ["TM" + H], 128)
        S(act(t("TFB" + H), t("TM" + H), AF.Identity, -MAGIC, 1.0), ["TM" + H], ["TFB" + H], 128)

    def update(vt):
        pa, pb = T.P2_0, T.P2_1
        for h in range(2):
            H = str(h)
            P(mms([(pa[:, 3, 8 * h:8 * h + 8], t("VMW" + H), t("BO", 0, 128, 16)), (pa[:, 3, 8 * h:8 * h + 8], t("CONSTL"), t("K63"))]),
              ["VMW%s%d" % (H, w) for w in range(8)] + ["BO", "CONSTL", "K63"], ["P2_03%d" % h], 128)
        V(ts(t("GL"), t("DC"), 1.0, A.subtract), ["DC0", "DC1"], ["GL"], 64)
        S(act(t("XS"), XALL.indirect(t("GL")), AF.Copy), XK + ["GL"], ["XS"], 400)
        for h in range(2):
            H = str(h)
            P(mms([(pb[:, h, :], t("IDENT"), t("XS", 128 * h, 128 * h + 128)), (pb[:, h, :], t("IDENT"), t("TFB" + H))]),
              ["IDENT", "XS", "TFB" + H], ["P2_1%d" % h], 256)
        V(ts(t("XN"), pb[:, 0:2, :], 0.5, A.mult, 0.25 if vt < NV - 1 else -0.75, A.add), ["P2_10", "P2_11"], ["XN"], 256)
        V(tt(t("WM"), pa[:, 3, 0:16], t("DC"), A.min), ["P2_030", "P2_031", "DC0", "DC1"], ["WM"], 64)
        V(ts(t("LL"), t("WM"), 0.5, A.is_lt), ["WM"], ["LL"], 64)
        V(tt(t("TT"), t("LL"), t("DUM"), A.mult), ["LL", "DUM"], ["TT"], 64)
        V(tt(t("OFF"), t("TT"), t("DC"), A.max), ["TT", "DC0", "DC1"], ["OFF"], 64)
        V(ts(t("SL"), t("OFF"), 1.0, A.subtract), ["OFF"], ["SL"], 64)
        if vt < NV - 1:
            V(tt(t("CI"), t("CNT", 0, 1), t("CNT", 1, 2), A.add), ["CNT0", "CNT1"], ["CI"], 64)
            V(ts(t("CI2"), t("CI"), 255, A.bitwise_and), ["CI"], ["CI2"], 64)
            V(ts(t("THETA"), t("CI2"), t("LIMF"), A.add, 120.0, A.subtract), ["CI2", "LIMF"], ["THETA"], 64)
        dst, keys = (T.X[:], XK) if vt < NV - 1 else (T.Y[:], ["Y%d" % k for k in range(NP)] + ["Yz"])
        for h in (1, 0):
            V(cp(dst.indirect(t("SL", 8 * h, 8 * h + 8)), t("XN", 128 * h, 128 * h + 128)), ["SL", "XN"], keys, 128 * 3)

    for vt in range(NV):
        if vt == NV - 1:
            V(lambda v: v.memset(T.Y[:, D:], 0.0), [], ["Yz"], 456)
            for k in range(NP):
                S(act(T.Y[:, k * PW:(k + 1) * PW], T.X[:, k * PW:(k + 1) * PW], AF.Identity, -1.0, 1.0), XK, ["Y%d" % k], PW)
        for ph in (phase1, phase2, phase3):
            for h in range(2):
                now[0] = BONUS[2 * (phase1, phase2, phase3).index(ph) + h]
                ph(vt, h)
        now[0] = BONUS[8]
        if vt == NV - 1:
            for h in range(2):
                dedup(vt, h)
            update(vt)
            for k in range(NP):
                dma("Y", T.yx[:, k * PW:(k + 1) * PW], T.Y[:, k * PW:(k + 1) * PW], ["Y%d" % k], [], 4.0)
        for h in range(2):
            now[0] = BONUS[6 + h]
            phase4(vt, h)
        now[0] = BONUS[8]
        if vt < NV - 1:
            for h in range(2):
                dedup(vt, h)
            update(vt)

    emit(g, T, ops, schedule(ops), QUEUE)


WAKE, LOOK, IDLE = 0.12, 0.06, 0.0


def schedule(ops):
    n = len(ops)
    succ = [[] for _ in range(n)]
    for k, o in enumerate(ops):
        for d in o["deps"]:
            succ[d].append(k)
    tail = [0.0] * n
    for k in range(n - 1, -1, -1):
        tail[k] = ops[k]["cost"] + max([tail[s] + WAKE for s in succ[k]] + [0.0])
    for k in range(n):
        tail[k] += ops[k]["bonus"]
    left = [len(o["deps"]) for o in ops]
    fin, free, order = [0.0] * n, {}, []
    ready = {}
    for k in range(n):
        if left[k] == 0:
            ready.setdefault(ops[k]["phys"], {})[k] = 0.0
    while ready:
        best = None
        for e, lst in ready.items():
            f = free.get(e, 0.0)
            t0 = max(f, min(lst.values()))
            if best is None or t0 < best[0]:
                best = (t0, e)
        t0, e = best
        lst = ready[e]
        k = max((tail[k] - IDLE * max(0.0, r - t0), -k) for k, r in lst.items() if r <= t0 + LOOK)[1] * -1
        st = max(free.get(e, 0.0), lst.pop(k))
        if not lst:
            del ready[e]
        o = ops[k]
        fin[k] = st + o["cost"]
        if e != "N":
            free[e] = st + (o["cost"] if o["comp"] else (0.1 if o["eng"] != "G" else 1.0))
        order.append(k)
        for s in succ[k]:
            left[s] -= 1
            if left[s] == 0:
                ready.setdefault(ops[s]["phys"], {})[s] = max([fin[d] + (WAKE if ops[s]["deps"][d] == "wait" else 0.0) for d in ops[s]["deps"]])
    ops[0]["makespan"] = max(fin)
    ops[0]["fin"] = dict(enumerate(fin))
    return order


def emit(g, T, ops, order, QUEUE):
    know = {e: {} for e in ("V", "S", "T", "G", "Y")}
    cnt = {}
    for k in order:
        o = ops[k]
        e = o["phys"]
        if e == "N":
            o["sig"], o["kn"] = (o["sem"], o["need"]), {}
            continue
        q, kn = QUEUE[o["eng"]], know[e]
        waits, src = {}, {}
        for d in o["deps"]:
            if o["deps"][d] == "wait":
                s, v = ops[d]["sig"]
                if kn.get(s, 0) < v and waits.get(s, 0) < v:
                    waits[s], src[s] = v, d
        for s in list(waits):
            if any(s2 != s and ops[src[s2]]["kn"].get(s, 0) >= waits[s] for s2 in waits):
                del waits[s]
        for s in sorted(waits):
            q.wait_ge(T.sem[s], waits[s])
            for a, b in ops[src[s]]["kn"].items():
                kn[a] = max(kn.get(a, 0), b)
            kn[s] = max(kn.get(s, 0), waits[s])
        ins = o["fn"]()
        if o["comp"]:
            s = "c" + e
            cnt[s] = cnt.get(s, 0) + 1
            ins.then_inc(T.sem[s], 1)
            o["sig"] = (s, cnt[s])
        else:
            o["sig"] = (o["sem"], o["need"])
            if o["eng"] != "G":
                ins.then_inc(T.sem[o["sem"]], 16)
        o["kn"] = dict(kn)
    for s in sorted(cnt):
        g.wait_ge(T.sem[s], cnt[s])
    for o in ops:
        if not o["comp"] and o["phys"] != "N":
            g.wait_ge(T.sem[o["sig"][0]], o["sig"][1])
